import numpy as np, ml_dtypes
CORES = [6,15,38,47]
N = 4
BF = ml_dtypes.bfloat16
W, E, S, M, RO, DB, DC, CM, EX = 3072, 256, 12, 12, 4, 1, 1, 9, 4
def pack(x, p, r, z):
    return {"x0": np.ascontiguousarray(x.reshape(N, 128, W)).astype(np.float32).astype(BF), "lk": np.ascontiguousarray(p.reshape(N, 128, W)).astype(np.int32),
            "rd": np.ascontiguousarray(r.reshape(N, 128, E)).astype(np.int32), "z0": np.ascontiguousarray(z.reshape(N, 128, E)).astype(np.float32).astype(BF)}
def parts(rng):
    lev = np.repeat(rng.choice(np.array([24, 60, 120, 190, 255]), (N, 8, 1, 8)), W // 8, axis=3)
    x = (rng.random((N, 8, 16, W)) * (lev + 1)).astype(np.int64) * (rng.random((N, 8, 1, W)) > 0.0625)
    share = np.stack([rng.permutation(np.array([0.1, 0.1, 0.3, 0.3, 0.6, 0.6, 0.9, 0.95])) for q in range(N)]).reshape(N, 8, 1, 1)
    to = np.where(rng.random((N, 8, 16, W)) < 0.5, S * rng.integers(0, E, (N, 8, 16, W)), rng.integers(0, W, (N, 8, 16, W)))
    p = np.where(rng.random((N, 8, 16, W)) < share, to, W)
    near = rng.integers(0, 8, (N, 8, 1, E)) * (W // 8) + rng.integers(0, W // 8, (N, 8, 16, E))
    r = np.where(rng.random((N, 8, 1, E)) < 0.5, near, rng.integers(0, W, (N, 8, 16, E)))
    z = (rng.random((N, 8, 16, E)) * (rng.choice(np.array([40, 120, 255]), (N, 8, 1, E)) + 1)).astype(np.int64)
    return x, p, r, z
def setup_inputs(rng):
    return pack(*parts(rng))
def setup_inputs_spread(rng):
    x = np.minimum((np.exp2(9 * rng.random((N, 8, 1, W))) * rng.random((N, 8, 16, W))).astype(np.int64), 255)
    z = np.minimum((np.exp2(9 * rng.random((N, 8, 1, E))) * rng.random((N, 8, 16, E))).astype(np.int64), 255)
    to = np.minimum((W * rng.random((N, 8, 16, W)) ** 3).astype(np.int64), W - 1)
    p = np.where(rng.random((N, 8, 16, W)) < rng.random((N, 8, 16, 1)), to, W)
    r = np.minimum((W * rng.random((N, 8, 16, E)) ** rng.choice(np.array([1.0, 2.0, 4.0]), (N, 8, 1, 1))).astype(np.int64), W - 1)
    return pack(x, p, r, z)
def setup_inputs_ends(rng):
    kind = rng.integers(0, 4, (N, 8, 1, W)); el = 255 * rng.integers(0, 2, (N, 8, 16, W))
    x = np.where(kind == 0, 0, np.where(kind == 1, 255, el))
    v = rng.permutation(np.array([0, 255] * 4)); x[..., 0] = v[None, :, None]; x[..., W - 1] = 255 - v[None, :, None]
    x[..., W - 2] = 255 - v[None, :, None]; x[:, :, 15, W - 2] = np.where(v == 0, 254, 1)[None, :]
    p = np.where(rng.random((N, 8, 16, W)) < 0.2, rng.integers(0, W, (N, 8, 16, W)), W * (rng.random((N, 8, 16, W)) < 0.65))
    p[..., 0] = W; p[:, :, 0, 0] = W - 2; p[:, :, [1, 15], 0] = W - 1; p[..., W - 1] = W; p[:, :, [0, 15], W - 1] = 0
    way = rng.integers(0, 4, (N, 8, 1, E)); way[..., 0] = 0; way[..., E - 2] = 0; way[..., E - 1] = 1
    end = (W - 1) * rng.integers(0, 2, (N, 8, 16, E)); some = np.where(rng.random((N, 8, 16, E)) < 0.5, end, rng.integers(0, W, (N, 8, 16, E)))
    r = np.where(way == 0, 0, np.where(way == 1, W - 1, np.where(way == 2, end, some)))
    z = 255 * np.where(rng.random((N, 8, 1, E)) < 0.5, rng.integers(0, 2, (N, 8, 1, E)), rng.integers(0, 2, (N, 8, 16, E)))
    return pack(x, p, r, z)
def setup_inputs_corners(rng):
    x, p, r, z = parts(rng); gt = rng.permutation(8); H = W // 2
    for g in range(8):
        m = int(gt[g])
        if m < 2:
            x[:, g, :, 1::2] = 128
            h = rng.integers(0, 17, (N, 1, H)) if m == 0 else rng.choice(np.array([EX, EX + 1, CM - 1, CM]), (N, 1, H))
            up = np.argsort(rng.random((N, 16, H)), axis=1) < h; one = rng.random((N, 16, H)) < (0.5 if m == 0 else 2.0)
            x[:, g, :, 0::2] = np.where(up, np.where(one, 128, rng.integers(128, 256, (N, 16, H))), np.where(one, 127, rng.integers(0, 128, (N, 16, H))))
            p[:, g] = np.where(rng.random((N, 16, W)) < 0.4, 2 * rng.integers(0, H, (N, 16, W)), W)
            r[:, g] = 2 * rng.integers(0, H, (N, 16, E)) + 1
        elif m == 2:
            full = rng.integers(0, W, (N, 16, W)); p[:, g] = np.where((np.arange(N) % 2 == 0)[:, None, None], full, W)
        elif m == 3:
            r[:, g] = S * np.arange(E)[None, :] + (np.arange(16) % S)[:, None]
            p[:, g] = np.where(rng.random((N, 16, W)) < 0.5, S * (np.arange(W) // S), W)
            x[:, g, :, 0::S] = x[:, g, :, 0::S] * (rng.random((N, 1, E)) < 0.5)
        elif m == 4:
            x[:, g] = x[:, g] * (rng.random((N, 1, W)) < 0.3); z[:, g] = z[:, g] * (rng.random((N, 1, E)) < 0.5)
            x[:, g, :15, 0::S] = 0; x[:, g, 15, 0::S] = rng.integers(1, 256, (N, E)) * (rng.random((N, E)) < 0.5)
            p[:, g] = np.where(rng.random((N, 16, W)) < 0.5, rng.integers(0, W, (N, 16, W)), W)
        elif m == 5:
            p[:, g] = rng.choice(np.array([0, W - 1, W]), (N, 16, W))
            r[:, g] = np.where(rng.random((N, 16, E)) < 0.5, (W - 1) * rng.integers(0, 2, (N, 16, E)), r[:, g])
        elif m == 6:
            p[:, g] = np.where(rng.random((N, 16, W)) < 0.5, rng.integers(0, W, (N, 16, W)), W)
            x[:, g, :, 0::S] = np.maximum(x[:, g, :, 0::S], 1)
            for b in range(N):
                a = S * rng.permutation(E) + 1; d = S * rng.permutation(E) + S - 1
                high = rng.integers(128, 256, (16, E)); low = rng.integers(1, 100, (16, E))
                x[b, g][:, a] = high if b % 2 == 0 else low
                x[(b + DC) % N, g][:, d] = low if b % 2 == 0 else high
                up = np.argsort(rng.random((16, E)), axis=0) < rng.integers(1, 16, (1, E))
                p[b, g][:, a] = np.where(up, d[None, :], W)
                r[(b - DB) % N, g] = a[None, :]
        else:
            p[:, g] = W; p[:, g, 0] = S * rng.integers(0, E, (N, W)); p[:, g, 15] = rng.integers(0, W, (N, W))
    return pack(x, p, r, z)
def setup_inputs_crowd(rng):
    x, p, r, z = parts(rng); gt = rng.permutation(8)
    for g in range(8):
        m = int(gt[g]); i = int(rng.integers(1, E - 1)); b = S * i + (0 if m in (0, 3, 5, 6) else S - 1)
        a = (0, W - 1, S * (i - 1) + 1, S * i + 1)[m % 4]
        x[:, g, :, a] = rng.integers(128, 256, (N, 16)); x[:, g, :, b] = rng.integers(1, 100, (N, 16))
        p[:, g, :, a] = W; rows = rng.permutation(16)[:5]; p[:, g, rows, a] = b
        r[:, g] = a
        if m >= 4: r[:, g, :, (0, E - 1, 1, i)[m % 4]] = rng.integers(0, W, (N, 16))
    return pack(x, p, r, z)
def check_inputs(d):
    bad = []
    for k, lo, hi in (("x0", 0, 255), ("lk", 0, W), ("rd", 0, W - 1), ("z0", 0, 255)):
        v = np.asarray(d[k]).astype(np.float64)
        if not (np.min(v) >= lo and np.max(v) <= hi): bad.append("range of " + k)
        if np.any(v != np.floor(v)): bad.append("whole numbers of " + k)
        if np.any((v == 0) & np.signbit(v)): bad.append("-0.0 in " + k)
    return bad
def reference(x0, lk, rd, z0):
    X = x0.astype(np.float32).astype(np.int64).reshape(N, 8, 16, W); P = lk.astype(np.int64).reshape(N, 8, 16, W)
    R = rd.astype(np.int64).reshape(N, 8, 16, E); z = z0.astype(np.float32).astype(np.int64).reshape(N, 8, 16, E)
    bi = (np.arange(N) + DB) % N; ci = (np.arange(N) + DB + DC) % N; lane = np.arange(E)
    q = np.zeros((N, 8, E), np.int64) + S * lane
    rows = np.arange(16)[None, None, :, None]; ai = np.arange(N)[:, None, None]; gi = np.arange(8)[None, :, None]
    for t in range(RO):
        XB = X[bi]; PB = P[bi]; flat = R.reshape(N, 8, 1, 16 * E)
        L = np.take_along_axis(PB, R, 3)
        xs = np.take_along_axis(XB, flat, 3).reshape(N, 8, 16, 16, E)
        free = (L == W)[:, :, None]
        top = np.max(np.where(free, xs, -1), axis=3); low = np.min(np.where(free, xs, 256), axis=3)
        y = np.where(top >= 0, (top + low) >> 1, z)
        XC = X[ci]
        orphan = ~np.any(np.take_along_axis(XC, q[:, :, None, :], 3) != 0, axis=2)
        q = np.where(orphan, S * lane + (y[:, :, 0] & 7), q)
        np.put_along_axis(XC, q[:, :, None, :], y, 3)
        es = np.take_along_axis(XC, np.minimum(L, W - 1).reshape(N, 8, 1, 16 * E), 3).reshape(N, 8, 16, 16, E)
        yk = y[:, :, :, None, :]
        n = np.add.reduce((es >= yk).astype(np.int64), axis=2); dist = np.add.reduce(np.abs(es - yk), axis=2)
        com = (L < W) & (n >= CM); late = (L < W) & (n <= EX); settled = com | late
        ks = np.where(np.any(settled, axis=2), np.argmax(np.where(settled, dist, -1), axis=2), 15); kk = ks[:, :, None, :]
        com = np.take_along_axis(com, kk, 2)[:, :, 0]; late = np.take_along_axis(late, kk, 2)[:, :, 0]
        Ls = np.take_along_axis(L, kk, 2)[:, :, 0]; cell = np.take_along_axis(R, kk, 2)[:, :, 0]
        ev = np.take_along_axis(es, ks[:, :, None, None, :], 3)[:, :, :, 0]
        a, g, e = np.nonzero(late); XC[a, g, :, Ls[a, g, e]] = 0
        X[ci] = XC
        best = np.full((N, 8, W), E, np.int64); np.minimum.at(best, (ai, gi, cell), lane + np.zeros_like(cell))
        win = np.take_along_axis(best, cell, 2) == lane
        XB = X[bi]; a, g, e = np.nonzero(win & com); c = cell[a, g, e]
        XB[a, g, :, c] = (XB[a, g, :, c] + ev[a, g, :, e]) >> 1
        X[bi] = XB
        if t < RO - 1:
            a, g, e = np.nonzero(win & (com | late)); PB[a, g, ks[a, g, e], cell[a, g, e]] = W
            a, g, e = np.nonzero(win); PB[a, g, (e + t) % 16, cell[a, g, e]] = q[a, g, e]
            P[bi] = PB
        v = np.where((rows == kk) & com[:, :, None], L, R) + M * np.where(orphan[:, :, None], 255 - y, y) + 1
        R = np.where(v >= W, v - W, v); z = y
    return {"xo": X.reshape(N, 128, W).astype(np.float32).astype(BF), "ro": R.reshape(N, 128, E).astype(np.float32), "zo": z.reshape(N, 128, E).astype(np.float32).astype(BF)}

@@ -1,0 +1,599 @@
+from concourse.mybir import AluOpType as Op, ActivationFunctionType as AF, AxisListType as AX
+
+W, E, RO, WIN, DUMP = 3072, 256, 4, 3584, 3328
+OFF = 1536.0
+BIG = float(2 ** 20)
+MAGIC = 12582912.0
+BF, F32, F16, I32, U16 = "bfloat16", "float32", "float16", "int32", "uint16"
+CFG = {
+    "lg": [("a", 0, 64), ("v", 192, 256), ("a", 64, 128), ("v", 160, 192), ("a", 128, 160)],
+    "sign": (0, 1),
+    "yg": [(0, k) for k in range(4)] + [(1, k) for k in range(9)],
+    "eqa": (12, 13, 14, 15),
+}
+
+
+def _s(n, d):
+    return ("sbuf", [128] + (n if isinstance(n, list) else [n]), d)
+
+
+SCRATCH = {
+    "XO": _s(WIN, BF), "XR": _s(WIN, BF), "PI": _s(W, I32), "PF": _s(WIN, F32),
+    "rds": _s(E, I32), "zs": _s(E, BF), "rdr": _s(E, I32),
+    "GL": _s(4096, F16), "GX": _s(4096, BF), "MX": _s(4096, BF), "MN": _s(4096, BF),
+    "YR": _s(4096, BF), "D": _s(4096, BF), "AB": _s([16, 256], BF), "GE": _s([16, 256], BF),
+    "E1": _s([16, 272], BF), "E2": _s([16, 272], BF), "EA": _s(E, BF),
+    "Ro": _s(E, F16), "Ru": _s(E, U16), "Lo": _s(E, F16), "Lu": _s(E, U16), "Rp": _s(E, F32), "Rq": _s(E, U16),
+    "FR": _s(E, BF), "SU": _s(512, F32), "N2": _s(E, BF), "OG": _s(E, BF), "OR": _s(E, BF), "U": _s(E, BF),
+    "t1": _s(E, F32), "DL": _s(E, F32), "JG": _s(E, BF), "C1": _s(E, F32), "C2": _s(E, F32), "CS": _s(E, BF),
+    "GK": _s(E, F32), "KY": _s(E, F32), "KS": _s(E, I32), "SB": _s(768, F16), "TB": _s(512, F16), "DK": _s(E, BF),
+    "EV": _s(E, BF), "MM": _s(E, F32), "NL": _s(E, BF), "LW": _s(E, BF), "LN": _s(512, BF), "SG": _s(E, BF),
+    "PT": _s(E, F32), "SX": _s(E, F32), "RS": _s(E, F32), "rr": _s(E, F32), "zr": _s(E, BF),
+    "sf": _s(256, F32), "si": _s(128, I32), "su": _s(128, U16),
+    "Ys": _s([RO, E], BF), "Yr": _s([RO, E], BF), "Ns": _s([RO, E], I32), "Nr": _s([RO, E], I32),
+    "qs": _s(RO * 16, U16), "qr": _s(RO * 16, U16), "ws": _s(RO * 16, U16), "wr": _s(RO * 16, U16),
+    "xs": _s(RO * 32, U16), "xr": _s(RO * 16, U16),
+    "COL": _s(E, F32), "CM": _s(272, F32), "IO": _s(512, F32), "pi": _s(16, I32), "pc": _s(16, F32),
+    "MK": _s(48, F32), "REL": _s(128, BF), "OH": _s(2048, BF), "DG": _s(2048, BF), "S0": _s(2048, BF),
+    "MB": _s(128 * 14, BF), "MF": _s(128 * 4, F32), "RS0": _s(1024, BF), "RS1": _s(1024, BF),
+    "KC": _s(E, BF), "C21": _s(E, BF), "NH": _s(E, BF), "ZE": _s(512, BF), "ZC": _s(E, BF), "TH": _s(E, BF),
+    "CT": _s(3 * E, F32), "TT": _s(9 * 64, F32), "TS": _s(1024, F32), "J": _s(128, BF), "cT": _s(80, F32),
+    "C16": _s(64, BF),
+}
+for _b in range(8):
+    SCRATCH["B%d" % _b] = ("psum", [128, 512], F32)
+MSG = ["y", "w", "n"]
+SEMAPHORES = (["v", "a", "p", "c", "sent", "left", "r_rd", "r_z", "r_x", "r_ro", "r_zo"]
+              + ["r_%s%d" % (m, t) for m in MSG for t in range(RO)] + ["d%d" % k for k in range(16)])
+
+
+def rank_program(g, core, T, topo):
+    rank = T.rank_of(core)
+    if rank is None:
+        return
+    N = len(T.cores)
+    nxt, prv = T.cores[(rank + 1) % N], T.cores[(rank - 1) % N]
+    Q = {"v": g.vector, "a": g.scalar, "p": g.tensor, "c": g, "s": g.sync}
+    ops = []
+    ndma = [0]
+    out_cnt = {"sent": 0, "left": 0}
+
+    def a(name, lo=0, hi=None, step=1):
+        hi = SCRATCH[name][1][1] if hi is None else hi
+        return (T[name][:, lo:hi:step] if step > 1 else T[name][:, lo:hi], [(name, lo, hi, step)])
+
+    def a3(name, r0, r1, lo, hi):
+        n = SCRATCH[name][1][2]
+        ap = T[name][:, r0, lo:hi] if r1 == r0 + 1 else T[name][:, r0:r1, lo:hi]
+        return (ap, [(name, r0 * n + lo, (r1 - 1) * n + hi, 1)])
+
+    def ind(win, off):
+        return (win[0].indirect(off[0]), win[1], off[1])
+
+    def val(x):
+        return x[0] if isinstance(x, tuple) else x
+
+    def op(eng, fn, outs, ins, **kw):
+        wr, rd = [], []
+        for o in outs:
+            wr += o[1]
+            if len(o) > 2:
+                rd += o[2]
+        for i in ins:
+            if isinstance(i, tuple):
+                rd += i[1] + (i[2] if len(i) > 2 else [])
+        d = {"eng": eng, "fn": fn, "wr": wr, "rd": rd}
+        d.update(kw)
+        ops.append(d)
+
+    def cp(out, in_):
+        op("v", lambda: g.vector.tensor_copy(out[0], in_[0]), [out], [in_])
+
+    def tt(out, x, y, o):
+        op("v", lambda: g.vector.tensor_tensor(out[0], x[0], y[0], o), [out], [x, y])
+
+    def ts(out, x, s1, o0, s2=None, o1=None):
+        if o1 is None:
+            op("v", lambda: g.vector.tensor_scalar(out[0], x[0], val(s1), None, o0), [out], [x, s1])
+        else:
+            op("v", lambda: g.vector.tensor_scalar(out[0], x[0], val(s1), val(s2), o0, o1), [out], [x, s1, s2])
+
+    def scan(out, d0, d1, o0, o1):
+        op("v", lambda: g.vector.tensor_tensor_scan(out[0], d0[0], d1[0], 0.0, o0, o1), [out], [d0, d1])
+
+    def ms(out, c):
+        op("v", lambda: g.vector.memset(out[0], c), [out], [])
+
+    def act(out, x, f=AF.Identity, bias=0.0, scale=1.0):
+        op("a", lambda: g.scalar.activation(out[0], x[0], f, bias=val(bias), scale=val(scale)), [out], [x, bias, scale])
+
+    def mm(out, l, r, st, sp):
+        op("p", lambda: g.tensor.matmul(out[0], l[0], r[0], st, sp), [out], [l, r])
+
+    def mms(out, pairs, st=True, sp=True):
+        for k, (l, r) in enumerate(pairs):
+            mm(out, l, r, st and k == 0, sp and k == len(pairs) - 1)
+
+    def iota(out, pat, base=0, cm=0, flag=True):
+        op("c", lambda: g.iota(out[0], pat, base, cm, allow_small_or_imprecise_dtypes=True) if flag
+           else g.iota(out[0], pat, base, cm), [out], [])
+
+    def gcopy(out, in_, n):
+        op("c", lambda: g.affine_select(out[0], in_[0], [[0, n]], Op.is_gt, 0.0, 1, 0), [out], [in_])
+
+    def dma(eng, out, in_):
+        s = "d%d" % ndma[0]
+        ndma[0] += 1
+        op(eng, lambda: Q[eng].dma_start(out[0], in_[0]), [out], [in_], sem=s, val=16)
+
+    def send(dst, out, in_, sem):
+        rid, pid, _ = topo.addr(dst)
+        loc = "left" if sem == "r_x" else "sent"
+        out_cnt[loc] += len(topo.engines(core, dst))
+        op("c", lambda: g.remote_dma(out[0], in_[0], T.sem[sem], T.sem[loc], pid, rid, topo.mask(core, dst)), [], [in_],
+           remote=loc, val=out_cnt[loc])
+
+    def recv(src, bufs, sem):
+        op("x", None, bufs, [], sem=sem, val=len(bufs) * len(topo.engines(src, core)))
+
+    def gather(eng, out, win, off):
+        if eng == "a":
+            act(out, ind(win, off))
+        else:
+            cp(out, ind(win, off))
+
+    def hbm(name, lo=None, hi=None):
+        return (T[name][:] if lo is None else T[name][:, lo:hi], [])
+
+    def m(buf, k):
+        return a(buf, 128 * k, 128 * k + 128)
+    ID, BLK, W1, IB, NIB, NBLK, HID, WD, B2, I1536, I255, NID, I12, TMP = [m("MB", k) for k in range(14)]
+    IDf, NIDf, BLKf, TMPf = [m("MF", k) for k in range(4)]
+    pp, pm, gb, cz, p2 = [a("pc", k, k + 1) for k in range(5)]
+    iT, b12, b16, dum2 = a("cT", 0, 16), a("cT", 16, 32), a("cT", 32, 48), a("cT", 48, 80)
+    KK, COM, SET, TOH, TOC, TOL, TNC, TNL, TOS = [a("TT", 64 * k, 64 * k + 64) for k in range(9)]
+    qf, oT, dq, kq, om, nl, tT, lm = (a("sf", 0, 16), a("sf", 16, 32), a("sf", 32, 48), a("sf", 48, 64), a("sf", 64, 80),
+                                      a("sf", 80, 96), a("sf", 96, 128), a("sf", 128, 160))
+    wT, ef, lw, ntT = a("sf", 160, 176), a("sf", 176, 192), a("sf", 192, 208), a("sf", 208, 240)
+    yi, y7, cd, kk, c33 = [a("si", 16 * k, 16 * k + 16) for k in range(5)]
+    q0, jl, cu, el, c1l = [a("su", 16 * k, 16 * k + 16) for k in range(5)]
+    XO, XR, PF = a("XO"), a("XR"), a("PF")
+    H = W // 2
+
+    dma("s", a("rds"), hbm("rd"))
+    dma("a", a("zs"), hbm("z0"))
+    dma("s", a("XO", 0, H), hbm("x0", 0, H))
+    for k in range(4):
+        dma("a" if k < 2 else "s", a("PI", 768 * k, 768 * k + 768), hbm("lk", 768 * k, 768 * k + 768))
+    dma("s", a("XO", H, W), hbm("x0", H, W))
+    iota(a("pi", 0, 1), [[0, 1]], 0, 1, False)
+    iota(a("COL"), [[1, 256]])
+    iota(KK, [[0, 2], [-1, 16], [0, 2]], 15)
+    iota(COM, [[0, 32], [1, 2]])
+    iota(SET, [[1, 2], [0, 32]])
+    send(nxt, a("rdr"), a("rds"), "r_rd")
+    send(nxt, a("XO", W, W + E), a("zs"), "r_z")
+    iota(a("IO", 0, 256), [[0, 16], [-2, 16]], 62)
+    send(prv, a("XR", 0, H), a("XO", 0, H), "r_x")
+    iota(a("IO", 256, 384), [[0, 16], [1, 8]])
+    iota(a("IO", 384, 512), [[1, 16], [0, 8]])
+    iota(a("CM"), [[0, 17], [1, 16]])
+    send(prv, a("XR", H, W), a("XO", H, W), "r_x")
+    recv(prv, [a("rdr")], "r_rd")
+    recv(prv, [a("XO", W, W + E)], "r_z")
+    recv(nxt, [a("XR", 0, H), a("XR", H, W)], "r_x")
+
+    ms(a("RS0"), 1.0)
+    ms(a("ZE"), 0.0)
+    cp(pp, a("pi", 0, 1))
+    ts(a("pi", 4, 5), a("pi", 0, 1), 15, Op.bitwise_and)
+    ms(a("RS1"), 0.0)
+    cp(pm, a("pi", 4, 5))
+    c128 = a("COL", 0, 128)
+    ts(ID, c128, pp, Op.is_equal)
+    tt(gb, pp, pm, Op.subtract)
+    ts(a("MK", 0, 16), a("COL", 0, 16), pm, Op.is_equal)
+    ts(a("REL"), c128, gb, Op.subtract)
+    ts(IDf, c128, pp, Op.is_equal)
+    act(TMPf, a("REL"), AF.Abs, bias=-7.5)
+    for k in range(16):
+        act(m("DG", k), ID, scale=a("MK", k, k + 1))
+    ms(a("RS0", 0, 1024, 16), 0.0)
+    ms(a("RS1", 0, 1024, 16), 512.0)
+    ts(BLK, TMPf, 8.0, Op.is_lt)
+    ts(BLKf, TMPf, 8.0, Op.is_lt)
+    ts(TMP, c128, pp, Op.is_gt, -4096.0, Op.mult)
+    ts(IB, ID, 4096.0, Op.mult)
+    tt(TMP, TMP, BLK, Op.mult)
+    ts(cz, a("MK", 1, 2), 3073.0, Op.mult, -1.0, Op.add)
+    tt(W1, TMP, IB, Op.add)
+    tt(cz, cz, a("MK", 0, 1), Op.add)
+    for k in range(16):
+        ts(m("OH", k), a("REL"), float(k), Op.is_equal)
+    ts(a("ZC"), a("COL"), a("MK", 0, 1), Op.mult, cz, Op.add)
+    ms(a("PF", W, WIN), 0.0)
+    ms(a("XO", DUMP, WIN), 0.0)
+    ms(a("XR", W, WIN), 0.0)
+    ms(a("NH"), -0.5)
+    ts(a("XR", W, W + 1), pm, 8.0, Op.is_lt, 513.0, Op.mult)
+    ts(iT, a("COL", 0, 16), 16.0, Op.mult, pm, Op.add)
+    ts(a("XR", W, W + 1), a("XR", W, W + 1), -1.0, Op.add)
+    for mat, src, c in ((NIB, ID, -4096.0), (NBLK, BLK, -4096.0), (HID, ID, 0.5), (I1536, ID, -1536.0),
+                        (I255, ID, 255.0), (NID, ID, -1.0), (I12, ID, 12.0), (B2, BLK, 2.0)):
+        act(mat, src, scale=c)
+    act(a("PF", 0, 768), a("PI", 0, 768), bias=-OFF)
+    act(a("S0"), a("OH"), scale=a("MK", 0, 1))
+    ts(a("PF", 768, 1536), a("PI", 768, 1536), -OFF, Op.add)
+    act(b12, iT, scale=12.0)
+    act(b16, iT, scale=16.0, bias=15.0)
+    act(a("cT", 48, 64), iT, bias=DUMP - OFF)
+    act(a("cT", 64, 80), iT, bias=DUMP - OFF)
+    act(qf, iT, scale=12.0)
+    ts(q0, iT, 12.0, Op.mult)
+    cp(a("Ru"), a("rdr"))
+    ts(a("Ro"), a("rdr"), -OFF, Op.add)
+    act(a("PF", 1536, 2304), a("PI", 1536, 2304), bias=-OFF)
+    ms(a("C21"), 2 * BIG)
+    ms(a("C16"), 16.0)
+    ts(a("KC"), a("IO", 0, 256), 0.5, Op.add)
+    ts(a("PF", 2304, 2688), a("PI", 2304, 2688), -OFF, Op.add)
+    act(a("PF", 2688, W), a("PI", 2688, W), bias=-OFF)
+
+    def tables():
+        ts(a("SG"), a("RS0", 0, 256), 0.5, Op.mult)
+        ts(a("LW"), a("RS1", 0, 256), -1.0 / 256, Op.mult)
+        ts(TOH, KK, pm, Op.is_equal)
+        scan(a("TH"), a("SG"), a("LW"), Op.mult, Op.add)
+        tt(TOC, TOH, COM, Op.mult)
+        tt(TOS, TOH, SET, Op.mult)
+        tt(a("MK", 16, 32), a("TH", 0, 16), a("MK", 0, 16), Op.mult)
+        ts(a("MK", 32, 48), a("MK", 0, 16), -0.5, Op.add)
+        op("v", lambda: g.vector.tensor_reduce(p2[0], T.MK[:, 16:32], AX.X, Op.add), [p2], [a("MK", 16, 32)])
+        tt(TOL, TOS, TOC, Op.subtract)
+        tt(TNL, COM, SET, Op.subtract)
+        ts(WD, BLK, p2, Op.mult, -0.5, Op.mult)
+        ts(TNC, COM, -4352.0, Op.mult, 4096.0, Op.add)
+        ts(TNL, TNL, 4.0, Op.mult, 4.0, Op.add)
+        ts(a("IO", 384, 512), a("IO", 384, 512), pm, Op.is_equal)
+        ts(a("pi", 8, 12), a("COL", 0, 4), pm, Op.add)
+        tt(a("J"), a("IO", 384, 512), a("IO", 256, 384), Op.mult)
+        ts(a("pi", 12, 16), a("pi", 8, 12), 15, Op.bitwise_and)
+        ts(a("PT"), a("COL"), 12.0, Op.mult, -3072.0, Op.add)
+        ts(a("pc", 5, 8), a("pi", 12, 15), 8.0, Op.mult)
+        ts(a("pc", 8, 11), a("pi", 12, 15), 64.0, Op.mult)
+
+    def lock_rows(t):
+        ts(a("CT", E * t, E * t + E), a("CM", t, t + E), pm, Op.is_equal)
+        tt(a("CT", E * t, E * t + E), a("CT", E * t, E * t + E), a("PT"), Op.mult)
+
+    def to_list(out, mats, src, n, st=True, sp=True):
+        mms(out, [(m(mats, k), a(src[0], src[1] + k, src[1] + n, 16)) for k in range(16)], st, sp)
+
+    def own_update(t):
+        recv(prv, [a("wr", 16 * t, 16 * t + 16)], "r_w%d" % t)
+        cp(ind(XO, a("wr", 16 * t, 16 * t + 16)), a("ZE", 0, E))
+        xl = a("xs", 32 * t + 16, 32 * t + 32)
+        tt(a("SX"), ind(XO, xl), a("EV"), Op.add)
+        nw = a3("Ns", t, t + 1, 0, E)
+        ts(nw, a("SX"), 0.5, Op.mult, -0.25, Op.add)
+        if t < RO - 1:
+            send(prv, a3("Nr", t, t + 1, 0, E), nw, "r_n%d" % t)
+            send(prv, a("xr", 16 * t, 16 * t + 16), xl, "r_n%d" % t)
+        cp(ind(XO, xl), nw)
+
+    def pairs_a(Eb, src0, col):
+        for f in range(2):
+            for b in CFG["eqa"]:
+                e = a3(Eb, b, b + 1, 0, 256 - 16 * b)
+                if f == 0:
+                    act(e, a("TB", src0 + 16 * b, src0 + 256), AF.Abs, bias=a("sf", col + b, col + b + 1), scale=-1.0)
+                else:
+                    act(e, e, AF.Relu, bias=1.0, scale=-1.0)
+
+    def pairs(Eb, src0, col, out, extra):
+        bank, lo, hi = out[1][0][:3]
+        mms(out, [(ID, a("TH"))] + extra, True, False)
+        for b in range(16):
+            if b not in CFG["eqa"]:
+                ts(a3(Eb, b, b + 1, 0, 256 - 16 * b), a("TB", src0 + 16 * b, src0 + 256), a("sf", col + b, col + b + 1), Op.is_equal)
+            if b < 15:
+                mm(a(bank, lo + 16 * b + 16, hi), B2, a3(Eb, b, b + 1, 16, 256 - 16 * b), False, False)
+        mm(out, WD, a3(Eb, 0, 16, 0, 16), False, True)
+
+    for t in range(RO):
+        last = t == RO - 1
+        Y = a3("Ys", t, t + 1, 0, E)
+        mms(a("B0", 0, 256), [(ID, a("ZE", 0, E))], True, False)
+        mms(a("B1"), [(ID, a("ZE"))], True, False)
+        mms(a("B1", 0, 256), [(ID, a("Ro"))], False, False)
+        mms(a("B1", 256, 512), [(ID, a("Ro"))], False, False)
+        mms(a("B2", 0, 256), [(ID, a("ZC"))], True, False)
+        for eng, lo, hi in CFG["lg"]:
+            gather(eng, a("GL", 16 * lo, 16 * hi), PF, a("Ru", lo, hi))
+        for c in (0, 3, 1, 2):
+            mms(a("B0", 64 * c, 64 * c + 64), [(m("DG", k), a("GL", 1024 * c + k, 1024 * c + 1024, 16)) for k in range(16)],
+                False, c == 2)
+        if t == 0:
+            tables()
+        else:
+            act(a("EV"), a("B6", 256, 512))
+            own_update(t - 1)
+        act(a("FR"), a("B0", 0, 256), AF.Relu, bias=-1535.0)
+        mms(a("B1", 0, 256), [(W1, a("FR"))], False, False)
+        mms(a("B1", 256, 512), [(IB, a("FR"))], False)
+        mms(a("B2", 0, 256), [(NBLK, a("FR"))], False)
+        act(a("Lo"), a("B0", 0, 256))
+        act(a("SU", 0, 256), a("B1", 0, 256), AF.Relu, bias=OFF - 4096.0)
+        act(a("N2"), a("B2", 0, 256), AF.Relu)
+        act(a("SU", 256, 512), a("B1", 256, 512), AF.Relu, bias=OFF - 4096.0)
+        mms(a("B3", 256, 512), [(NIB, a("FR")), (BLKf, a("SU", 0, 256)), (BLK, a("N2"))])
+        mms(a("B0", 0, 256), [(ID, a("Lo")), (NID, a("Ro"))])
+        tt(a("Rp"), a("B3", 256, 512), a("SU", 256, 512), Op.max)
+        cp(a("Rq"), a("Rp"))
+        for c in range(4):
+            gather("a", a("GX", 1024 * c, 1024 * c + 1024), XO, a("Rq", 64 * c, 64 * c + 64))
+        ql = q0 if t == 0 else a("qs", 16 * t - 16, 16 * t)
+        if t == 0:
+            for u in range(RO - 1):
+                lock_rows(u)
+        else:
+            cp(ind(XR, a("ws", 16 * t - 16, 16 * t)), a("ZE", 0, E))
+        tt(dq, b12, qf, Op.subtract)
+        for c in range(4):
+            lo, hi = 1024 * c, 1024 * c + 1024
+            if c == 2 and t > 0:
+                recv(nxt, [a3("Nr", t - 1, t, 0, E), a("xr", 16 * t - 16, 16 * t)], "r_n%d" % (t - 1))
+                cp(ind(XR, a("xr", 16 * t - 16, 16 * t)), a3("Nr", t - 1, t, 0, E))
+            scan(a("MX", lo, hi), a("RS0"), a("GX", lo, hi), Op.mult, Op.max)
+            scan(a("MN", lo, hi), a("RS1"), a("GX", lo, hi), Op.add, Op.min)
+            if c == 2:
+                act(a("OG"), ind(XR, ql))
+            if c == 3:
+                to_list(a("B4", 0, 16), "OH", ("OG", 0), 256)
+            if c >= 2:
+                l0, l1, bank = (0, 192, "B3") if c == 2 else (192, 256, "B6")
+                mms(a(bank, l0, l1), [(ID, a("NH", l0, l1)), (ID, a("MX", 16 * l0 + 15, 16 * l1, 16)), (ID, a("MN", 16 * l0 + 15, 16 * l1, 16))])
+                act(a("t1", l0, l1), a(bank, l0, l1), bias=MAGIC, scale=0.5)
+                act(a3("Ys", t, t + 1, l0, l1), a("t1", l0, l1), bias=-MAGIC)
+        ts(a("Lu"), a("Lo"), OFF, Op.add)
+        ts(oT, a("B4", 0, 16), 0.0, Op.is_equal)
+        tt(dq, dq, oT, Op.mult)
+        tt(kq, dq, qf, Op.add)
+        mms(a("B4", 16, 32), [(m("S0", k), (T.Ys[:, t, k:E:16], Y[1])) for k in range(16)])
+        mms(a("B5", 0, 256), [(ID, a("KC")), (ID, a("C21"))], True, False)
+        def spread(h, k):
+            o, i = a("YR", 2048 * h + k, 2048 * h + 2048, 16), a3("Ys", t, t + 1, 128 * h, 128 * h + 128)
+            if (h, k) in CFG["yg"]:
+                gcopy(o, i, 128)
+            else:
+                act(o, i)
+        late = CFG["yg"][4:]
+        for h in range(2):
+            for k in range(16):
+                if (h, k) not in late:
+                    spread(h, k)
+        cp(yi, a("B4", 16, 32))
+        ts(y7, yi, 7, Op.bitwise_and)
+        tt(om, y7, oT, Op.mult)
+        tt(qf, om, kq, Op.add)
+        ql = a("qs", 16 * t, 16 * t + 16)
+        cp(ql, qf)
+        cp(ind(XR, ql), Y)
+        send(nxt, a3("Yr", t, t + 1, 0, E), Y, "r_y%d" % t)
+        send(nxt, a("qr", 16 * t, 16 * t + 16), ql, "r_y%d" % t)
+        for h, k in late:
+            spread(h, k)
+        if last:
+            send(prv, a("zr"), Y, "r_zo")
+        mms(a("B7", 0, 256), [(BLK, a("OG"))])
+        act(a("OR"), a("B7", 0, 256), AF.Relu, bias=1.0, scale=-1.0)
+        mms(a("B7", 256, 512), [(I255, a("OR")), (NID, Y)])
+        act(a("DL"), a("B0", 0, 256))
+        for c in range(4):
+            lo, hi = 1024 * c, 1024 * c + 1024
+            tt(a("D", lo, hi), ind(XR, a("Lu", 64 * c, 64 * c + 64)), a("YR", lo, hi), Op.subtract)
+            act(a3("AB", 4 * c, 4 * c + 4, 0, 256), a("D", lo, hi), AF.Abs, scale=64.0)
+            ge = [(m("OH", k), a3("GE", 4 * c, 4 * c + 4, 16 * k, 16 * k + 16)) for k in range(16)]
+            if c in CFG["sign"]:
+                act(a3("GE", 4 * c, 4 * c + 4, 0, 256), a("D", lo, hi), AF.Sign, bias=0.5)
+                ge = [(ID, a("C16"))] + ge
+            else:
+                ts(a3("GE", 4 * c, 4 * c + 4, 0, 256), a("D", lo, hi), 0.0, Op.is_ge, 2.0, Op.mult)
+            if c == 1:
+                act(a("U"), a("B7", 256, 512), AF.Abs)
+                if not last:
+                    tt(dq, qf, b12, Op.subtract)
+                    ts(jl, dq, a("pc", 5 + t, 6 + t), Op.add)
+            if c == 2 and not last:
+                act(a("JG"), ind(a("J"), jl))
+            if c not in CFG["sign"]:
+                mms(a("B6", 64 * c, 64 * c + 64), ge)
+            mms(a("B5", 64 * c, 64 * c + 64), [(m("OH", k), a3("AB", 4 * c, 4 * c + 4, 16 * k, 16 * k + 16)) for k in range(16)], False, False)
+            if c in CFG["sign"]:
+                mms(a("B6", 64 * c, 64 * c + 64), ge)
+        recv(prv, [a3("Yr", t, t + 1, 0, E), a("qr", 16 * t, 16 * t + 16)], "r_y%d" % t)
+        cp(ind(XO, a("qr", 16 * t, 16 * t + 16)), a3("Yr", t, t + 1, 0, E))
+        act(a("CS"), a("B6", 0, 256), AF.Sign, bias=-17.0)
+        mms(a("B5", 0, 256), [(HID, a("CS"))], False)
+        act(a("GK"), a("B6", 0, 256), AF.Abs, bias=-6.5 * BIG, scale=BIG / 2)
+        mms(a("B7", 0, 256), [(ID, a("Ro")), (I12, a("U"))], True, False)
+        if not last:
+            act(a("XO", W, W + E), Y)
+        if t == 0:
+            for k in range(16):
+                act(a("TS", 64 * k, 64 * k + 64), TOS, AF.Sign, bias=a("MK", 32 + k, 33 + k))
+        tt(a("KY"), a("B5", 0, 256), a("GK"), Op.min)
+        if not last:
+            mms(a("B6", 256, 512), [(IDf, a("CT", E * t, E * t + E)), (ID, a("JG"))])
+            act(a("C2"), a("B6", 256, 512))
+        mms(a("B5", 0, 256), [(ID, a("Ro")), (I12, a("U"))], True, False)
+        scan(a("KS"), a("RS0", 0, 256), a("KY"), Op.mult, Op.max)
+        ts(cd, a("KS", 15, 256, 16), 63, Op.bitwise_and)
+        cp(cu, cd)
+        tt(a("SB", 256, 512), ind(TOH, cu), a("Ro"), Op.mult)
+        tt(a("SB", 0, 256), ind(TOL, cu), a("Lo"), Op.mult)
+        act(a("LN", 256, 512), ind(TNC, cu))
+        act(a("NL"), ind(TNL, cu))
+        h0, h1 = (0, 256) if last else (256, 0)
+        mms(a("B0", 256, 512), [(BLK, a("SB", 256, 512))])
+        mms(a("B3", 0, 256), [(BLK, a("SB", 0, 256))])
+        to_list(a("B4", 32, 64), "OH", ("SB", 0), 512)
+        act(a("TB", h0, h0 + 256), a("B0" if h0 else "B3", h0, h0 + 256))
+        act(tT, a("B4", 32, 64))
+        tt(a("MM"), ind(TOC, cu), a("DL"), Op.mult)
+        ts(c33, cd, 33, Op.bitwise_and)
+        ts(kk, cd, 1, Op.logical_shift_right, 15, Op.bitwise_and)
+        ts(nl, c33, 32.0, Op.not_equal, 5000.0, Op.mult)
+        tt(ef, b16, kk, Op.subtract)
+        if not last:
+            ts(c1l, cd, a("pc", 8 + t, 9 + t), Op.add)
+        cp(el, ef)
+        tt(wT, a("sf", 96, 112), nl, Op.add)
+        mms(a("B7", 0, 256), [(IDf, a("MM"))], False)
+
+        def second_half():
+            act(a("TB", h1, h1 + 256), a("B0" if h1 else "B3", h1, h1 + 256))
+
+        def winners():
+            pairs("E2", 256, 112, a("B2", 0, 256), [])
+
+        def winners_b():
+            act(a("LN", 0, 256), a("B2", 0, 256), AF.Relu, scale=float(2 ** 24))
+            mms(a("B3", 0, 32), [(ID, a("ZE", 0, 32))], True, False)
+            mms(a("B3", 0, 16), [(IDf, a("sf", 112, 128))], False, False)
+            to_list(a("B3", 0, 32), "OH", ("LN", 0), 512, False)
+
+        def winner_lists():
+            tt(lm, a("B3", 0, 32), dum2, Op.min)
+            tt(a("sf", 144, 160), a("sf", 128, 144), a("sf", 144, 160), Op.max)
+            ts(a("xs", 32 * t, 32 * t + 32), lm, OFF, Op.add)
+
+        def wipes():
+            pairs("E1", 0, 160, a("B1", 0, 256), [(ID, a("NL"))])
+
+        def wipes_b():
+            act(a("LW"), a("B1", 0, 256), AF.Relu, scale=float(2 ** 24))
+            mms(a("B4", 32, 48), [(IDf, a("sf", 96, 112))], True, False)
+            to_list(a("B4", 32, 48), "OH", ("LW", 0), 256, False)
+
+        def wipe_list():
+            wl = a("ws", 16 * t, 16 * t + 16)
+            tt(lw, a("B4", 32, 48), a("cT", 48, 64), Op.min)
+            ts(wl, lw, OFF, Op.add)
+            send(nxt, a("wr", 16 * t, 16 * t + 16), wl, "r_w%d" % t)
+
+        def move_a():
+            act(a("SG"), a("B7", 0, 256), AF.Sign, bias=-1534.5)
+
+        def move_p():
+            mms(a("B5", 0, 256), [(IDf, a("MM")), (I1536, a("SG"))], False)
+
+        def move_b():
+            if last:
+                act(a("RS"), a("B5", 0, 256), bias=1.0)
+                send(prv, a("rr"), a("RS"), "r_ro")
+            else:
+                act(a("Ro"), a("B5", 0, 256), bias=1.0 - OFF)
+
+        def partner():
+            mms(a("B6", 256, 512), [(ID, Y), (ID, a("DK"))])
+            act(a("EV"), a("B6", 256, 512))
+
+        if last:
+            pairs_a("E1", 0, 160)
+            second_half()
+            move_a()
+            wipes()
+            wipes_b()
+            pairs_a("E2", 256, 112)
+            winners()
+            wipe_list()
+            move_p()
+            move_b()
+            winners_b()
+            act(a("DK"), ind(a("D"), el))
+            partner()
+            winner_lists()
+        else:
+            pairs_a("E2", 256, 112)
+            second_half()
+            move_a()
+            winners()
+            winners_b()
+            move_p()
+            pairs_a("E1", 0, 160)
+            act(a("C1"), ind(a("TS"), c1l), bias=-256.0, scale=1792.0)
+            move_b()
+            wipes()
+            winner_lists()
+            pl = a("xs", 32 * t, 32 * t + 16)
+            tt(a("PT"), ind(PF, pl), a("C1"), Op.max)
+            ts(a("Ru"), a("Ro"), OFF, Op.add)
+            act(a("DK"), ind(a("D"), el))
+            wipes_b()
+            tt(ind(PF, pl), a("PT"), a("C2"), Op.add)
+            wipe_list()
+            mms(a("B6", 256, 512), [(ID, Y), (ID, a("DK"))])
+    own_update(RO - 1)
+    recv(nxt, [a("zr")], "r_zo")
+    dma("s", hbm("zo"), a("zr"))
+    recv(nxt, [a("rr")], "r_ro")
+    dma("s", hbm("ro"), a("rr"))
+    dma("s", hbm("xo", 0, H), a("XO", 0, H))
+    dma("a", hbm("xo", H, W), a("XO", H, W))
+
+    def meet(x, y, cross):
+        if cross and SCRATCH[x[0]][0] == "psum":
+            return True
+        if x[1] >= y[2] or y[1] >= x[2]:
+            return False
+        return not (x[3] > 1 and x[3] == y[3] and (x[1] - y[1]) % x[3])
+
+    seen = {}
+    for j, o in enumerate(ops):
+        deps = {}
+        for r, w in [(r, False) for r in o["rd"]] + [(r, True) for r in o["wr"]]:
+            ps = SCRATCH[r[0]][0] == "psum"
+            for (i, r2, w2) in seen.get(r[0], []):
+                p = ops[i]
+                cross = p["eng"] != o["eng"]
+                if ps and not cross and o["eng"] == "p":
+                    continue
+                if (w or w2 or (ps and cross)) and meet(r, r2, cross) and not p.get("remote"):
+                    key = p.get("sem", p["eng"])
+                    deps[key] = max(deps.get(key, -1), i)
+                elif w and p.get("remote") and meet(r, r2, cross):
+                    assert p["remote"] == "left"
+                    deps["left"] = max(deps.get("left", -1), i)
+        o["deps"] = {} if o["eng"] == "x" else deps
+        for r, w in [(r, False) for r in o["rd"]] + [(r, True) for r in o["wr"]]:
+            seen.setdefault(r[0], []).append((j, r, w))
+    done = {}
+    for o in ops:
+        keep = {}
+        for key, i in o["deps"].items():
+            if done.get((o["eng"], key), -1) < i:
+                done[(o["eng"], key)] = i
+                keep[key] = i
+                ops[i]["inc"] = True
+        o["deps"] = keep
+    cnt = {"v": 0, "a": 0, "p": 0, "c": 0}
+    for o in ops:
+        if o["eng"] == "x":
+            continue
+        q = Q[o["eng"]]
+        for key, i in o["deps"].items():
+            q.wait_ge(T.sem[key], ops[i]["val"])
+        ins = o["fn"]()
+        if o.get("remote"):
+            continue
+        if "sem" in o:
+            ins.then_inc(T.sem[o["sem"]], 16)
+        elif o.get("inc"):
+            cnt[o["eng"]] += 1
+            o["val"] = cnt[o["eng"]]
+            ins.then_inc(T.sem[o["eng"]], 1)
+    g.wait_ge(T.sem.sent, out_cnt["sent"])
+    for o in ops:
+        if "sem" in o and o["eng"] != "x" and not o.get("inc"):
+            Q[o["eng"]].wait_ge(T.sem[o["sem"]], 16)

@@ -1,16 +1,57 @@
+import numpy as np
 from concourse.mybir import AluOpType as Op, ActivationFunctionType as AF, AxisListType as AX
 
 W, E, RO, WIN, DUMP = 3072, 256, 4, 3584, 3328
 OFF = 1536.0
 BIG = float(2 ** 20)
-MAGIC = 12582912.0
+LOSE = float(2 ** 28)
 BF, F32, F16, I32, U16 = "bfloat16", "float32", "float16", "int32", "uint16"
+CYC, PE, SEM, GATHER, SCATTER, ISSUE, FLIGHT, START, LINK, HBM = 0.83, 0.42, 100, 1.56, 3.8, 600, 2300, 1800, 55, 220
+CALL, PCALL, FIRST = {"v": 75, "a": 40}, 3, 2000
+PASSES = 6
 CFG = {
-    "lg": [("a", 0, 64), ("v", 192, 256), ("a", 64, 128), ("v", 160, 192), ("a", 128, 160)],
-    "sign": (0, 1),
-    "yg": [(0, k) for k in range(4)] + [(1, k) for k in range(9)],
-    "eqa": (12, 13, 14, 15),
+    "dq": (((0, 8), (8, 16)), ((0, 16),), ((0, 16),), ((0, 8), (8, 16))),
+    "kcut": 16, "on_v": ("Y1", "DL"),
+    "gev": ((1, 0), (3, 0), (3, 8)),
+    "eqa2": (10, 11, 12, 13, 14, 15),
+    "eqa1": (10, 11, 12, 13, 14, 15),
+    "picks": (0, 256), "lax": False, "lscan": (0, 256), "zscan": (0, 256), "pk": 64, "kq": ((0, 1), (1, 2), (2, 3), (3, 4)),
+    "pairs": ("l", "w"), "pairline": None,
+    "s1line": None, "transitive": True,
+    "s1_0": (("L", "a", 0, 64), ("L", "v", 64, 128), ("P", 0), ("P", 1), ("L", "a", 128, 160), ("L", "v", 192, 256), ("F", 0),
+             ("L", "a", 160, 192), ("P", 2), ("P", 3), ("S", 0), ("R", 0), ("F", 1), ("X", "a", 0, 32), ("S", 1), ("R", 1), ("X", "v", 32, 64),
+             ("X", "a", 64, 128), ("X", "a", 128, 192), ("X", "a", 192, 224), ("X", "a", 224, 256)),
+    "s1": (("L", "a", 0, 64), ("L", "v", 64, 96), ("L", "a", 96, 128), ("P", 0), ("P", 1), ("L", "a", 128, 160), ("F", 0),
+           ("L", "a", 160, 192), ("P", 2), ("S", 0), ("L", "v", 224, 256), ("L", "a", 192, 224), ("R", 0), ("P", 3), ("F", 1),
+           ("X", "a", 0, 32), ("S", 1), ("R", 1), ("X", "a", 32, 64), ("X", "a", 64, 128), ("X", "v", 128, 160),
+           ("X", "a", 160, 192), ("X", "a", 192, 224), ("X", "a", 224, 256)),
+    "sc": ((0, 64), (64, 128), (128, 192), (192, 224), (224, 256)),
+    "yp": ((0, 256),), "cuts": (0, 768, 1792, W), "rz": (0, 1), "pl": True, "late": 0,
+    "gxv": 32,
 }
+ORDER = {"v": "GL:1024< GL:3072< XO:0<ZE SX Ns*<SX Rp:0< XO:0<Ns Rq:0< Rp:128 XR:0<ZE Rq:128 MN:1024< MX:1024< XR:0<Nr MX:0< MN:0< MX:2048< MX:3072< MN:3072< MN:2048< MX:3584< MN:3584< Lu YS si:0< si:16< sf:0< qs XR:0<Ys D:0< D:512< D:1024< D:3072< D:2560< D:2048< GE:2560< D:3584< GE:3072< GE:3584< XO:0<Yr KY KS si:32 su:32 SB:256 SB:0 MM E2 E1 su:48 sf:208<B4 sf:208<sf Ns*<sf PT Ru PF:0<PT sf:192 ws", "a": "GL:0< GL:2048< FR:0< Lo:0< SU:0< GL:3584< N2:0< FR:128 Lo:128 SU:256 N2:128 GX:1024< GX:0< GX:2048< GX:3072< OG GX:3584< OR Y4:0< Y4:1< Ys sf:16<si U Y4:2< sf:48<si Y4:3< SG JG DL AB:0< GE:0< GE:512< AB:512< C2 AB:1024< GE:1024< AB:2560< GE:2048< AB:2048< AB:3072< AB:3584< CS GK LN:0< NE TB:0< sf:112 sf:128 E2*<TB TB:256 sf:160 E2*<E2 sf:96 Ro LN:256 E1*<TB C1 E1*<E1 LW EV", "v0": "QM PF:0<PI OH GL:1024< GL:3072< PF:1536<PI Rp:0< Rq:0< Rp:128 GX:0< Rq:128 MX:1024< Lu MN:1024< MX:0< MN:0< MX:2048< MX:3072< MN:2048< MN:3072< MX:3584< MN:3584< YS si:0< si:16< sf:0< qs XR:0<Ys D:0< D:512< D:1024< D:3072< D:3584< D:2560< GE:3584< D:2048< GE:2560< XO:0<Yr GE:3072< KY KS si:32 su:32 SB:256 SB:0 MM E2 E1 su:48 sf:208<B4 sf:208<sf Ns*<sf PT PF:0<PT Ru sf:192 ws", "a0": "GL:0< GL:2048< FR:0< SU:0< Lo:0< N2:0< FR:128 Lo:128 SU:256 N2:128 GX:1024< GX:512< GX:2048< GX:3072< OG GX:3584< OR Y4:0< Y4:1< Ys sf:16<si Y4:2< sf:48<si Y4:3< U JG SG AB:0< GE:0< DL C2 GE:512< AB:512< GE:1024< AB:3072< AB:1024< AB:2560< GE:2048< AB:2048< AB:3584< CS GK TS LN:0< NE TB:0< sf:128 sf:112 TB:256 E2*<TB sf:160 E2*<E2 sf:96 Ro LN:256 E1*<TB C1 E1*<E1 LW EV", "v3": "GL:1024< GL:3072< XO:0<ZE SX Ns*<SX Rp:0< XO:0<Ns Rq:0< Rp:128 Rq:128 XR:0<ZE MN:1024< MX:1024< XR:0<Nr MX:0< MN:0< MX:3072< MN:3072< MX:2048< MN:2048< MX:3584< MN:3584< Lu YS si:0< si:16< sf:0< qs XR:0<Ys D:0< D:512< D:1024< D:3072< D:2560< D:2048< GE:2560< D:3584< GE:3072< GE:3584< XO:0<Yr KY KS si:32 su:32 SB:0 SB:256 MM E1 su:48 sf:192 ws E2 sf:208<B4 sf:208<sf Ns*<sf", "a3": "GL:0< GL:2048< FR:0< Lo:0< SU:0< GL:3584< N2:0< FR:128 Lo:128 SU:256 N2:128 GX:1024< GX:0< GX:3072< GX:2048< OG GX:3584< OR Y4:0< Y4:1< Ys U Y4:2< Y4:3< SG AB:0< GE:0< GE:512< AB:512< DL AB:1024< GE:1024< AB:2560< GE:2048< AB:2048< AB:3072< AB:3584< CS GK NE TB:256 LN:0< sf:160 E1*<TB sf:96 TB:0< E1*<E1 LW sf:112 E2*<TB RS EV E2*<E2 LN:256"}
+
+
+ORDER = {"v": "GL:1024< GL:3072< XO:0<ZE SX Ns*<SX Rp:0< XO:0<Ns Rq:0< XR:0<ZE Rp:128 Rq:128 MX:1024< MN:1024< MX:0< MN:0< XR:0<Nr MX:2048< MN:3072< MX:3072< MN:3584< MX:3584< MN:2048< Lu YS si:0< si:16< sf:0< qs XR:0<Ys D:0< D:512< D:1024< D:2560< D:2048< D:3072< D:3584< GE:2560< GE:3072< GE:3584< KY KS si:32 su:32 SB:256 SB:0 E2 E1 su:48 MM sf:208<B4 sf:208<sf PT pl Ns*<sf PF:0<PT Ru sf:192 ws XO:0<Yr", "a": "GL:0< GL:2048< FR:0< Lo:0< GL:3584< SU:0< N2:0< FR:128 Lo:128 SU:256 N2:128 GX:1024< GX:0< GX:2048< GX:3072< GX:3584< OG OR Y4:0< Y4:1< Ys sf:16<si Y4:2< U Y4:3< sf:48<si JG SG C2 AB:0< GE:0< DL GE:512< AB:512< GE:1024< AB:2560< AB:1024< AB:2048< GE:2048< AB:3072< AB:3584< CS GK NE LN:0< TB:0< sf:112 E2*<TB TB:256 sf:160 E2*<E2 sf:128 sf:96 LN:256 E1*<TB C1 E1*<E1 Ro LW EV", "v0": "OH QM GL:1024< GL:3072< PF:0<PI Rp:0< Rq:0< GX:0< MX:0< MN:0< Rp:128 Rq:128 PF:1536<PI MX:1024< MN:2048< MX:2048< MN:3584< MN:1024< MX:3584< MX:3072< MN:3072< Lu YS si:0< si:16< sf:0< qs XR:0<Ys D:512< D:0< D:1024< D:2560< D:2048< GE:2560< D:3072< D:3584< GE:3072< GE:3584< KY KS si:32 su:32 SB:256 SB:0 MM E2 E1 Ru su:48 PT sf:208<B4 pl sf:208<sf PF:0<PT sf:192 ws XO:0<Yr Ns*<sf", "a0": "TS GL:0< GL:2048< FR:0< SU:0< Lo:0< N2:0< FR:128 GX:512< SU:256 N2:128 Lo:128 GX:1024< GX:2048< GX:3584< GX:3072< OG OR Y4:0< Y4:1< sf:16<si Ys Y4:2< Y4:3< U JG sf:48<si SG C2 AB:512< GE:512< GE:0< AB:0< AB:1024< GE:1024< AB:2048< AB:2560< GE:2048< AB:3584< AB:3072< CS GK DL sf:128 NE LN:0< TB:0< sf:112 E2*<TB TB:256 sf:160 E2*<E2 Ro sf:96 LN:256 E1*<TB C1 E1*<E1 LW EV", "v3": "GL:1024< GL:3072< XO:0<ZE SX Ns*<SX Rp:0< XO:0<Ns Rq:0< XR:0<ZE Rp:128 MX:1024< Rq:128 MN:1024< MX:0< MN:0< MX:3072< XR:0<Nr MX:2048< MN:3072< MN:2048< MX:3584< MN:3584< Lu YS si:0< si:16< sf:0< qs XR:0<Ys D:0< D:512< D:1024< D:2560< D:2048< D:3072< GE:2560< D:3584< GE:3072< GE:3584< KY KS si:32 su:32 SB:0 MM SB:256 E1 XO:0<Yr su:48 sf:192 ws E2 sf:208<B4 sf:208<sf Ns*<sf", "a3": "GL:0< GL:3584< GL:2048< FR:0< Lo:0< SU:0< N2:0< FR:128 SU:256 Lo:128 N2:128 GX:1024< GX:0< GX:3072< GX:2048< GX:3584< OG OR Y4:0< Y4:1< Y4:2< Ys Y4:3< U SG AB:0< GE:0< GE:512< DL AB:512< GE:1024< AB:1024< AB:2560< GE:2048< AB:2048< AB:3584< AB:3072< CS GK NE TB:256 sf:160 sf:96 sf:112 E1*<TB E1*<E1 LW TB:0< E2*<TB RS E2*<E2 LN:0< LN:256 EV"}
+
+
+def _s1(lg, xg):
+    o = []
+    for e, lo, hi in lg:
+        o.append(("L", e, lo, hi))
+        if hi % 64 == 0:
+            o.append(("P", hi // 64 - 1))
+        if hi % 128 == 0:
+            o += [("F", hi // 128 - 1), ("S", hi // 128 - 1), ("R", hi // 128 - 1)]
+    return tuple(o + [("X", e, lo, hi) for e, lo, hi in xg])
+
+
+CFG.update(s1=_s1([("a", 0, 64), ("v", 64, 128), ("a", 128, 192), ("v", 192, 224), ("a", 224, 256)],
+                  [("a", 0, 64), ("a", 64, 128), ("a", 128, 192), ("a", 192, 224), ("a", 224, 256)]),
+           s1_0=_s1([("a", 0, 64), ("v", 64, 128), ("a", 128, 192), ("v", 192, 256)],
+                    [("v", 0, 32), ("a", 32, 64), ("a", 64, 128), ("a", 128, 192), ("a", 192, 224), ("a", 224, 256)]),
+           dq=(((0, 8), (8, 16)), ((0, 16),), ((0, 8), (8, 16)), ((0, 8), (8, 16))),
+           on_v=(), gev=((2, 8), (3, 0), (3, 8)), eqa1=tuple(range(10, 16)), eqa2=tuple(range(8, 16)), picks=(256, 0))
 
 
 def _s(n, d):
@@ -19,31 +60,31 @@ def _s(n, d):
 
 SCRATCH = {
     "XO": _s(WIN, BF), "XR": _s(WIN, BF), "PI": _s(W, I32), "PF": _s(WIN, F32),
-    "rds": _s(E, I32), "zs": _s(E, BF), "rdr": _s(E, I32),
+    "rds": _s(E, I32), "zs": _s(E, BF),
     "GL": _s(4096, F16), "GX": _s(4096, BF), "MX": _s(4096, BF), "MN": _s(4096, BF),
-    "YR": _s(4096, BF), "D": _s(4096, BF), "AB": _s([16, 256], BF), "GE": _s([16, 256], BF),
-    "E1": _s([16, 272], BF), "E2": _s([16, 272], BF), "EA": _s(E, BF),
-    "Ro": _s(E, F16), "Ru": _s(E, U16), "Lo": _s(E, F16), "Lu": _s(E, U16), "Rp": _s(E, F32), "Rq": _s(E, U16),
+    "D": _s(4096, F16), "AB": _s([64, 64], BF), "GE": _s([64, 64], BF), "KS": _s(E, I32), "YS": _s(E, F32), "Y4": _s(1024, F16),
+    "QM": _s(2048, BF), "X0": _s(512, BF),
+    "E1": _s([16, 272], BF), "E2": _s([16, 272], BF),
+    "Ro": _s(E, F16), "Ru": _s(E, U16), "Lo": _s(E, F16), "Lu": _s(E, U16),
+    "OD": _s(E, BF), "NE": _s(E, BF), "pl": _s(16, U16), "Rp": _s(E, F32), "Rq": _s(E, U16),
     "FR": _s(E, BF), "SU": _s(512, F32), "N2": _s(E, BF), "OG": _s(E, BF), "OR": _s(E, BF), "U": _s(E, BF),
-    "t1": _s(E, F32), "DL": _s(E, F32), "JG": _s(E, BF), "C1": _s(E, F32), "C2": _s(E, F32), "CS": _s(E, BF),
-    "GK": _s(E, F32), "KY": _s(E, F32), "KS": _s(E, I32), "SB": _s(768, F16), "TB": _s(512, F16), "DK": _s(E, BF),
-    "EV": _s(E, BF), "MM": _s(E, F32), "NL": _s(E, BF), "LW": _s(E, BF), "LN": _s(512, BF), "SG": _s(E, BF),
+    "DL": _s(E, F32), "JG": _s(E, BF), "C1": _s(E, F32), "C2": _s(E, F32), "CS": _s([16, 16], BF),
+    "GK": _s([16, 16], F32), "KY": _s(E, F32), "SB": _s(512, F16), "TB": _s(2 * E, F16),
+    "EV": _s(E, BF), "MM": _s(E, F32), "LW": _s(E, BF), "LN": _s(2 * E, BF), "SG": _s(512, BF),
     "PT": _s(E, F32), "SX": _s(E, F32), "RS": _s(E, F32), "rr": _s(E, F32), "zr": _s(E, BF),
     "sf": _s(256, F32), "si": _s(128, I32), "su": _s(128, U16),
-    "Ys": _s([RO, E], BF), "Yr": _s([RO, E], BF), "Ns": _s([RO, E], I32), "Nr": _s([RO, E], I32),
-    "qs": _s(RO * 16, U16), "qr": _s(RO * 16, U16), "ws": _s(RO * 16, U16), "wr": _s(RO * 16, U16),
-    "xs": _s(RO * 32, U16), "xr": _s(RO * 16, U16),
-    "COL": _s(E, F32), "CM": _s(272, F32), "IO": _s(512, F32), "pi": _s(16, I32), "pc": _s(16, F32),
-    "MK": _s(48, F32), "REL": _s(128, BF), "OH": _s(2048, BF), "DG": _s(2048, BF), "S0": _s(2048, BF),
-    "MB": _s(128 * 14, BF), "MF": _s(128 * 4, F32), "RS0": _s(1024, BF), "RS1": _s(1024, BF),
-    "KC": _s(E, BF), "C21": _s(E, BF), "NH": _s(E, BF), "ZE": _s(512, BF), "ZC": _s(E, BF), "TH": _s(E, BF),
-    "CT": _s(3 * E, F32), "TT": _s(9 * 64, F32), "TS": _s(1024, F32), "J": _s(128, BF), "cT": _s(80, F32),
-    "C16": _s(64, BF),
+    "Ys": _s([RO, E], BF), "Yr": _s([RO, E], BF), "Ns": _s([RO, 288], U16), "Nr": _s([RO, 272], U16),
+    "qs": _s(RO * 32, U16), "qr": _s(RO * 16, U16), "ws": _s(RO * 16, U16), "wr": _s(RO * 16, U16),
+    "COL": _s(E, F32), "XK": _s(272, BF), "IO": _s(E, F32), "IK": _s(E, BF), "pi": _s(16, I32), "pc": _s(16, F32),
+    "MK": _s(80, F32), "AD": _s(272, BF), "OH": _s([16, 128], BF), "DG": _s(2048, BF),
+    "MB": _s(128 * 18, BF), "MF": _s(128 * 4, F32), "RS0": _s(1024, BF), "RS1": _s(1024, BF),
+    "KC": _s(E, BF), "C21": _s(E, BF), "C16": _s([16, 16], BF), "ZE": _s(512, BF), "ZC": _s(E, BF), "TH": _s(E, BF),
+    "CT": _s(E, F32), "TT": _s(5 * 64, F32), "TS": _s(1024, F32), "J": _s(16, BF), "cT": _s(80, F32),
 }
 for _b in range(8):
-    SCRATCH["B%d" % _b] = ("psum", [128, 512], F32)
+    SCRATCH["B%d" % _b] = ("psum", [128, 32, 16] if _b in (5, 6) else [128, 512], F32)
 MSG = ["y", "w", "n"]
-SEMAPHORES = (["v", "a", "p", "c", "sent", "left", "r_rd", "r_z", "r_x", "r_ro", "r_zo"]
+SEMAPHORES = (["v", "a", "p", "c", "sent", "left", "gone", "r_rd", "r_z", "r_x", "r_ro", "r_zo"]
               + ["r_%s%d" % (m, t) for m in MSG for t in range(RO)] + ["d%d" % k for k in range(16)])
 
 
@@ -55,17 +96,32 @@ def rank_program(g, core, T, topo):
     nxt, prv = T.cores[(rank + 1) % N], T.cores[(rank - 1) % N]
     Q = {"v": g.vector, "a": g.scalar, "p": g.tensor, "c": g, "s": g.sync}
     ops = []
-    ndma = [0]
-    out_cnt = {"sent": 0, "left": 0}
+    ndma, queued = [0], [0]
+    line = [None]
+    now = [-1]
+    later = [0]
+    out_cnt = {"sent": 0, "left": 0, "gone": 0}
+    S = slice
+    ALL = slice(None)
+
+    def v(name, *ix):
+        shape = SCRATCH[name][1][1:]
+        bits = np.zeros(shape, np.uint8)
+        bits[ix] = 1
+        mask = int.from_bytes(np.packbits(bits.reshape(-1), bitorder="little").tobytes(), "little")
+        return (T[name][(ALL,) + ix], [(name, mask)])
 
     def a(name, lo=0, hi=None, step=1):
-        hi = SCRATCH[name][1][1] if hi is None else hi
-        return (T[name][:, lo:hi:step] if step > 1 else T[name][:, lo:hi], [(name, lo, hi, step)])
+        shape = SCRATCH[name][1]
+        if len(shape) > 2:
+            n = shape[2]
+            hi = shape[1] * n if hi is None else hi
+            return v(name, S(lo // n, hi // n), ALL)
+        hi = shape[1] if hi is None else hi
+        return v(name, S(lo, hi, step) if step > 1 else S(lo, hi))
 
     def a3(name, r0, r1, lo, hi):
-        n = SCRATCH[name][1][2]
-        ap = T[name][:, r0, lo:hi] if r1 == r0 + 1 else T[name][:, r0:r1, lo:hi]
-        return (ap, [(name, r0 * n + lo, (r1 - 1) * n + hi, 1)])
+        return v(name, r0 if r1 == r0 + 1 else S(r0, r1), S(lo, hi))
 
     def ind(win, off):
         return (win[0].indirect(off[0]), win[1], off[1])
@@ -82,30 +138,66 @@ def rank_program(g, core, T, topo):
         for i in ins:
             if isinstance(i, tuple):
                 rd += i[1] + (i[2] if len(i) > 2 else [])
-        d = {"eng": eng, "fn": fn, "wr": wr, "rd": rd}
+        d = {"eng": eng, "fn": fn, "wr": wr, "rd": rd, "lat": SEM, "line": line[0] and (line[0], eng), "rank": len(ops) + later[0]}
         d.update(kw)
+        if wr and rd:
+            d["name"] = (now[0], eng, "%s:%d<%s" % (wr[0][0], (wr[0][1] & -wr[0][1]).bit_length() - 1,
+                                                   [i for i in ins if isinstance(i, tuple)][0][1][0][0]))
+        if "cost" not in d:
+            d["cost"] = cost(eng, outs[0], [i for i in ins if isinstance(i, tuple)], kw.get("per", 1.0))
         ops.append(d)
 
+    def width(x):
+        return 16 * x[2][0][1].bit_count() if len(x) > 2 else x[1][0][1].bit_count()
+
+    def cost(eng, out, ins, per):
+        n = width(out)
+        kinds = [SCRATCH[x[1][0][0]] for x in [out] + ins if width(x) == n]
+        if eng == "p":
+            return PCALL + max(64, n) * PE * (4 if SCRATCH[ins[0][1][0][0]][2] == F32 else 1)
+        if eng == "c":
+            return 170 + 2 * n * CYC
+        if len(out) > 2:
+            return 55 + n * SCATTER * CYC
+        if any(len(x) > 2 for x in ins):
+            return 55 + n * GATHER * CYC
+        if per == 0.5 and any(k[2] in (F32, I32) for k in kinds):
+            per = 1.0
+        if per == 2.0 and any(k[0] == "psum" for k in kinds):
+            per = 1.0
+        return CALL[eng] + max(64, n * per) * CYC
+
     def cp(out, in_):
-        op("v", lambda: g.vector.tensor_copy(out[0], in_[0]), [out], [in_])
+        op("v", lambda: g.vector.tensor_copy(out[0], in_[0]), [out], [in_], per=0.5)
 
     def tt(out, x, y, o):
-        op("v", lambda: g.vector.tensor_tensor(out[0], x[0], y[0], o), [out], [x, y])
+        op("v", lambda: g.vector.tensor_tensor(out[0], x[0], y[0], o), [out], [x, y], per=2.0)
 
     def ts(out, x, s1, o0, s2=None, o1=None):
         if o1 is None:
-            op("v", lambda: g.vector.tensor_scalar(out[0], x[0], val(s1), None, o0), [out], [x, s1])
+            op("v", lambda: g.vector.tensor_scalar(out[0], x[0], val(s1), None, o0), [out], [x, s1], per=0.5)
         else:
-            op("v", lambda: g.vector.tensor_scalar(out[0], x[0], val(s1), val(s2), o0, o1), [out], [x, s1, s2])
+            op("v", lambda: g.vector.tensor_scalar(out[0], x[0], val(s1), val(s2), o0, o1), [out], [x, s1, s2], per=0.5)
 
     def scan(out, d0, d1, o0, o1):
-        op("v", lambda: g.vector.tensor_tensor_scan(out[0], d0[0], d1[0], 0.0, o0, o1), [out], [d0, d1])
+        op("v", lambda: g.vector.tensor_tensor_scan(out[0], d0[0], d1[0], 0.0, o0, o1), [out], [d0, d1], per=0.5)
+
+    def turn(out, in_):
+        op("v", lambda: g.vector.transpose(out[0], in_[0]), [out], [in_], per=0.5)
 
     def ms(out, c):
-        op("v", lambda: g.vector.memset(out[0], c), [out], [])
+        op("v", lambda: g.vector.memset(out[0], c), [out], [], per=0.5)
 
     def act(out, x, f=AF.Identity, bias=0.0, scale=1.0):
         op("a", lambda: g.scalar.activation(out[0], x[0], f, bias=val(bias), scale=val(scale)), [out], [x, bias, scale])
+
+    def take(name, out, x, bias=0.0, relu=False):
+        if name not in CFG["on_v"]:
+            act(out, x, AF.Relu if relu else AF.Identity, bias=bias)
+        elif relu:
+            ts(out, x, bias, Op.add, 0.0, Op.max)
+        else:
+            ts(out, x, bias, Op.add)
 
     def mm(out, l, r, st, sp):
         op("p", lambda: g.tensor.matmul(out[0], l[0], r[0], st, sp), [out], [l, r])
@@ -121,150 +213,169 @@ def rank_program(g, core, T, topo):
     def gcopy(out, in_, n):
         op("c", lambda: g.affine_select(out[0], in_[0], [[0, n]], Op.is_gt, 0.0, 1, 0), [out], [in_])
 
+    def nbytes(x, y):
+        name, mask = (x[1] or y[1])[0]
+        return 128 * mask.bit_count() * (4 if SCRATCH[name][2] in (F32, I32) else 2)
+
     def dma(eng, out, in_):
         s = "d%d" % ndma[0]
         ndma[0] += 1
-        op(eng, lambda: Q[eng].dma_start(out[0], in_[0]), [out], [in_], sem=s, val=16)
+        op(eng, lambda: Q[eng].dma_start(out[0], in_[0]), [out], [in_], sem=s, val=16, cost=60, dma=nbytes(out, in_))
 
     def send(dst, out, in_, sem):
         rid, pid, _ = topo.addr(dst)
-        loc = "left" if sem == "r_x" else "sent"
+        loc = "left" if sem == "r_x" else "gone" if sem == "r_rd" else "sent"
         out_cnt[loc] += len(topo.engines(core, dst))
         op("c", lambda: g.remote_dma(out[0], in_[0], T.sem[sem], T.sem[loc], pid, rid, topo.mask(core, dst)), [], [in_],
-           remote=loc, val=out_cnt[loc])
+           remote=loc, cost=ISSUE + (FIRST if sum(out_cnt.values()) == len(topo.engines(core, dst)) else 0), msg=sem,
+           lat=FLIGHT + (nbytes(in_, in_) + (queued[0] if now[0] < 0 else 0)) / LINK)
+        queued[0] += nbytes(in_, in_) * 0.8
 
     def recv(src, bufs, sem):
-        op("x", None, bufs, [], sem=sem, val=len(bufs) * len(topo.engines(src, core)))
+        op("x", None, bufs, [], sem=sem, val=len(bufs) * len(topo.engines(src, core)), cost=0, lat=0)
 
-    def gather(eng, out, win, off):
+    def gather(eng, out, win, off, bias=None):
         if eng == "a":
-            act(out, ind(win, off))
-        else:
+            act(out, ind(win, off), bias=bias or 0.0)
+        elif bias is None:
             cp(out, ind(win, off))
+        else:
+            ts(out, ind(win, off), bias, Op.add)
 
     def hbm(name, lo=None, hi=None):
         return (T[name][:] if lo is None else T[name][:, lo:hi], [])
 
     def m(buf, k):
-        return a(buf, 128 * k, 128 * k + 128)
-    ID, BLK, W1, IB, NIB, NBLK, HID, WD, B2, I1536, I255, NID, I12, TMP = [m("MB", k) for k in range(14)]
-    IDf, NIDf, BLKf, TMPf = [m("MF", k) for k in range(4)]
-    pp, pm, gb, cz, p2 = [a("pc", k, k + 1) for k in range(5)]
-    iT, b12, b16, dum2 = a("cT", 0, 16), a("cT", 16, 32), a("cT", 32, 48), a("cT", 48, 80)
-    KK, COM, SET, TOH, TOC, TOL, TNC, TNL, TOS = [a("TT", 64 * k, 64 * k + 64) for k in range(9)]
+        return v(buf, k, ALL) if buf == "OH" else a(buf, 128 * k, 128 * k + 128)
+    ID, BLK, NTRI, IB, NIB, NBLK, HID, WD, B2, I1536, I255, NID, I12, P1536, BC0, I1024 = [m("MB", k) for k in range(16)]
+    IDf, BLKf, TMPf = [m("MF", k) for k in range(3)]
+    pp, pm, pm4, gb, nb, pq, n4, npm = [a("pc", k, k + 1) for k in range(8)]
+    cz, half, p2, lo8 = [a("pc", k, k + 1) for k in range(11, 15)]
+    iT, b12, dum2 = a("cT", 0, 16), a("cT", 16, 32), a("cT", 48, 80)
+    TOH, TOC, TOS, COM, TNL = [a("TT", 64 * k, 64 * k + 64) for k in range(5)]
     qf, oT, dq, kq, om, nl, tT, lm = (a("sf", 0, 16), a("sf", 16, 32), a("sf", 32, 48), a("sf", 48, 64), a("sf", 64, 80),
-                                      a("sf", 80, 96), a("sf", 96, 128), a("sf", 128, 160))
-    wT, ef, lw, ntT = a("sf", 160, 176), a("sf", 176, 192), a("sf", 192, 208), a("sf", 208, 240)
+                                      a("sf", 80, 96), a("sf", 96, 128), a("sf", 128, 144))
+    lx, dum = a("sf", 144, 160), a("cT", 48, 64)
+    wT, ef, lw = a("sf", 160, 176), a("sf", 176, 192), a("sf", 192, 208)
     yi, y7, cd, kk, c33 = [a("si", 16 * k, 16 * k + 16) for k in range(5)]
-    q0, jl, cu, el, c1l = [a("su", 16 * k, 16 * k + 16) for k in range(5)]
+    q0, jl, cu, el, cl, c1l = [a("su", 16 * k, 16 * k + 16) for k in range(6)]
     XO, XR, PF = a("XO"), a("XR"), a("PF")
+    Lo = a("Lo")
     H = W // 2
 
-    dma("s", a("rds"), hbm("rd"))
+    cuts = CFG["cuts"]
+    pieces = list(zip(cuts, cuts[1:]))
+    dma("a", a("rds"), hbm("rd"))
+    dma("s", a("XO", *pieces[0]), hbm("x0", *pieces[0]))
     dma("a", a("zs"), hbm("z0"))
-    dma("s", a("XO", 0, H), hbm("x0", 0, H))
+    for lo, hi in pieces[1:len(pieces) - CFG["late"]]:
+        dma("s", a("XO", lo, hi), hbm("x0", lo, hi))
     for k in range(4):
-        dma("a" if k < 2 else "s", a("PI", 768 * k, 768 * k + 768), hbm("lk", 768 * k, 768 * k + 768))
-    dma("s", a("XO", H, W), hbm("x0", H, W))
+        dma("as"[k % 2], a("PI", 768 * k, 768 * k + 768), hbm("lk", 768 * k, 768 * k + 768))
+    for lo, hi in pieces[len(pieces) - CFG["late"]:]:
+        dma("s", a("XO", lo, hi), hbm("x0", lo, hi))
     iota(a("pi", 0, 1), [[0, 1]], 0, 1, False)
     iota(a("COL"), [[1, 256]])
-    iota(KK, [[0, 2], [-1, 16], [0, 2]], 15)
+    iota(a("X0"), [[-4, 4], [1, 128]])
+    cp(a("Rq"), a("rds"))
+    for n, (lo, hi) in enumerate(pieces):
+        if n == CFG["rz"][0]:
+            send(nxt, a("Ru"), a("Rq"), "r_rd")
+        if n == CFG["rz"][1]:
+            send(nxt, a("XO", W, W + E), a("zs"), "r_z")
+        send(prv, a("XR", lo, hi), a("XO", lo, hi), "r_x")
+    iota(a("XK"), [[0, 17], [1, 16]])
+    iota(a("IO", 0, 64), [[0, 2], [-1, 16], [0, 2]], 15)
+    iota(a("IO", 64, 128), [[0, 2], [-1, 16], [-100, 2]], 115)
+    iota(a("IO", 128, 192), [[-100, 2], [-1, 16], [0, 2]], 115)
+    iota(a("IO", 192, 256), [[-1, 2], [0, 16], [1, 2]], 1)
     iota(COM, [[0, 32], [1, 2]])
-    iota(SET, [[1, 2], [0, 32]])
-    send(nxt, a("rdr"), a("rds"), "r_rd")
-    send(nxt, a("XO", W, W + E), a("zs"), "r_z")
-    iota(a("IO", 0, 256), [[0, 16], [-2, 16]], 62)
-    send(prv, a("XR", 0, H), a("XO", 0, H), "r_x")
-    iota(a("IO", 256, 384), [[0, 16], [1, 8]])
-    iota(a("IO", 384, 512), [[1, 16], [0, 8]])
-    iota(a("CM"), [[0, 17], [1, 16]])
-    send(prv, a("XR", H, W), a("XO", H, W), "r_x")
-    recv(prv, [a("rdr")], "r_rd")
+    iota(a("IK"), [[0, 16], [-2, 16]], 62)
+    iota(a("CT"), [[-12, 256]], W)
+    iota(a("J"), [[1, 16]])
+    iota(a("pi", 8, 11), [[1, 3]], 0, 1, False)
+    recv(prv, [a("Ru")], "r_rd")
     recv(prv, [a("XO", W, W + E)], "r_z")
-    recv(nxt, [a("XR", 0, H), a("XR", H, W)], "r_x")
+    recv(nxt, [a("XR", lo, hi) for lo, hi in pieces], "r_x")
 
-    ms(a("RS0"), 1.0)
     ms(a("ZE"), 0.0)
-    cp(pp, a("pi", 0, 1))
-    ts(a("pi", 4, 5), a("pi", 0, 1), 15, Op.bitwise_and)
-    ms(a("RS1"), 0.0)
-    cp(pm, a("pi", 4, 5))
+    ts(a("pi", 1, 2), a("pi", 0, 1), 15, Op.bitwise_and)
+    ts(a("pi", 2, 3), a("pi", 0, 1), 2, Op.logical_shift_right, 3, Op.bitwise_and)
+    cp(a("pc", 0, 3), a("pi", 0, 3))
     c128 = a("COL", 0, 128)
     ts(ID, c128, pp, Op.is_equal)
-    tt(gb, pp, pm, Op.subtract)
     ts(a("MK", 0, 16), a("COL", 0, 16), pm, Op.is_equal)
-    ts(a("REL"), c128, gb, Op.subtract)
-    ts(IDf, c128, pp, Op.is_equal)
-    act(TMPf, a("REL"), AF.Abs, bias=-7.5)
+    act(gb, pm, scale=-1.0, bias=pp)
+    act(nb, gb, scale=-1.0, bias=-7.5)
+    act(TMPf, c128, AF.Abs, bias=nb)
+    ts(BLK, TMPf, 8.0, Op.is_lt)
     for k in range(16):
         act(m("DG", k), ID, scale=a("MK", k, k + 1))
-    ms(a("RS0", 0, 1024, 16), 0.0)
-    ms(a("RS1", 0, 1024, 16), 512.0)
-    ts(BLK, TMPf, 8.0, Op.is_lt)
-    ts(BLKf, TMPf, 8.0, Op.is_lt)
-    ts(TMP, c128, pp, Op.is_gt, -4096.0, Op.mult)
-    ts(IB, ID, 4096.0, Op.mult)
-    tt(TMP, TMP, BLK, Op.mult)
-    ts(cz, a("MK", 1, 2), 3073.0, Op.mult, -1.0, Op.add)
-    tt(W1, TMP, IB, Op.add)
-    tt(cz, cz, a("MK", 0, 1), Op.add)
-    for k in range(16):
-        ts(m("OH", k), a("REL"), float(k), Op.is_equal)
-    ts(a("ZC"), a("COL"), a("MK", 0, 1), Op.mult, cz, Op.add)
+    act(IDf, ID)
+    act(BLKf, BLK)
+    for mat, src, c in ((IB, ID, 4096.0), (NIB, ID, -4096.0), (NBLK, BLK, -4096.0), (HID, ID, 0.5), (I1536, ID, -1536.0),
+                        (P1536, ID, 1536.0), (I1024, ID, 1024.0), (I255, ID, 255.0), (NID, ID, -1.0), (I12, ID, 12.0),
+                        (B2, BLK, 2 * LOSE)):
+        act(mat, src, scale=c)
+    op("c", lambda: g.affine_select(NTRI[0], NBLK[0], [[1, 128]], Op.is_gt, 0.0, 0, -1), [NTRI], [NBLK])
+    act(cz, a("MK", 1, 2), scale=float(W))
+    act(a("ZC"), a("COL"), scale=a("MK", 0, 1), bias=cz)
+    act(pq, pm4, scale=-4.0, bias=pp)
+    act(n4, pm4, scale=-1.0)
+    act(a("MK", 48, 52), a("COL", 0, 4), bias=gb)
+    act(a("MK", 56, 60), a("COL", 0, 4), AF.Abs, bias=n4)
+    act(a("MK", 52, 56), a("MK", 56, 60), scale=-1000.0, bias=pq)
+    now[0] = 0
+    for k in range(4):
+        ts(a("QM", 512 * k, 512 * k + 512), a("X0"), a("MK", 52 + k, 53 + k), Op.is_equal)
+    for k in range(4):
+        ts(v("OH", S(k, 16, 4), ALL), a("X0"), a("MK", 48 + k, 49 + k), Op.is_equal)
+    now[0] = -1
     ms(a("PF", W, WIN), 0.0)
     ms(a("XO", DUMP, WIN), 0.0)
-    ms(a("XR", W, WIN), 0.0)
-    ms(a("NH"), -0.5)
-    ts(a("XR", W, W + 1), pm, 8.0, Op.is_lt, 513.0, Op.mult)
-    ts(iT, a("COL", 0, 16), 16.0, Op.mult, pm, Op.add)
-    ts(a("XR", W, W + 1), a("XR", W, W + 1), -1.0, Op.add)
-    for mat, src, c in ((NIB, ID, -4096.0), (NBLK, BLK, -4096.0), (HID, ID, 0.5), (I1536, ID, -1536.0),
-                        (I255, ID, 255.0), (NID, ID, -1.0), (I12, ID, 12.0), (B2, BLK, 2.0)):
-        act(mat, src, scale=c)
-    act(a("PF", 0, 768), a("PI", 0, 768), bias=-OFF)
-    act(a("S0"), a("OH"), scale=a("MK", 0, 1))
-    ts(a("PF", 768, 1536), a("PI", 768, 1536), -OFF, Op.add)
+    ms(a("XR", W + 16, WIN), 0.0)
+    act(lo8, pm, AF.Sign, scale=-1.0, bias=7.5)
+    act(lo8, lo8, scale=256.5, bias=255.5)
+    act(a("XR", W, W + 16), a("ZE", 0, 16), bias=lo8)
+    ms(a("RS0"), 1.0)
+    ms(a("RS1"), 0.0)
+    ms(a("RS0", 0, 1024, 16), 0.0)
+    ms(a("RS1", 0, 1024, 16), 512.0)
+    act(iT, a("COL", 0, 16), scale=16.0, bias=pm)
     act(b12, iT, scale=12.0)
-    act(b16, iT, scale=16.0, bias=15.0)
     act(a("cT", 48, 64), iT, bias=DUMP - OFF)
     act(a("cT", 64, 80), iT, bias=DUMP - OFF)
-    act(qf, iT, scale=12.0)
-    ts(q0, iT, 12.0, Op.mult)
-    cp(a("Ru"), a("rdr"))
-    ts(a("Ro"), a("rdr"), -OFF, Op.add)
-    act(a("PF", 1536, 2304), a("PI", 1536, 2304), bias=-OFF)
-    ms(a("C21"), 2 * BIG)
-    ms(a("C16"), 16.0)
-    ts(a("KC"), a("IO", 0, 256), 0.5, Op.add)
-    ts(a("PF", 2304, 2688), a("PI", 2304, 2688), -OFF, Op.add)
-    act(a("PF", 2688, W), a("PI", 2688, W), bias=-OFF)
-
-    def tables():
-        ts(a("SG"), a("RS0", 0, 256), 0.5, Op.mult)
-        ts(a("LW"), a("RS1", 0, 256), -1.0 / 256, Op.mult)
-        ts(TOH, KK, pm, Op.is_equal)
-        scan(a("TH"), a("SG"), a("LW"), Op.mult, Op.add)
-        tt(TOC, TOH, COM, Op.mult)
-        tt(TOS, TOH, SET, Op.mult)
-        tt(a("MK", 16, 32), a("TH", 0, 16), a("MK", 0, 16), Op.mult)
-        ts(a("MK", 32, 48), a("MK", 0, 16), -0.5, Op.add)
-        op("v", lambda: g.vector.tensor_reduce(p2[0], T.MK[:, 16:32], AX.X, Op.add), [p2], [a("MK", 16, 32)])
-        tt(TOL, TOS, TOC, Op.subtract)
-        tt(TNL, COM, SET, Op.subtract)
-        ts(WD, BLK, p2, Op.mult, -0.5, Op.mult)
-        ts(TNC, COM, -4352.0, Op.mult, 4096.0, Op.add)
-        ts(TNL, TNL, 4.0, Op.mult, 4.0, Op.add)
-        ts(a("IO", 384, 512), a("IO", 384, 512), pm, Op.is_equal)
-        ts(a("pi", 8, 12), a("COL", 0, 4), pm, Op.add)
-        tt(a("J"), a("IO", 384, 512), a("IO", 256, 384), Op.mult)
-        ts(a("pi", 12, 16), a("pi", 8, 12), 15, Op.bitwise_and)
-        ts(a("PT"), a("COL"), 12.0, Op.mult, -3072.0, Op.add)
-        ts(a("pc", 5, 8), a("pi", 12, 15), 8.0, Op.mult)
-        ts(a("pc", 8, 11), a("pi", 12, 15), 64.0, Op.mult)
-
-    def lock_rows(t):
-        ts(a("CT", E * t, E * t + E), a("CM", t, t + E), pm, Op.is_equal)
-        tt(a("CT", E * t, E * t + E), a("CT", E * t, E * t + E), a("PT"), Op.mult)
+    act(kq, a("ZE", 0, 16), bias=512.0)
+    act(half, a("MK", 0, 1), scale=0.5)
+    act(BC0, BLK, scale=half)
+    act(npm, pm, scale=-8192.0)
+    act(a("AD"), a("XK", 0, 272), AF.Abs, scale=8192.0, bias=npm)
+    act(a("OD"), a("AD", 0, E), scale=-1.0, bias=-0.25)
+    cp(q0, b12)
+    act(a("C21"), a("ZE", 0, E), bias=2 * BIG)
+    act(a("C16"), a("ZE", 0, E), bias=16.0)
+    for c in range(4):
+        for lo, hi in CFG["dq"][c]:
+            if (c, lo) in CFG["gev"]:
+                act(v("C16", S(lo, hi), S(4 * c, 4 * c + 4)), a("ZE", 0, 4 * (hi - lo)))
+    act(a("KC"), a("IK"), bias=0.5)
+    act(a("SG", 0, 256), a("RS0", 0, 256), scale=0.5)
+    act(a("LW"), a("RS1", 0, 256), scale=-LOSE / 256)
+    scan(a("TH"), a("SG", 0, 256), a("LW"), Op.mult, Op.add)
+    ts(a("TT", 0, 192), a("IO", 0, 192), pm, Op.is_equal)
+    act(TNL, a("IO", 192, 256), AF.Sign)
+    tt(a("MK", 16, 32), a("TH", 0, 16), a("MK", 0, 16), Op.mult)
+    op("a", lambda: g.scalar.activation(T.MK[:, 64:80], T.MK[:, 16:32], AF.Identity, scale=-0.5, accum_out=p2[0]),
+       [a("MK", 64, 80), p2], [a("MK", 16, 32)])
+    act(WD, BLK, scale=p2)
+    act(a("MK", 32, 48), a("MK", 0, 16), bias=-0.5)
+    ts(a("pi", 12, 15), a("pi", 8, 11), 15, Op.bitwise_and)
+    act(a("pc", 8, 11), a("pi", 12, 15), scale=64.0, bias=-OFF)
+    now[0] = 0
+    for k in range(16):
+        act(a("TS", 64 * k, 64 * k + 64), TOS, AF.Sign, bias=a("MK", 32 + k, 33 + k))
+    now[0] = -1
+    ts(a("Ro"), a("Ru"), -OFF, Op.add)
 
     def to_list(out, mats, src, n, st=True, sp=True):
         mms(out, [(m(mats, k), a(src[0], src[1] + k, src[1] + n, 16)) for k in range(16)], st, sp)
@@ -272,268 +383,266 @@ def rank_program(g, core, T, topo):
     def own_update(t):
         recv(prv, [a("wr", 16 * t, 16 * t + 16)], "r_w%d" % t)
         cp(ind(XO, a("wr", 16 * t, 16 * t + 16)), a("ZE", 0, E))
-        xl = a("xs", 32 * t + 16, 32 * t + 32)
+        xl = a3("Ns", t, t + 1, 256, 272)
         tt(a("SX"), ind(XO, xl), a("EV"), Op.add)
         nw = a3("Ns", t, t + 1, 0, E)
         ts(nw, a("SX"), 0.5, Op.mult, -0.25, Op.add)
         if t < RO - 1:
-            send(prv, a3("Nr", t, t + 1, 0, E), nw, "r_n%d" % t)
-            send(prv, a("xr", 16 * t, 16 * t + 16), xl, "r_n%d" % t)
+            send(prv, a3("Nr", t, t + 1, 0, 272), a3("Ns", t, t + 1, 0, 272), "r_n%d" % t)
         cp(ind(XO, xl), nw)
 
-    def pairs_a(Eb, src0, col):
+    def pairs(Eb, src, col, bank, blocks):
+        line[0] = CFG["pairline"] or Eb
         for f in range(2):
-            for b in CFG["eqa"]:
+            for b in blocks:
                 e = a3(Eb, b, b + 1, 0, 256 - 16 * b)
                 if f == 0:
-                    act(e, a("TB", src0 + 16 * b, src0 + 256), AF.Abs, bias=a("sf", col + b, col + b + 1), scale=-1.0)
+                    act(e, src(16 * b), AF.Abs, bias=a("sf", col + b, col + b + 1), scale=-1.0)
                 else:
                     act(e, e, AF.Relu, bias=1.0, scale=-1.0)
-
-    def pairs(Eb, src0, col, out, extra):
-        bank, lo, hi = out[1][0][:3]
-        mms(out, [(ID, a("TH"))] + extra, True, False)
+        mms(a(bank, 0, 256), [(ID, a("TH"))], True, False)
         for b in range(16):
-            if b not in CFG["eqa"]:
-                ts(a3(Eb, b, b + 1, 0, 256 - 16 * b), a("TB", src0 + 16 * b, src0 + 256), a("sf", col + b, col + b + 1), Op.is_equal)
+            if b not in blocks:
+                ts(a3(Eb, b, b + 1, 0, 256 - 16 * b), src(16 * b), a("sf", col + b, col + b + 1), Op.is_equal)
             if b < 15:
-                mm(a(bank, lo + 16 * b + 16, hi), B2, a3(Eb, b, b + 1, 16, 256 - 16 * b), False, False)
-        mm(out, WD, a3(Eb, 0, 16, 0, 16), False, True)
+                mm(a(bank, 16 * b + 16, 256), B2, a3(Eb, b, b + 1, 16, 256 - 16 * b), False, False)
+        mm(a(bank, 0, 256), WD, a3(Eb, 0, 16, 0, 16), False, True)
+        line[0] = None
 
     for t in range(RO):
         last = t == RO - 1
+        now[0] = t
         Y = a3("Ys", t, t + 1, 0, E)
-        mms(a("B0", 0, 256), [(ID, a("ZE", 0, E))], True, False)
-        mms(a("B1"), [(ID, a("ZE"))], True, False)
-        mms(a("B1", 0, 256), [(ID, a("Ro"))], False, False)
-        mms(a("B1", 256, 512), [(ID, a("Ro"))], False, False)
-        mms(a("B2", 0, 256), [(ID, a("ZC"))], True, False)
-        for eng, lo, hi in CFG["lg"]:
-            gather(eng, a("GL", 16 * lo, 16 * hi), PF, a("Ru", lo, hi))
-        for c in (0, 3, 1, 2):
-            mms(a("B0", 64 * c, 64 * c + 64), [(m("DG", k), a("GL", 1024 * c + k, 1024 * c + 1024, 16)) for k in range(16)],
-                False, c == 2)
-        if t == 0:
-            tables()
-        else:
-            act(a("EV"), a("B6", 256, 512))
+        locks = a("PI") if t == 0 else PF
+
+        def lk_open(h):
+            bs = "B%d" % (2 * h + 1)
+            mms(a(bs, 0, 384), [(ID, a("ZE", 0, 384))], True, False)
+            mms(a(bs, 0, 128), [(ID, a("Ro", 128 * h, 128 * h + 128))], False, False)
+            mms(a(bs, 128, 256), [(ID, a("Ro", 128 * h, 128 * h + 128))], False, False)
+            mms(a(bs, 256, 384), [(ID, a("ZC", 128 * h, 128 * h + 128))], False, False)
+
+        def lk_gather(eng, lo, hi):
+            line[0] = "gathers"
+            gather(eng, a("GL", 16 * lo, 16 * hi), locks, a("Ru", lo, hi), -OFF)
+            line[0] = None
+
+        def lk_pick(c):
+            if CFG["pk"] == 64:
+                mms(a("B%d" % (c // 2 * 2), 64 * (c % 2), 64 * (c % 2) + 64),
+                    [(m("DG", k), a("GL", 1024 * c + k, 1024 * c + 1024, 16)) for k in range(16)])
+            elif c % 2:
+                mms(a("B%d" % (c - 1), 0, 128), [(m("DG", k), a("GL", 1024 * c - 1024 + k, 1024 * c + 1024, 16)) for k in range(16)])
+
+        def lk_free(h):
+            bl, bs, fr = "B%d" % (2 * h), "B%d" % (2 * h + 1), a("FR", 128 * h, 128 * h + 128)
+            line[0] = CFG["s1line"]
+            take("FR%d" % h, fr, a(bl, 0, 128), -1535.0, True)
+            line[0] = None
+            mms(a(bs, 0, 128), [(IB, fr), (NTRI, fr)], False, False)
+            mms(a(bs, 128, 256), [(IB, fr)], False, False)
+            mms(a(bs, 256, 384), [(NBLK, fr)], False)
+            take("Lo%d" % h, a("Lo", 128 * h, 128 * h + 128), a(bl, 0, 128))
+
+        def lk_first(h):
+            bl, bs, fr = "B%d" % (2 * h), "B%d" % (2 * h + 1), a("FR", 128 * h, 128 * h + 128)
+            line[0] = CFG["s1line"]
+            take("SU%d" % h, a("SU", 256 * h, 256 * h + 256), a(bs, 0, 256), OFF - 4096.0, True)
+            take("N2%d" % h, a("N2", 128 * h, 128 * h + 128), a(bs, 256, 384), 0.0, True)
+            line[0] = None
+            mms(a(bl, 128, 256), [(NIB, fr), (BLKf, a("SU", 256 * h, 256 * h + 128)), (BLK, a("N2", 128 * h, 128 * h + 128))])
+
+        def lk_list(h):
+            tt(a("Rp", 128 * h, 128 * h + 128), a("B%d" % (2 * h), 128, 256), a("SU", 256 * h + 128, 256 * h + 256), Op.max)
+            cp(a("Rq", 128 * h, 128 * h + 128), a("Rp", 128 * h, 128 * h + 128))
+
+        def cells(eng, lo, hi):
+            line[0] = "gathers"
+            gather(eng, a("GX", 16 * lo, 16 * hi), XO, a("Rq", lo, hi))
+            line[0] = None
+
+        def scans(lo, hi):
+            n = 16 * (hi - lo)
+            line[0] = "scans"
+            scan(a("MX", 16 * lo, 16 * hi), a("RS0", 0, n), a("GX", 16 * lo, 16 * hi), Op.mult, Op.max)
+            scan(a("MN", 16 * lo, 16 * hi), a("RS1", 0, n), a("GX", 16 * lo, 16 * hi), Op.add, Op.min)
+            line[0] = None
+
+        def turn_locks():
+            for kh in range(4):
+                mms(a("B4", 64 * kh, 64 * kh + 64), [(m("QM", 4 * kh + sl), a("Lo", sl, E, 4)) for sl in range(4)])
+
+        ql = q0 if t == 0 else a("qs", 32 * t - 32, 32 * t - 16)
+
+        def orphans():
+            act(a("OG"), ind(XR, ql))
+            mms(a("B3", 0, 256), [(BLK, a("OG"))])
+
+        def y_val(l0, l1):
+            mx, mn = a("MX", 16 * l0 + 15, 16 * l1, 16), a("MN", 16 * l0 + 15, 16 * l1, 16)
+            mms(a("B1", l0, l1), [(BC0, mx), (BC0, mn)], False, l1 == E)
+            mms(a("B5", l0, l1), [(HID, mx), (HID, mn)])
+            for r in range(4):
+                take("Y%d" % r, a("Y4", 4 * l0 + r, 4 * l1, 4), a("B5", l0, l1), 1023.75)
+                if r == 0:
+                    take("Y", a3("Ys", t, t + 1, l0, l1), a("Y4", 4 * l0, 4 * l1, 4), -1024.0)
+
+        def primaries():
+            scan(a("YS"), a("RS0", 0, E), a("B1", 0, E), Op.mult, Op.max)
+            tt(yi, a("YS", 15, E, 16), kq, Op.max)
+            ts(y7, yi, 7, Op.bitwise_and)
+            tt(qf, y7, b12, Op.add)
+            if not last:
+                act(oT, y7)
+                act(kq, y7, bias=512.0)
+            cp(a("qs", 32 * t, 32 * t + (16 if last else 32)), a("sf", 0, 16 if last else 32))
+            cp(ind(XR, a("qs", 32 * t, 32 * t + 16)), Y)
+
+        lk_open(0)
+        lk_open(1)
+        if t > 0:
             own_update(t - 1)
-        act(a("FR"), a("B0", 0, 256), AF.Relu, bias=-1535.0)
-        mms(a("B1", 0, 256), [(W1, a("FR"))], False, False)
-        mms(a("B1", 256, 512), [(IB, a("FR"))], False)
-        mms(a("B2", 0, 256), [(NBLK, a("FR"))], False)
-        act(a("Lo"), a("B0", 0, 256))
-        act(a("SU", 0, 256), a("B1", 0, 256), AF.Relu, bias=OFF - 4096.0)
-        act(a("N2"), a("B2", 0, 256), AF.Relu)
-        act(a("SU", 256, 512), a("B1", 256, 512), AF.Relu, bias=OFF - 4096.0)
-        mms(a("B3", 256, 512), [(NIB, a("FR")), (BLKf, a("SU", 0, 256)), (BLK, a("N2"))])
-        mms(a("B0", 0, 256), [(ID, a("Lo")), (NID, a("Ro"))])
-        tt(a("Rp"), a("B3", 256, 512), a("SU", 256, 512), Op.max)
-        cp(a("Rq"), a("Rp"))
-        for c in range(4):
-            gather("a", a("GX", 1024 * c, 1024 * c + 1024), XO, a("Rq", 64 * c, 64 * c + 64))
-        ql = q0 if t == 0 else a("qs", 16 * t - 16, 16 * t)
-        if t == 0:
-            for u in range(RO - 1):
-                lock_rows(u)
         else:
+            cp(a("PF", 0, 1536), a("PI", 0, 1536))
+        steps = {"L": lk_gather, "X": cells, "P": lk_pick, "F": lk_free, "S": lk_first, "R": lk_list}
+        for st in CFG["s1_0" if t == 0 else "s1"]:
+            steps[st[0]](*st[1:])
+        if t == 0:
+            cp(a("PF", 1536, W), a("PI", 1536, W))
+        turn_locks()
+        if t > 0:
+            recv(nxt, [a3("Nr", t - 1, t, 0, 272)], "r_n%d" % (t - 1))
             cp(ind(XR, a("ws", 16 * t - 16, 16 * t)), a("ZE", 0, E))
-        tt(dq, b12, qf, Op.subtract)
-        for c in range(4):
-            lo, hi = 1024 * c, 1024 * c + 1024
-            if c == 2 and t > 0:
-                recv(nxt, [a3("Nr", t - 1, t, 0, E), a("xr", 16 * t - 16, 16 * t)], "r_n%d" % (t - 1))
-                cp(ind(XR, a("xr", 16 * t - 16, 16 * t)), a3("Nr", t - 1, t, 0, E))
-            scan(a("MX", lo, hi), a("RS0"), a("GX", lo, hi), Op.mult, Op.max)
-            scan(a("MN", lo, hi), a("RS1"), a("GX", lo, hi), Op.add, Op.min)
-            if c == 2:
-                act(a("OG"), ind(XR, ql))
-            if c == 3:
-                to_list(a("B4", 0, 16), "OH", ("OG", 0), 256)
-            if c >= 2:
-                l0, l1, bank = (0, 192, "B3") if c == 2 else (192, 256, "B6")
-                mms(a(bank, l0, l1), [(ID, a("NH", l0, l1)), (ID, a("MX", 16 * l0 + 15, 16 * l1, 16)), (ID, a("MN", 16 * l0 + 15, 16 * l1, 16))])
-                act(a("t1", l0, l1), a(bank, l0, l1), bias=MAGIC, scale=0.5)
-                act(a3("Ys", t, t + 1, l0, l1), a("t1", l0, l1), bias=-MAGIC)
-        ts(a("Lu"), a("Lo"), OFF, Op.add)
-        ts(oT, a("B4", 0, 16), 0.0, Op.is_equal)
-        tt(dq, dq, oT, Op.mult)
-        tt(kq, dq, qf, Op.add)
-        mms(a("B4", 16, 32), [(m("S0", k), (T.Ys[:, t, k:E:16], Y[1])) for k in range(16)])
-        mms(a("B5", 0, 256), [(ID, a("KC")), (ID, a("C21"))], True, False)
-        def spread(h, k):
-            o, i = a("YR", 2048 * h + k, 2048 * h + 2048, 16), a3("Ys", t, t + 1, 128 * h, 128 * h + 128)
-            if (h, k) in CFG["yg"]:
-                gcopy(o, i, 128)
-            else:
-                act(o, i)
-        late = CFG["yg"][4:]
-        for h in range(2):
-            for k in range(16):
-                if (h, k) not in late:
-                    spread(h, k)
-        cp(yi, a("B4", 16, 32))
-        ts(y7, yi, 7, Op.bitwise_and)
-        tt(om, y7, oT, Op.mult)
-        tt(qf, om, kq, Op.add)
-        ql = a("qs", 16 * t, 16 * t + 16)
-        cp(ql, qf)
-        cp(ind(XR, ql), Y)
+            cp(ind(XR, a3("Nr", t - 1, t, 256, 272)), a3("Nr", t - 1, t, 0, E))
+        for lo, hi in CFG["sc"]:
+            scans(lo, hi)
+        ts(a("Lu"), a("B4", 0, 256), OFF, Op.add)
+        orphans()
+        act(a("OR"), a("B3", 0, 256), AF.Relu, bias=1.0, scale=-1.0)
+        mms(a("B1", 0, E), [(ID, a("OD", 0, E)), (I1024, a("OR"))], True, False)
+        for lo, hi in CFG["yp"]:
+            y_val(lo, hi)
+        primaries()
+        ql = a("qs", 32 * t, 32 * t + 16)
         send(nxt, a3("Yr", t, t + 1, 0, E), Y, "r_y%d" % t)
         send(nxt, a("qr", 16 * t, 16 * t + 16), ql, "r_y%d" % t)
-        for h, k in late:
-            spread(h, k)
         if last:
             send(prv, a("zr"), Y, "r_zo")
-        mms(a("B7", 0, 256), [(BLK, a("OG"))])
-        act(a("OR"), a("B7", 0, 256), AF.Relu, bias=1.0, scale=-1.0)
-        mms(a("B7", 256, 512), [(I255, a("OR")), (NID, Y)])
-        act(a("DL"), a("B0", 0, 256))
+        else:
+            gcopy(a("XO", W, W + E), Y, E)
+        mms(a("B7", 256, 512), [(I255, a("OR", 0, 256)), (NID, Y)])
+        act(a("U"), a("B7", 256, 512), AF.Abs)
+        mms(a("B7", 0, 256), [(ID, a("Ro")), (I12, a("U"))])
+        mms(a("B7", 256, 512), [(ID, Lo), (I12, a("U"))])
+        act(a("SG"), a("B7"), AF.Sign, bias=-1534.5)
+        mms(a("B7", 0, 256), [(ID, a("Ro")), (I12, a("U")), (I1536, a("SG", 0, 256))], True, False)
+        mms(a("B0", 256, 512), [(ID, Lo), (NID, a("Ro")), (I1536, a("SG", 256, 512)), (P1536, a("SG", 0, 256))])
+        take("DL", a("DL"), a("B0", 256, 512))
+
+        parts = (("B5", 0, "B6", 0, 0, CFG["kcut"]), ("B5", 16, "B6", 16, CFG["kcut"], 16))
+        if CFG["kcut"] < 16:
+            parts = (("B5", 0, "B6", 0, 0, CFG["kcut"]), ("B2", 0, "B3", 0, CFG["kcut"], 16))
+        parts = [p for p in parts if p[4] < p[5]]
+        for bd, _, bn, _, k0, k1 in parts:
+            mms(a(bd, 0, 256), [(ID, a("KC")), (ID, a("C21"))], True, False)
+            mms(a(bn, 0, 256), [(ID, a("C16"))], True, False)
+        if not last:
+            act(a("JG"), ind(a("J"), a("qs", 32 * t + 16, 32 * t + 32)))
+            mms(a("B1", 256, 512), [(IDf, a("CT")), (NID, a("AD", t, t + E)), (NID, a("JG"))])
+            take("C2", a("C2"), a("B1", 256, 512), 0.0, True)
         for c in range(4):
-            lo, hi = 1024 * c, 1024 * c + 1024
-            tt(a("D", lo, hi), ind(XR, a("Lu", 64 * c, 64 * c + 64)), a("YR", lo, hi), Op.subtract)
-            act(a3("AB", 4 * c, 4 * c + 4, 0, 256), a("D", lo, hi), AF.Abs, scale=64.0)
-            ge = [(m("OH", k), a3("GE", 4 * c, 4 * c + 4, 16 * k, 16 * k + 16)) for k in range(16)]
-            if c in CFG["sign"]:
-                act(a3("GE", 4 * c, 4 * c + 4, 0, 256), a("D", lo, hi), AF.Sign, bias=0.5)
-                ge = [(ID, a("C16"))] + ge
-            else:
-                ts(a3("GE", 4 * c, 4 * c + 4, 0, 256), a("D", lo, hi), 0.0, Op.is_ge, 2.0, Op.mult)
-            if c == 1:
-                act(a("U"), a("B7", 256, 512), AF.Abs)
-                if not last:
-                    tt(dq, qf, b12, Op.subtract)
-                    ts(jl, dq, a("pc", 5 + t, 6 + t), Op.add)
-            if c == 2 and not last:
-                act(a("JG"), ind(a("J"), jl))
-            if c not in CFG["sign"]:
-                mms(a("B6", 64 * c, 64 * c + 64), ge)
-            mms(a("B5", 64 * c, 64 * c + 64), [(m("OH", k), a3("AB", 4 * c, 4 * c + 4, 16 * k, 16 * k + 16)) for k in range(16)], False, False)
-            if c in CFG["sign"]:
-                mms(a("B6", 64 * c, 64 * c + 64), ge)
-        recv(prv, [a3("Yr", t, t + 1, 0, E), a("qr", 16 * t, 16 * t + 16)], "r_y%d" % t)
-        cp(ind(XO, a("qr", 16 * t, 16 * t + 16)), a3("Yr", t, t + 1, 0, E))
-        act(a("CS"), a("B6", 0, 256), AF.Sign, bias=-17.0)
-        mms(a("B5", 0, 256), [(HID, a("CS"))], False)
-        act(a("GK"), a("B6", 0, 256), AF.Abs, bias=-6.5 * BIG, scale=BIG / 2)
-        mms(a("B7", 0, 256), [(ID, a("Ro")), (I12, a("U"))], True, False)
-        if not last:
-            act(a("XO", W, W + E), Y)
-        if t == 0:
-            for k in range(16):
-                act(a("TS", 64 * k, 64 * k + 64), TOS, AF.Sign, bias=a("MK", 32 + k, 33 + k))
-        tt(a("KY"), a("B5", 0, 256), a("GK"), Op.min)
-        if not last:
-            mms(a("B6", 256, 512), [(IDf, a("CT", E * t, E * t + E)), (ID, a("JG"))])
-            act(a("C2"), a("B6", 256, 512))
-        mms(a("B5", 0, 256), [(ID, a("Ro")), (I12, a("U"))], True, False)
+            line[0] = "step 3"
+            for lo, hi in CFG["dq"][c]:
+                dd = a("D", 1024 * c + 64 * lo, 1024 * c + 64 * hi)
+                tt(dd, ind(XR, a("Lu", 64 * c + 4 * lo, 64 * c + 4 * hi)), a("Y4", 64 * lo, 64 * hi), Op.subtract)
+                ge = v("GE", S(16 * c + lo, 16 * c + hi), ALL)
+                if (c, lo) in CFG["gev"]:
+                    ts(ge, dd, -1024.0, Op.is_ge, 2.0, Op.mult)
+                else:
+                    act(ge, dd, AF.Sign, bias=1024.5)
+                act(v("AB", S(16 * c + lo, 16 * c + hi), ALL), dd, AF.Abs, bias=65536.0, scale=64.0)
+            line[0] = None
+            bd, _, bn, _, k0, k1 = [p for p in parts if p[4] <= 4 * c < p[5]][0]
+            for src, bank in (("GE", bn), ("AB", bd)):
+                mms(v(bank, S(0, 16), S(4 * c, 4 * c + 4)),
+                    [(m("OH", s), v(src, S(16 * c, 16 * c + 16), S(4 * s, 4 * s + 4))) for s in range(16)], False,
+                    4 * c + 4 == k1 and src == "GE")
+            if 4 * c + 4 == k1:
+                n, d, ks = v(bn, S(0, 16), S(k0, k1)), v(bd, S(0, 16), S(k0, k1)), S(k0, k1)
+                act(v("CS", ALL, ks), n, AF.Sign, bias=-17.0)
+                act(v("GK", ALL, ks), n, AF.Abs, bias=-6.5 * BIG, scale=BIG / 2)
+                mms(d, [(HID, v("CS", ALL, ks))], False)
+                tt(a("KY"), d, v("GK", ALL, ks), Op.min)
         scan(a("KS"), a("RS0", 0, 256), a("KY"), Op.mult, Op.max)
         ts(cd, a("KS", 15, 256, 16), 63, Op.bitwise_and)
         cp(cu, cd)
-        tt(a("SB", 256, 512), ind(TOH, cu), a("Ro"), Op.mult)
-        tt(a("SB", 0, 256), ind(TOL, cu), a("Lo"), Op.mult)
-        act(a("LN", 256, 512), ind(TNC, cu))
-        act(a("NL"), ind(TNL, cu))
-        h0, h1 = (0, 256) if last else (256, 0)
-        mms(a("B0", 256, 512), [(BLK, a("SB", 256, 512))])
-        mms(a("B3", 0, 256), [(BLK, a("SB", 0, 256))])
-        to_list(a("B4", 32, 64), "OH", ("SB", 0), 512)
-        act(a("TB", h0, h0 + 256), a("B0" if h0 else "B3", h0, h0 + 256))
-        act(tT, a("B4", 32, 64))
-        tt(a("MM"), ind(TOC, cu), a("DL"), Op.mult)
-        ts(c33, cd, 33, Op.bitwise_and)
-        ts(kk, cd, 1, Op.logical_shift_right, 15, Op.bitwise_and)
-        ts(nl, c33, 32.0, Op.not_equal, 5000.0, Op.mult)
-        tt(ef, b16, kk, Op.subtract)
-        if not last:
-            ts(c1l, cd, a("pc", 8 + t, 9 + t), Op.add)
-        cp(el, ef)
-        tt(wT, a("sf", 96, 112), nl, Op.add)
-        mms(a("B7", 0, 256), [(IDf, a("MM"))], False)
-
-        def second_half():
-            act(a("TB", h1, h1 + 256), a("B0" if h1 else "B3", h1, h1 + 256))
-
-        def winners():
-            pairs("E2", 256, 112, a("B2", 0, 256), [])
-
-        def winners_b():
-            act(a("LN", 0, 256), a("B2", 0, 256), AF.Relu, scale=float(2 ** 24))
-            mms(a("B3", 0, 32), [(ID, a("ZE", 0, 32))], True, False)
-            mms(a("B3", 0, 16), [(IDf, a("sf", 112, 128))], False, False)
-            to_list(a("B3", 0, 32), "OH", ("LN", 0), 512, False)
-
-        def winner_lists():
-            tt(lm, a("B3", 0, 32), dum2, Op.min)
-            tt(a("sf", 144, 160), a("sf", 128, 144), a("sf", 144, 160), Op.max)
-            ts(a("xs", 32 * t, 32 * t + 32), lm, OFF, Op.add)
+        line[0] = "picks"
+        for hh in (0, 256) if last else CFG["picks"]:
+            bank = "B0" if hh else "B3"
+            if hh:
+                tt(a("SB", 256, 512), ind(TOH, cu), a("Ro"), Op.mult)
+            else:
+                tt(a("SB", 0, 256), ind(TOS, cu), Lo, Op.mult)
+            if hh:
+                mms(a(bank, 256, 512), [(BLK, a("SB", hh, hh + 256))])
+                to_list(a("B4", 288, 304), "OH", ("SB", hh), 256)
+            else:
+                act(a("NE"), ind(TNL, cu), scale=256.0)
+                mms(a(bank, 256, 512), [(BLK, a("NE")), (BLK, a("SB", hh, hh + 256))])
+                to_list(a("B6", 288, 304), "OH", ("NE", 0), 256, True, False)
+                to_list(a("B6", 288, 304), "OH", ("SB", 0), 256, False)
+        line[0] = None
 
         def wipes():
-            pairs("E1", 0, 160, a("B1", 0, 256), [(ID, a("NL"))])
-
-        def wipes_b():
-            act(a("LW"), a("B1", 0, 256), AF.Relu, scale=float(2 ** 24))
-            mms(a("B4", 32, 48), [(IDf, a("sf", 96, 112))], True, False)
-            to_list(a("B4", 32, 48), "OH", ("LW", 0), 256, False)
-
-        def wipe_list():
+            act(a("TB", E, 2 * E), a("B3", 256, 512))
+            act(wT, a("B6", 288, 304))
+            act(a("sf", 96, 112), a("B6", 288, 304), bias=-4096.0)
+            pairs("E1", lambda lo: a("TB", E + lo, 2 * E), 160, "B1", CFG["eqa1"])
+            act(a("LW"), a("B1", 0, 256), AF.Relu)
+            mms(a("B5", 0, 16), [(IDf, wT)], True, False)
+            to_list(a("B5", 0, 16), "OH", ("LW", 0), 256, False)
+            tt(lw, a("B5", 0, 16), dum, Op.min)
             wl = a("ws", 16 * t, 16 * t + 16)
-            tt(lw, a("B4", 32, 48), a("cT", 48, 64), Op.min)
             ts(wl, lw, OFF, Op.add)
             send(nxt, a("wr", 16 * t, 16 * t + 16), wl, "r_w%d" % t)
 
-        def move_a():
-            act(a("SG"), a("B7", 0, 256), AF.Sign, bias=-1534.5)
-
-        def move_p():
-            mms(a("B5", 0, 256), [(IDf, a("MM")), (I1536, a("SG"))], False)
-
-        def move_b():
-            if last:
-                act(a("RS"), a("B5", 0, 256), bias=1.0)
-                send(prv, a("rr"), a("RS"), "r_ro")
-            else:
-                act(a("Ro"), a("B5", 0, 256), bias=1.0 - OFF)
-
-        def partner():
-            mms(a("B6", 256, 512), [(ID, Y), (ID, a("DK"))])
-            act(a("EV"), a("B6", 256, 512))
-
+        def winners():
+            act(a("TB", 0, E), a("B0", 256, 512))
+            act(a("sf", 112, 128), a("B4", 288, 304))
+            pairs("E2", lambda lo: a("TB", lo, E), 112, "B2", CFG["eqa2"])
+            act(a("LN", 0, E), ind(COM, cu), scale=-4352.0, bias=4096.0)
+            act(a("LN", E, 2 * E), a("B2", 0, 256), AF.Relu)
+            mms(a("B4", 320, 352), [(ID, a("ZE", 0, 32))], True, False)
+            mms(a("B4", 336, 352), [(IDf, a("sf", 112, 128))], False, False)
+            to_list(a("B4", 320, 352), "OH", ("LN", 0), 512, False)
+        for hh in (0, 256) if last else CFG["picks"]:
+            (winners if hh else wipes)()
+        tt(a("MM"), ind(TOC, cu), a("DL"), Op.mult)
+        mms(a("B7", 0, 256), [(IDf, a("MM"))], False)
+        if not last:
+            act(a("sf", 128, 144), cd, bias=a("pc", 8 + t, 9 + t))
+        ts(a("su", 48, 80 if last else 96), a("sf", 96, 128 if last else 144), OFF, Op.add)
+        act(a("EV"), ind(XR, el))
         if last:
-            pairs_a("E1", 0, 160)
-            second_half()
-            move_a()
-            wipes()
-            wipes_b()
-            pairs_a("E2", 256, 112)
-            winners()
-            wipe_list()
-            move_p()
-            move_b()
-            winners_b()
-            act(a("DK"), ind(a("D"), el))
-            partner()
-            winner_lists()
+            act(a("RS"), a("B7", 0, 256), bias=1.0)
+            send(prv, a("rr"), a("RS"), "r_ro")
         else:
-            pairs_a("E2", 256, 112)
-            second_half()
-            move_a()
-            winners()
-            winners_b()
-            move_p()
-            pairs_a("E1", 0, 160)
-            act(a("C1"), ind(a("TS"), c1l), bias=-256.0, scale=1792.0)
-            move_b()
-            wipes()
-            winner_lists()
-            pl = a("xs", 32 * t, 32 * t + 16)
-            tt(a("PT"), ind(PF, pl), a("C1"), Op.max)
+            act(a("Ro"), a("B7", 0, 256), bias=1.0 - OFF)
+            act(a("C1"), ind(a("TS"), c1l), bias=1536.0, scale=1536.0)
+            tt(a("PT"), ind(PF, cl), a("C1"), Op.max)
             ts(a("Ru"), a("Ro"), OFF, Op.add)
-            act(a("DK"), ind(a("D"), el))
-            wipes_b()
-            tt(ind(PF, pl), a("PT"), a("C2"), Op.add)
-            wipe_list()
-            mms(a("B6", 256, 512), [(ID, Y), (ID, a("DK"))])
+        tt(a("sf", 208, 240), a("B4", 320, 352), dum2, Op.min)
+        if not last and CFG["pl"]:
+            ts(a("pl"), a("sf", 224, 240), OFF, Op.add)
+            tt(ind(PF, a("pl")), a("PT"), a("C2"), Op.subtract)
+        tt(a("sf", 208, 224), a("sf", 208, 224), a("sf", 224, 240), Op.max)
+        wide = 16 if last or CFG["pl"] else 32
+        ts(a3("Ns", t, t + 1, 256, 256 + wide), a("sf", 208, 208 + wide), OFF, Op.add)
+        if not last and not CFG["pl"]:
+            tt(ind(PF, a3("Ns", t, t + 1, 272, 288)), a("PT"), a("C2"), Op.subtract)
+        recv(prv, [a3("Yr", t, t + 1, 0, E), a("qr", 16 * t, 16 * t + 16)], "r_y%d" % t)
+        cp(ind(XO, a("qr", 16 * t, 16 * t + 16)), a3("Yr", t, t + 1, 0, E))
+    now[0] = RO
     own_update(RO - 1)
     recv(nxt, [a("zr")], "r_zo")
     dma("s", hbm("zo"), a("zr"))
@@ -542,48 +651,119 @@ def rank_program(g, core, T, topo):
     dma("s", hbm("xo", 0, H), a("XO", 0, H))
     dma("a", hbm("xo", H, W), a("XO", H, W))
 
-    def meet(x, y, cross):
-        if cross and SCRATCH[x[0]][0] == "psum":
-            return True
-        if x[1] >= y[2] or y[1] >= x[2]:
-            return False
-        return not (x[3] > 1 and x[3] == y[3] and (x[1] - y[1]) % x[3])
-
-    seen = {}
+    seen, bank, chain, sent_as = {}, {}, {}, {}
     for j, o in enumerate(ops):
-        deps = {}
-        for r, w in [(r, False) for r in o["rd"]] + [(r, True) for r in o["wr"]]:
-            ps = SCRATCH[r[0]][0] == "psum"
-            for (i, r2, w2) in seen.get(r[0], []):
-                p = ops[i]
-                cross = p["eng"] != o["eng"]
-                if ps and not cross and o["eng"] == "p":
+        pre = {}
+        for (name, mask), w in [(r, False) for r in o["rd"]] + [(r, True) for r in o["wr"]]:
+            if SCRATCH[name][0] == "psum":
+                i = bank.get(name, j)
+                if i != j:
+                    pre[i] = pre.get(i, False) or ops[i]["eng"] != o["eng"]
+                bank[name] = j
+                if o["eng"] == "p":
                     continue
-                if (w or w2 or (ps and cross)) and meet(r, r2, cross) and not p.get("remote"):
-                    key = p.get("sem", p["eng"])
-                    deps[key] = max(deps.get(key, -1), i)
-                elif w and p.get("remote") and meet(r, r2, cross):
-                    assert p["remote"] == "left"
-                    deps["left"] = max(deps.get("left", -1), i)
-        o["deps"] = {} if o["eng"] == "x" else deps
-        for r, w in [(r, False) for r in o["rd"]] + [(r, True) for r in o["wr"]]:
-            seen.setdefault(r[0], []).append((j, r, w))
-    done = {}
+            keep = []
+            for (i, m2, w2) in seen.get(name, []):
+                if i != j and (w or w2) and mask & m2:
+                    if ops[i].get("remote") != "sent":
+                        same = ops[i]["eng"] == o["eng"] and o["eng"] in "va" and "sem" not in ops[i] and w and CFG["lax"]
+                        pre[i] = pre.get(i, False) or (o["eng"] != "x" and not same)
+                if i == j or not (w and not m2 & ~mask):
+                    keep.append((i, m2, w2))
+            seen[name] = keep + [(j, mask, w)]
+        ln = "remote" if o.get("remote") else "dma" if "dma" in o else o["line"] if o["eng"] == "p" or not ORDER["v"] else None
+        if ln:
+            if ln in chain:
+                pre.setdefault(chain[ln], False)
+            chain[ln] = j
+        if o.get("remote"):
+            sent_as.setdefault(o["msg"], []).append(j)
+        o["pre"] = pre
+    for e in "va":
+        prev = None
+        for t in range(RO):
+            left = [j for j, o in enumerate(ops) if o.get("name", (0, 0))[:2] == (t, e)]
+            for name in ORDER[e + ("0" if t == 0 else "3" if t == RO - 1 else "")].split():
+                head, tail = (name + "*").split("*")[:2]
+                hit = [j for j in left if ops[j]["name"][2].startswith(head) and ops[j]["name"][2].endswith(tail)]
+                for j in hit:
+                    left.remove(j)
+                    if prev is not None:
+                        ops[j]["pre"].setdefault(prev, False)
+                    prev = j
     for o in ops:
-        keep = {}
-        for key, i in o["deps"].items():
-            if done.get((o["eng"], key), -1) < i:
-                done[(o["eng"], key)] = i
-                keep[key] = i
+        if o["eng"] == "x":
+            o["pre"].update({i: False for i in sent_as[o["sem"]]})
+
+    before, after = [[] for o in ops], [[] for o in ops]
+    moved_bytes = {True: 0, False: 0}
+    for o in ops:
+        if "dma" in o:
+            moved_bytes[bool(o["wr"])] += o["dma"]
+            o["lat"] = START + moved_bytes[bool(o["wr"])] / HBM
+    for j, o in enumerate(ops):
+        for i, sem in o["pre"].items():
+            gap = ops[i]["lat"] if sem or o["eng"] == "x" else 0
+            before[j].append((i, gap))
+            after[i].append((j, gap))
+
+    def lay(pre, post, rank_of, first):
+        todo, end, busy = [len(x) for x in pre], [0.0] * len(ops), {e: [] for e in "vapcsx"}
+        ready = [j for j in range(len(ops)) if not todo[j]]
+        while ready:
+            j = min(ready, key=lambda k: (rank_of[k], k))
+            ready.remove(j)
+            at, c, q = max([end[i] + gap for i, gap in pre[j]] + [first[j]]), ops[j]["cost"], busy[ops[j]["eng"]]
+            n = len(q)
+            while n and q[n - 1][1] > at:
+                n -= 1
+            while n < len(q) and q[n][0] < at + c:
+                at = max(at, q[n][1])
+                n += 1
+            if c:
+                q.insert(n, (at, at + c))
+            end[j] = at + c
+            for k, gap in post[j]:
+                todo[k] -= 1
+                if not todo[k]:
+                    ready.append(k)
+        assert not any(todo), [ops[j].get("name") for j in range(len(ops)) if todo[j]][:20]
+        return end
+
+    zero, lat = [0.0] * len(ops), [o["lat"] for o in ops]
+    if "hook" in CFG:
+        CFG["hook"](ops, before, after, lay)
+    best, first = None, CFG.get("first") or [o["rank"] for o in ops]
+    for n in range(PASSES):
+        end = lay(before, after, first, zero)
+        span = max(x + y for x, y in zip(end, lat))
+        if best is None or span < best[0]:
+            best = (span, end)
+        first = [-x for x in lay(after, before, [-x for x in end], lat)]
+    order = sorted(range(len(ops)), key=lambda j: (best[1][j] - ops[j]["cost"], best[1][j], j))
+
+    place = {j: n for n, j in enumerate(order)}
+    done = {e: {} for e in "vapcsx"}
+    for j in order:
+        o, known = ops[j], done[ops[j]["eng"]]
+        o["deps"] = {}
+        for i in sorted([i for i, sem in o["pre"].items() if sem], key=lambda i: -place[i]):
+            key = ops[i].get("remote") or ops[i].get("sem", ops[i]["eng"])
+            if place[i] > known.get(key, -1):
+                o["deps"][key] = i
                 ops[i]["inc"] = True
-        o["deps"] = keep
+                known[key] = place[i]
+                for k, p in ops[i]["knew"].items():
+                    known[k] = max(known.get(k, -1), p)
+        o["knew"] = dict(known) if CFG["transitive"] else {}
     cnt = {"v": 0, "a": 0, "p": 0, "c": 0}
-    for o in ops:
+    for j in order:
+        o = ops[j]
         if o["eng"] == "x":
             continue
         q = Q[o["eng"]]
         for key, i in o["deps"].items():
-            q.wait_ge(T.sem[key], ops[i]["val"])
+            q.wait_ge(T.sem[key], out_cnt[key] if key in out_cnt else ops[i]["val"])
         ins = o["fn"]()
         if o.get("remote"):
             continue

@@ -26,13 +26,29 @@ CFG = {
            ("X", "a", 0, 32), ("S", 1), ("R", 1), ("X", "a", 32, 64), ("X", "a", 64, 128), ("X", "v", 128, 160),
            ("X", "a", 160, 192), ("X", "a", 192, 224), ("X", "a", 224, 256)),
     "sc": ((0, 64), (64, 128), (128, 192), (192, 224), (224, 256)),
-    "yp": ((0, 256),), "cuts": (0, 768, 1792, W), "rz": (0, 1), "pl": True, "late": 0,
+    "yp": ((0, 256),), "cuts": (0, 768, 1792, W), "rz": (0, 1), "pl": True, "late": 0, "ypool": (), "upper": True, "eqa3": tuple(range(10, 16)), "via": (), "whole": False,
     "gxv": 32,
 }
 ORDER = {"v": "GL:1024< GL:3072< XO:0<ZE SX Ns*<SX Rp:0< XO:0<Ns Rq:0< Rp:128 XR:0<ZE Rq:128 MN:1024< MX:1024< XR:0<Nr MX:0< MN:0< MX:2048< MX:3072< MN:3072< MN:2048< MX:3584< MN:3584< Lu YS si:0< si:16< sf:0< qs XR:0<Ys D:0< D:512< D:1024< D:3072< D:2560< D:2048< GE:2560< D:3584< GE:3072< GE:3584< XO:0<Yr KY KS si:32 su:32 SB:256 SB:0 MM E2 E1 su:48 sf:208<B4 sf:208<sf Ns*<sf PT Ru PF:0<PT sf:192 ws", "a": "GL:0< GL:2048< FR:0< Lo:0< SU:0< GL:3584< N2:0< FR:128 Lo:128 SU:256 N2:128 GX:1024< GX:0< GX:2048< GX:3072< OG GX:3584< OR Y4:0< Y4:1< Ys sf:16<si U Y4:2< sf:48<si Y4:3< SG JG DL AB:0< GE:0< GE:512< AB:512< C2 AB:1024< GE:1024< AB:2560< GE:2048< AB:2048< AB:3072< AB:3584< CS GK LN:0< NE TB:0< sf:112 sf:128 E2*<TB TB:256 sf:160 E2*<E2 sf:96 Ro LN:256 E1*<TB C1 E1*<E1 LW EV", "v0": "QM PF:0<PI OH GL:1024< GL:3072< PF:1536<PI Rp:0< Rq:0< Rp:128 GX:0< Rq:128 MX:1024< Lu MN:1024< MX:0< MN:0< MX:2048< MX:3072< MN:2048< MN:3072< MX:3584< MN:3584< YS si:0< si:16< sf:0< qs XR:0<Ys D:0< D:512< D:1024< D:3072< D:3584< D:2560< GE:3584< D:2048< GE:2560< XO:0<Yr GE:3072< KY KS si:32 su:32 SB:256 SB:0 MM E2 E1 su:48 sf:208<B4 sf:208<sf Ns*<sf PT PF:0<PT Ru sf:192 ws", "a0": "GL:0< GL:2048< FR:0< SU:0< Lo:0< N2:0< FR:128 Lo:128 SU:256 N2:128 GX:1024< GX:512< GX:2048< GX:3072< OG GX:3584< OR Y4:0< Y4:1< Ys sf:16<si Y4:2< sf:48<si Y4:3< U JG SG AB:0< GE:0< DL C2 GE:512< AB:512< GE:1024< AB:3072< AB:1024< AB:2560< GE:2048< AB:2048< AB:3584< CS GK TS LN:0< NE TB:0< sf:128 sf:112 TB:256 E2*<TB sf:160 E2*<E2 sf:96 Ro LN:256 E1*<TB C1 E1*<E1 LW EV", "v3": "GL:1024< GL:3072< XO:0<ZE SX Ns*<SX Rp:0< XO:0<Ns Rq:0< Rp:128 Rq:128 XR:0<ZE MN:1024< MX:1024< XR:0<Nr MX:0< MN:0< MX:3072< MN:3072< MX:2048< MN:2048< MX:3584< MN:3584< Lu YS si:0< si:16< sf:0< qs XR:0<Ys D:0< D:512< D:1024< D:3072< D:2560< D:2048< GE:2560< D:3584< GE:3072< GE:3584< XO:0<Yr KY KS si:32 su:32 SB:0 SB:256 MM E1 su:48 sf:192 ws E2 sf:208<B4 sf:208<sf Ns*<sf", "a3": "GL:0< GL:2048< FR:0< Lo:0< SU:0< GL:3584< N2:0< FR:128 Lo:128 SU:256 N2:128 GX:1024< GX:0< GX:3072< GX:2048< OG GX:3584< OR Y4:0< Y4:1< Ys U Y4:2< Y4:3< SG AB:0< GE:0< GE:512< AB:512< DL AB:1024< GE:1024< AB:2560< GE:2048< AB:2048< AB:3072< AB:3584< CS GK NE TB:256 LN:0< sf:160 E1*<TB sf:96 TB:0< E1*<E1 LW sf:112 E2*<TB RS EV E2*<E2 LN:256"}
 
 
 ORDER = {"v": "GL:1024< GL:3072< XO:0<ZE SX Ns*<SX Rp:0< XO:0<Ns Rq:0< XR:0<ZE Rp:128 Rq:128 MX:1024< MN:1024< MX:0< MN:0< XR:0<Nr MX:2048< MN:3072< MX:3072< MN:3584< MX:3584< MN:2048< Lu YS si:0< si:16< sf:0< qs XR:0<Ys D:0< D:512< D:1024< D:2560< D:2048< D:3072< D:3584< GE:2560< GE:3072< GE:3584< KY KS si:32 su:32 SB:256 SB:0 E2 E1 su:48 MM sf:208<B4 sf:208<sf PT pl Ns*<sf PF:0<PT Ru sf:192 ws XO:0<Yr", "a": "GL:0< GL:2048< FR:0< Lo:0< GL:3584< SU:0< N2:0< FR:128 Lo:128 SU:256 N2:128 GX:1024< GX:0< GX:2048< GX:3072< GX:3584< OG OR Y4:0< Y4:1< Ys sf:16<si Y4:2< U Y4:3< sf:48<si JG SG C2 AB:0< GE:0< DL GE:512< AB:512< GE:1024< AB:2560< AB:1024< AB:2048< GE:2048< AB:3072< AB:3584< CS GK NE LN:0< TB:0< sf:112 E2*<TB TB:256 sf:160 E2*<E2 sf:128 sf:96 LN:256 E1*<TB C1 E1*<E1 Ro LW EV", "v0": "OH QM GL:1024< GL:3072< PF:0<PI Rp:0< Rq:0< GX:0< MX:0< MN:0< Rp:128 Rq:128 PF:1536<PI MX:1024< MN:2048< MX:2048< MN:3584< MN:1024< MX:3584< MX:3072< MN:3072< Lu YS si:0< si:16< sf:0< qs XR:0<Ys D:512< D:0< D:1024< D:2560< D:2048< GE:2560< D:3072< D:3584< GE:3072< GE:3584< KY KS si:32 su:32 SB:256 SB:0 MM E2 E1 Ru su:48 PT sf:208<B4 pl sf:208<sf PF:0<PT sf:192 ws XO:0<Yr Ns*<sf", "a0": "TS GL:0< GL:2048< FR:0< SU:0< Lo:0< N2:0< FR:128 GX:512< SU:256 N2:128 Lo:128 GX:1024< GX:2048< GX:3584< GX:3072< OG OR Y4:0< Y4:1< sf:16<si Ys Y4:2< Y4:3< U JG sf:48<si SG C2 AB:512< GE:512< GE:0< AB:0< AB:1024< GE:1024< AB:2048< AB:2560< GE:2048< AB:3584< AB:3072< CS GK DL sf:128 NE LN:0< TB:0< sf:112 E2*<TB TB:256 sf:160 E2*<E2 Ro sf:96 LN:256 E1*<TB C1 E1*<E1 LW EV", "v3": "GL:1024< GL:3072< XO:0<ZE SX Ns*<SX Rp:0< XO:0<Ns Rq:0< XR:0<ZE Rp:128 MX:1024< Rq:128 MN:1024< MX:0< MN:0< MX:3072< XR:0<Nr MX:2048< MN:3072< MN:2048< MX:3584< MN:3584< Lu YS si:0< si:16< sf:0< qs XR:0<Ys D:0< D:512< D:1024< D:2560< D:2048< D:3072< GE:2560< D:3584< GE:3072< GE:3584< KY KS si:32 su:32 SB:0 MM SB:256 E1 XO:0<Yr su:48 sf:192 ws E2 sf:208<B4 sf:208<sf Ns*<sf", "a3": "GL:0< GL:3584< GL:2048< FR:0< Lo:0< SU:0< N2:0< FR:128 SU:256 Lo:128 N2:128 GX:1024< GX:0< GX:3072< GX:2048< GX:3584< OG OR Y4:0< Y4:1< Y4:2< Ys Y4:3< U SG AB:0< GE:0< GE:512< DL AB:512< GE:1024< AB:1024< AB:2560< GE:2048< AB:2048< AB:3584< AB:3072< CS GK NE TB:256 sf:160 sf:96 sf:112 E1*<TB E1*<E1 LW TB:0< E2*<TB RS E2*<E2 LN:0< LN:256 EV"}
+
+
+_V2 = ("YS si:16< sf:0< qs XR:0<Ys D:0< D:512< D:1024< D:2048< D:2560< D:3072< GE:2560< D:3584< GE:3072< GE:3584< XO:0<Yr "
+       "KY KS si:32 su:32 ")
+_SC = "MN:1024< MX:1024< MN:2048< MX:2048< MX:3072< MN:3072< MX:3840< MN:3840< "
+_V1 = "GL:1024< XR:0<ZE XO:0<ZE SX Ns*<SX XO:0<Ns Rp:0< Rq:0< Rp:128 Rq:128 Lu GX MX:0< MN:0< XR:0<Nr " + _SC
+_V3 = "SB:256 si:64 SB:0 MM E2 su:48 E1 sf:208<B4 PT pl PF:0<PT sf:192 ws Ru sf:208<sf Ns*<sf"
+_A1 = "GL:0< GL:3584< GL:2048< GL:2560< FR:0< GL:3072< Lo:0< SU:0< N2:0< FR:128 Lo:128 SU:256 N2:128 GX:0< GX:1024< GX:2048< GX:3072< OG GX:3840< OR "
+_A2 = ("Y4:0< Ys sf:16<si Y4:1< U Y4:2< sf:48<si Y4:3< SG AB:0< GE:0< GE:512< AB:512< AB:1024< GE:1024< GE:2048< AB:2560< AB:2048< "
+       "AB:3072< AB:3584< CS GK DL JG ")
+_A3 = "C2 G:0<B2 sf:80 sf:128 TB:0< sf:176 sf:112 TB:256 E2*<TB sf:160 sf:96 E2*<E2 C1 LN E1*<TB E1*<E1 LW Ro EV"
+ORDER = {"v": _V1 + _V2 + _V3, "a": _A1 + _A2 + _A3,
+         "v0": "QM OH PF:0<PI PF:768< GL:1024< GL:3072< PF:1536<PI PF:2304< TH MK Rp:0< Rq:0< Lu GX Rp:128 Rq:128 G:0<KB MX:0< MN:0< " + _SC + _V2 + _V3,
+         "a0": "GL:0< GL:2048< FR:0< Lo:0< Os SU:0< N2:0< FR:128 Lo:128 SU:256 N2:128 GX:0< GX:1536< GX:2048< GX:3072< GX:3840< MK MB TS:0< TS:6 TS:1 TS:2 TS:3 TS:4 " + _A2 + "TS " + _A3,
+         "v3": _V1 + _V2 + "SB:0 si:64 SB:256 E1 E2:0< su:48 E2:544< MM sf:192 ws E2 sf:208<B4 sf:208<sf Ns*<sf",
+         "a3": _A1 + _A2 + "sf:80 TB:256 sf:176 sf:160 sf:96 E1*<TB TB:0< E1*<E1 sf:112 LW E2*<TB RS E2*<E2 EV LN"}
 
 
 def _s1(lg, xg):
@@ -46,12 +62,14 @@ def _s1(lg, xg):
     return tuple(o + [("X", e, lo, hi) for e, lo, hi in xg])
 
 
-CFG.update(s1=_s1([("a", 0, 64), ("v", 64, 128), ("a", 128, 192), ("v", 192, 224), ("a", 224, 256)],
-                  [("a", 0, 64), ("a", 64, 128), ("a", 128, 192), ("a", 192, 224), ("a", 224, 256)]),
+CFG.update(s1=_s1([("a", 0, 64), ("v", 64, 128), ("a", 128, 160), ("a", 160, 192), ("a", 192, 224), ("a", 224, 256)],
+                  [("a", 0, 64), ("a", 64, 112), ("v", 112, 128), ("a", 128, 192), ("a", 192, 240), ("a", 240, 256)]),
            s1_0=_s1([("a", 0, 64), ("v", 64, 128), ("a", 128, 192), ("v", 192, 256)],
-                    [("v", 0, 32), ("a", 32, 64), ("a", 64, 128), ("a", 128, 192), ("a", 192, 224), ("a", 224, 256)]),
+                    [("a", 0, 64), ("v", 64, 96), ("a", 96, 128), ("a", 128, 192), ("a", 192, 240), ("a", 240, 256)]),
+           sc=((0, 64), (64, 128), (128, 192), (192, 240), (240, 256)),
            dq=(((0, 8), (8, 16)), ((0, 16),), ((0, 8), (8, 16)), ((0, 8), (8, 16))),
-           on_v=(), gev=((2, 8), (3, 0), (3, 8)), eqa1=tuple(range(10, 16)), eqa2=tuple(range(8, 16)), picks=(256, 0))
+           on_v=(), gev=((2, 8), (3, 0), (3, 8)), eqa1=tuple(range(11, 16)), eqa2=tuple(range(9, 16)), picks=(256, 0),
+           cuts=(0, 512, 1472, 2304, W), via=(0, 1), late=3, rz=(1, 0))
 
 
 def _s(n, d):
@@ -62,15 +80,15 @@ SCRATCH = {
     "XO": _s(WIN, BF), "XR": _s(WIN, BF), "PI": _s(W, I32), "PF": _s(WIN, F32),
     "rds": _s(E, I32), "zs": _s(E, BF),
     "GL": _s(4096, F16), "GX": _s(4096, BF), "MX": _s(4096, BF), "MN": _s(4096, BF),
-    "D": _s(4096, F16), "AB": _s([64, 64], BF), "GE": _s([64, 64], BF), "KS": _s(E, I32), "YS": _s(E, F32), "Y4": _s(1024, F16),
+    "D": _s(4096, F16), "AB": _s([64, 64], BF), "GE": _s([64, 64], BF), "KS": _s(E, I32), "YS": _s(E, I32), "G": _s(E, F32), "KB": _s(2 * E, BF), "Y4": _s(1024, F16),
     "QM": _s(2048, BF), "X0": _s(512, BF),
     "E1": _s([16, 272], BF), "E2": _s([16, 272], BF),
     "Ro": _s(E, F16), "Ru": _s(E, U16), "Lo": _s(E, F16), "Lu": _s(E, U16),
     "OD": _s(E, BF), "NE": _s(E, BF), "pl": _s(16, U16), "Rp": _s(E, F32), "Rq": _s(E, U16),
-    "FR": _s(E, BF), "SU": _s(512, F32), "N2": _s(E, BF), "OG": _s(E, BF), "OR": _s(E, BF), "U": _s(E, BF),
-    "DL": _s(E, F32), "JG": _s(E, BF), "C1": _s(E, F32), "C2": _s(E, F32), "CS": _s([16, 16], BF),
-    "GK": _s([16, 16], F32), "KY": _s(E, F32), "SB": _s(512, F16), "TB": _s(2 * E, F16),
-    "EV": _s(E, BF), "MM": _s(E, F32), "LW": _s(E, BF), "LN": _s(2 * E, BF), "SG": _s(512, BF),
+    "FR": _s(E, BF), "SU": _s(512, F32), "N2": _s(E, BF), "OG": _s(E, BF), "OR": _s(E, BF), "Os": _s(E, BF), "U": _s(E, BF),
+    "DL": _s(E, F32), "JG": _s(E, BF), "C1": _s(E, F32), "C2": _s(E, F32), "CS": _s(E, BF),
+    "GK": _s(E, F32), "KY": _s(E, F32), "SB": _s(512, F16), "TB": _s(2 * E, F16),
+    "EV": _s(E, BF), "MM": _s(E, F32), "LW": _s(E, BF), "LN": _s(E, BF), "SG": _s(512, BF),
     "PT": _s(E, F32), "SX": _s(E, F32), "RS": _s(E, F32), "rr": _s(E, F32), "zr": _s(E, BF),
     "sf": _s(256, F32), "si": _s(128, I32), "su": _s(128, U16),
     "Ys": _s([RO, E], BF), "Yr": _s([RO, E], BF), "Ns": _s([RO, 288], U16), "Nr": _s([RO, 272], U16),
@@ -78,25 +96,46 @@ SCRATCH = {
     "COL": _s(E, F32), "XK": _s(272, BF), "IO": _s(E, F32), "IK": _s(E, BF), "pi": _s(16, I32), "pc": _s(16, F32),
     "MK": _s(80, F32), "AD": _s(272, BF), "OH": _s([16, 128], BF), "DG": _s(2048, BF),
     "MB": _s(128 * 18, BF), "MF": _s(128 * 4, F32), "RS0": _s(1024, BF), "RS1": _s(1024, BF),
-    "KC": _s(E, BF), "C21": _s(E, BF), "C16": _s([16, 16], BF), "ZE": _s(512, BF), "ZC": _s(E, BF), "TH": _s(E, BF),
-    "CT": _s(E, F32), "TT": _s(5 * 64, F32), "TS": _s(1024, F32), "J": _s(16, BF), "cT": _s(80, F32),
+    "KC": _s([16, 16], BF), "C21": _s([16, 16], BF), "C16": _s([16, 16], BF), "ZE": _s(512, BF), "ZC": _s(E, BF), "TH": _s(E, BF),
+    "CT": _s(E, F32), "TT": _s(5 * 64, F32), "TS": _s(1024, F32), "J": _s(W, BF), "cT": _s(80, F32),
 }
 for _b in range(8):
     SCRATCH["B%d" % _b] = ("psum", [128, 32, 16] if _b in (5, 6) else [128, 512], F32)
 MSG = ["y", "w", "n"]
-SEMAPHORES = (["v", "a", "p", "c", "sent", "left", "gone", "r_rd", "r_z", "r_x", "r_ro", "r_zo"]
+SEMAPHORES = (["v", "a", "p", "c", "sent", "left", "gone", "h0", "h1", "h2", "h3", "r_o", "r_rd", "r_z", "r_x", "r_ro", "r_zo"]
               + ["r_%s%d" % (m, t) for m in MSG for t in range(RO)] + ["d%d" % k for k in range(16)])
 
 
 def rank_program(g, core, T, topo):
     rank = T.rank_of(core)
-    if rank is None:
-        return
     N = len(T.cores)
+    cuts = CFG["cuts"]
+    pieces = list(zip(cuts, cuts[1:]))
+
+    def helper(r, n):
+        me, to = T.cores[r], T.cores[(r - 1) % N]
+        return [c for c in topo.cores_of(me) if c not in T.cores and topo.die(c) != topo.die(me) and topo.may_write(c, to)][0]
+
+    def spare(r, n):
+        me = T.cores[r]
+        return topo.mask(me, helper(r, n)) & topo.mask(me, T.cores[(r - 1) % N])
+
+    if rank is None:
+        for r in range(N):
+            for n in CFG["via"]:
+                if helper(r, n) == core:
+                    to = T.cores[(r - 1) % N]
+                    rid, pid, _ = topo.addr(to)
+                    lo, hi = pieces[n]
+                    g.wait_ge(T.sem["h%d" % n], spare(r, n).bit_count())
+                    g.remote_dma(T.XR[:, lo:hi], T.XO[:, lo:hi], T.sem.r_x, T.sem.sent, pid, rid, topo.mask(core, to))
+                    if n == CFG["via"][-1]:
+                        g.wait_ge(T.sem.sent, len(CFG["via"]) * len(topo.engines(core, to)))
+        return
     nxt, prv = T.cores[(rank + 1) % N], T.cores[(rank - 1) % N]
     Q = {"v": g.vector, "a": g.scalar, "p": g.tensor, "c": g, "s": g.sync}
     ops = []
-    ndma, queued = [0], [0]
+    ndma, queued = [0], [0, 0]
     line = [None]
     now = [-1]
     later = [0]
@@ -224,15 +263,18 @@ def rank_program(g, core, T, topo):
 
     def send(dst, out, in_, sem):
         rid, pid, _ = topo.addr(dst)
-        loc = "left" if sem == "r_x" else "gone" if sem == "r_rd" else "sent"
-        out_cnt[loc] += len(topo.engines(core, dst))
-        op("c", lambda: g.remote_dma(out[0], in_[0], T.sem[sem], T.sem[loc], pid, rid, topo.mask(core, dst)), [], [in_],
-           remote=loc, cost=ISSUE + (FIRST if sum(out_cnt.values()) == len(topo.engines(core, dst)) else 0), msg=sem,
-           lat=FLIGHT + (nbytes(in_, in_) + (queued[0] if now[0] < 0 else 0)) / LINK)
-        queued[0] += nbytes(in_, in_) * 0.8
+        hop = sem[0] == "h"
+        loc = "left" if sem == "r_x" or hop else "gone" if sem == "r_rd" else "sent"
+        mask = spare(rank, int(sem[1])) if hop else topo.mask(core, dst)
+        out_cnt[loc] += mask.bit_count()
+        op("c", lambda: g.remote_dma(out[0], in_[0], T.sem[sem], T.sem[loc], pid, rid, mask), [], [in_],
+           remote=loc, cost=ISSUE + (FIRST if sum(out_cnt.values()) == mask.bit_count() else 0), msg="r_x" if hop else sem,
+           lat=FLIGHT + (FLIGHT + FIRST if hop else 0) + (nbytes(in_, in_) * (1.4 if hop else 1) + (queued[hop] if now[0] < 0 else 0)) / LINK)
+        queued[hop] += nbytes(in_, in_) * (0.3 if hop else 0.8) * (loc == "left")
 
     def recv(src, bufs, sem):
-        op("x", None, bufs, [], sem=sem, val=len(bufs) * len(topo.engines(src, core)), cost=0, lat=0)
+        srcs = src if isinstance(src, list) else [src] * len(bufs)
+        op("x", None, bufs, [], sem=sem, val=sum(len(topo.engines(s, core)) for s in srcs), cost=0, lat=0)
 
     def gather(eng, out, win, off, bias=None):
         if eng == "a":
@@ -263,11 +305,9 @@ def rank_program(g, core, T, topo):
     Lo = a("Lo")
     H = W // 2
 
-    cuts = CFG["cuts"]
-    pieces = list(zip(cuts, cuts[1:]))
-    dma("a", a("rds"), hbm("rd"))
-    dma("s", a("XO", *pieces[0]), hbm("x0", *pieces[0]))
     dma("a", a("zs"), hbm("z0"))
+    dma("s", a("XO", *pieces[0]), hbm("x0", *pieces[0]))
+    dma("a", a("rds"), hbm("rd"))
     for lo, hi in pieces[1:len(pieces) - CFG["late"]]:
         dma("s", a("XO", lo, hi), hbm("x0", lo, hi))
     for k in range(4):
@@ -283,20 +323,22 @@ def rank_program(g, core, T, topo):
             send(nxt, a("Ru"), a("Rq"), "r_rd")
         if n == CFG["rz"][1]:
             send(nxt, a("XO", W, W + E), a("zs"), "r_z")
-        send(prv, a("XR", lo, hi), a("XO", lo, hi), "r_x")
+        if n == len(pieces) - CFG["late"]:
+            queued[:] = [0, -FIRST * LINK]
+        if n in CFG["via"]:
+            send(helper(rank, n), a("XO", lo, hi), a("XO", lo, hi), "h%d" % n)
+        elif n < len(pieces) - 1:
+            send(prv, a("XR", lo, hi), a("XO", lo, hi), "r_x")
     iota(a("XK"), [[0, 17], [1, 16]])
     iota(a("IO", 0, 64), [[0, 2], [-1, 16], [0, 2]], 15)
     iota(a("IO", 64, 128), [[0, 2], [-1, 16], [-100, 2]], 115)
     iota(a("IO", 128, 192), [[-100, 2], [-1, 16], [0, 2]], 115)
-    iota(a("IO", 192, 256), [[-1, 2], [0, 16], [1, 2]], 1)
-    iota(COM, [[0, 32], [1, 2]])
     iota(a("IK"), [[0, 16], [-2, 16]], 62)
     iota(a("CT"), [[-12, 256]], W)
-    iota(a("J"), [[1, 16]])
     iota(a("pi", 8, 11), [[1, 3]], 0, 1, False)
     recv(prv, [a("Ru")], "r_rd")
     recv(prv, [a("XO", W, W + E)], "r_z")
-    recv(nxt, [a("XR", lo, hi) for lo, hi in pieces], "r_x")
+    recv([helper((rank + 1) % N, n) if n in CFG["via"] else nxt for n in range(len(pieces))], [a("XR", lo, hi) for lo, hi in pieces], "r_x")
 
     ms(a("ZE"), 0.0)
     ts(a("pi", 1, 2), a("pi", 0, 1), 15, Op.bitwise_and)
@@ -310,7 +352,10 @@ def rank_program(g, core, T, topo):
     act(TMPf, c128, AF.Abs, bias=nb)
     ts(BLK, TMPf, 8.0, Op.is_lt)
     for k in range(16):
-        act(m("DG", k), ID, scale=a("MK", k, k + 1))
+        if k % 2:
+            ts(m("DG", k), ID, a("MK", k, k + 1), Op.mult)
+        else:
+            act(m("DG", k), ID, scale=a("MK", k, k + 1))
     act(IDf, ID)
     act(BLKf, BLK)
     for mat, src, c in ((IB, ID, 4096.0), (NIB, ID, -4096.0), (NBLK, BLK, -4096.0), (HID, ID, 0.5), (I1536, ID, -1536.0),
@@ -345,13 +390,17 @@ def rank_program(g, core, T, topo):
     act(b12, iT, scale=12.0)
     act(a("cT", 48, 64), iT, bias=DUMP - OFF)
     act(a("cT", 64, 80), iT, bias=DUMP - OFF)
-    act(kq, a("ZE", 0, 16), bias=512.0)
+    tt(a("G"), a("COL"), a("XK", 0, E), Op.subtract)
+    act(a("KB", 0, E), a("G"), scale=128.0)
+    act(a("KB", E, 2 * E), a("G"), scale=128.0, bias=512.0)
     act(half, a("MK", 0, 1), scale=0.5)
     act(BC0, BLK, scale=half)
     act(npm, pm, scale=-8192.0)
     act(a("AD"), a("XK", 0, 272), AF.Abs, scale=8192.0, bias=npm)
     act(a("OD"), a("AD", 0, E), scale=-1.0, bias=-0.25)
-    cp(q0, b12)
+    now[0] = 0
+    tt(a("G"), a("KB", E, 2 * E), a("AD", 0, E), Op.subtract)
+    now[0] = -1
     act(a("C21"), a("ZE", 0, E), bias=2 * BIG)
     act(a("C16"), a("ZE", 0, E), bias=16.0)
     for c in range(4):
@@ -361,13 +410,14 @@ def rank_program(g, core, T, topo):
     act(a("KC"), a("IK"), bias=0.5)
     act(a("SG", 0, 256), a("RS0", 0, 256), scale=0.5)
     act(a("LW"), a("RS1", 0, 256), scale=-LOSE / 256)
-    scan(a("TH"), a("SG", 0, 256), a("LW"), Op.mult, Op.add)
     ts(a("TT", 0, 192), a("IO", 0, 192), pm, Op.is_equal)
-    act(TNL, a("IO", 192, 256), AF.Sign)
+    now[0] = 0
+    scan(a("TH"), a("SG", 0, 256), a("LW"), Op.mult, Op.add)
     tt(a("MK", 16, 32), a("TH", 0, 16), a("MK", 0, 16), Op.mult)
     op("a", lambda: g.scalar.activation(T.MK[:, 64:80], T.MK[:, 16:32], AF.Identity, scale=-0.5, accum_out=p2[0]),
        [a("MK", 64, 80), p2], [a("MK", 16, 32)])
     act(WD, BLK, scale=p2)
+    now[0] = -1
     act(a("MK", 32, 48), a("MK", 0, 16), bias=-0.5)
     ts(a("pi", 12, 15), a("pi", 8, 11), 15, Op.bitwise_and)
     act(a("pc", 8, 11), a("pi", 12, 15), scale=64.0, bias=-OFF)
@@ -376,6 +426,15 @@ def rank_program(g, core, T, topo):
         act(a("TS", 64 * k, 64 * k + 64), TOS, AF.Sign, bias=a("MK", 32 + k, 33 + k))
     now[0] = -1
     ts(a("Ro"), a("Ru"), -OFF, Op.add)
+    now[0] = 0
+    mms(a("B7", 0, E), [(BLK, a("XO", 0, W, 12))])
+    act(a("Os"), a("B7", 0, E), AF.Relu, bias=1.0, scale=-1.0)
+    send(prv, a("OR"), a("Os"), "r_o")
+    now[0] = -1
+    send(prv, a("XR", *pieces[-1]), a("XO", *pieces[-1]), "r_x")
+    iota(a("J"), [[0, E], [1, 12]])
+    ops[-1]["behind"] = len(ops) - 2
+    recv(nxt, [a("OR")], "r_o")
 
     def to_list(out, mats, src, n, st=True, sp=True):
         mms(out, [(m(mats, k), a(src[0], src[1] + k, src[1] + n, 16)) for k in range(16)], st, sp)
@@ -416,11 +475,32 @@ def rank_program(g, core, T, topo):
         locks = a("PI") if t == 0 else PF
 
         def lk_open(h):
+            if CFG["whole"]:
+                if h:
+                    mms(a("B1"), [(ID, a("ZE"))], True, False)
+                    mms(a("B1", 0, E), [(ID, a("Ro"))], False, False)
+                    mms(a("B1", E, 2 * E), [(ID, a("Ro"))], False, False)
+                    mms(a("B2", 0, E), [(ID, a("ZC"))], True, False)
+                return
             bs = "B%d" % (2 * h + 1)
             mms(a(bs, 0, 384), [(ID, a("ZE", 0, 384))], True, False)
             mms(a(bs, 0, 128), [(ID, a("Ro", 128 * h, 128 * h + 128))], False, False)
             mms(a(bs, 128, 256), [(ID, a("Ro", 128 * h, 128 * h + 128))], False, False)
             mms(a(bs, 256, 384), [(ID, a("ZC", 128 * h, 128 * h + 128))], False, False)
+
+        def lk_whole():
+            fr = a("FR")
+            act(fr, a("B0", 0, E), AF.Relu, bias=-1535.0)
+            mms(a("B1", 0, E), [(IB, fr), (NTRI, fr)], False, False)
+            mms(a("B1", E, 2 * E), [(IB, fr)], False)
+            mms(a("B2", 0, E), [(NBLK, fr)], False)
+            act(Lo, a("B0", 0, E))
+            act(a("SU", 0, E), a("B1", 0, E), AF.Relu, bias=OFF - 4096.0)
+            act(a("N2"), a("B2", 0, E), AF.Relu)
+            act(a("SU", E, 2 * E), a("B1", E, 2 * E), AF.Relu, bias=OFF - 4096.0)
+            mms(a("B3", 0, E), [(NIB, fr), (BLKf, a("SU", 0, E)), (BLK, a("N2"))])
+            tt(a("Rp"), a("B3", 0, E), a("SU", E, 2 * E), Op.max)
+            cp(a("Rq"), a("Rp"))
 
         def lk_gather(eng, lo, hi):
             line[0] = "gathers"
@@ -428,7 +508,9 @@ def rank_program(g, core, T, topo):
             line[0] = None
 
         def lk_pick(c):
-            if CFG["pk"] == 64:
+            if CFG["whole"]:
+                mms(a("B0", 64 * c, 64 * c + 64), [(m("DG", k), a("GL", 1024 * c + k, 1024 * c + 1024, 16)) for k in range(16)])
+            elif CFG["pk"] == 64:
                 mms(a("B%d" % (c // 2 * 2), 64 * (c % 2), 64 * (c % 2) + 64),
                     [(m("DG", k), a("GL", 1024 * c + k, 1024 * c + 1024, 16)) for k in range(16)])
             elif c % 2:
@@ -479,23 +561,23 @@ def rank_program(g, core, T, topo):
             mms(a("B3", 0, 256), [(BLK, a("OG"))])
 
         def y_val(l0, l1):
-            mx, mn = a("MX", 16 * l0 + 15, 16 * l1, 16), a("MN", 16 * l0 + 15, 16 * l1, 16)
-            mms(a("B1", l0, l1), [(BC0, mx), (BC0, mn)], False, l1 == E)
-            mms(a("B5", l0, l1), [(HID, mx), (HID, mn)])
+            for lo, hi in ((l0, CFG["sc"][-1][0]), CFG["sc"][-1]):
+                mx, mn = a("MX", 16 * lo + 15, 16 * hi, 16), a("MN", 16 * lo + 15, 16 * hi, 16)
+                mms(a("B1", lo, hi), [(BC0, mx), (BC0, mn)], False, hi == E)
+                mms(a("B5", lo, hi), [(HID, mx), (HID, mn)])
             for r in range(4):
-                take("Y%d" % r, a("Y4", 4 * l0 + r, 4 * l1, 4), a("B5", l0, l1), 1023.75)
+                if r in CFG["ypool"]:
+                    gcopy(a("Y4", 4 * l0 + r, 4 * l1, 4), a("Y4", 4 * l0, 4 * l1, 4), l1 - l0)
+                else:
+                    take("Y%d" % r, a("Y4", 4 * l0 + r, 4 * l1, 4), a("B5", l0, l1), 1023.75)
                 if r == 0:
                     take("Y", a3("Ys", t, t + 1, l0, l1), a("Y4", 4 * l0, 4 * l1, 4), -1024.0)
 
         def primaries():
-            scan(a("YS"), a("RS0", 0, E), a("B1", 0, E), Op.mult, Op.max)
-            tt(yi, a("YS", 15, E, 16), kq, Op.max)
-            ts(y7, yi, 7, Op.bitwise_and)
+            scan(a("YS"), a("G"), a("B1", 0, E), Op.max, Op.max)
+            ts(y7, a("YS", 15, E, 16), 7, Op.bitwise_and)
             tt(qf, y7, b12, Op.add)
-            if not last:
-                act(oT, y7)
-                act(kq, y7, bias=512.0)
-            cp(a("qs", 32 * t, 32 * t + (16 if last else 32)), a("sf", 0, 16 if last else 32))
+            cp(a("qs", 32 * t, 32 * t + 16), qf)
             cp(ind(XR, a("qs", 32 * t, 32 * t + 16)), Y)
 
         lk_open(0)
@@ -503,12 +585,14 @@ def rank_program(g, core, T, topo):
         if t > 0:
             own_update(t - 1)
         else:
-            cp(a("PF", 0, 1536), a("PI", 0, 1536))
+            for k in range(4):
+                cp(a("PF", 768 * k, 768 * k + 768), a("PI", 768 * k, 768 * k + 768))
         steps = {"L": lk_gather, "X": cells, "P": lk_pick, "F": lk_free, "S": lk_first, "R": lk_list}
         for st in CFG["s1_0" if t == 0 else "s1"]:
-            steps[st[0]](*st[1:])
-        if t == 0:
-            cp(a("PF", 1536, W), a("PI", 1536, W))
+            if not CFG["whole"] or st[0] in "LXP":
+                steps[st[0]](*st[1:])
+            elif st == ("F", 1):
+                lk_whole()
         turn_locks()
         if t > 0:
             recv(nxt, [a3("Nr", t - 1, t, 0, 272)], "r_n%d" % (t - 1))
@@ -517,9 +601,10 @@ def rank_program(g, core, T, topo):
         for lo, hi in CFG["sc"]:
             scans(lo, hi)
         ts(a("Lu"), a("B4", 0, 256), OFF, Op.add)
-        orphans()
-        act(a("OR"), a("B3", 0, 256), AF.Relu, bias=1.0, scale=-1.0)
-        mms(a("B1", 0, E), [(ID, a("OD", 0, E)), (I1024, a("OR"))], True, False)
+        if t > 0:
+            orphans()
+            act(a("OR"), a("B3", 0, 256), AF.Relu, bias=1.0, scale=-1.0)
+        mms(a("B1", 0, E), [(ID, a("OD", 0, E)), (ID, a("KB", 0, E)), (I1024, a("OR"))], True, False)
         for lo, hi in CFG["yp"]:
             y_val(lo, hi)
         primaries()
@@ -539,17 +624,14 @@ def rank_program(g, core, T, topo):
         mms(a("B0", 256, 512), [(ID, Lo), (NID, a("Ro")), (I1536, a("SG", 256, 512)), (P1536, a("SG", 0, 256))])
         take("DL", a("DL"), a("B0", 256, 512))
 
-        parts = (("B5", 0, "B6", 0, 0, CFG["kcut"]), ("B5", 16, "B6", 16, CFG["kcut"], 16))
-        if CFG["kcut"] < 16:
-            parts = (("B5", 0, "B6", 0, 0, CFG["kcut"]), ("B2", 0, "B3", 0, CFG["kcut"], 16))
-        parts = [p for p in parts if p[4] < p[5]]
-        for bd, _, bn, _, k0, k1 in parts:
-            mms(a(bd, 0, 256), [(ID, a("KC")), (ID, a("C21"))], True, False)
-            mms(a(bn, 0, 256), [(ID, a("C16"))], True, False)
+        mms(a("B5", 0, E), [(ID, a("KC")), (ID, a("C21"))], True, False)
+        mms(a("B6", 0, E), [(ID, a("C16"))], True, False)
         if not last:
-            act(a("JG"), ind(a("J"), a("qs", 32 * t + 16, 32 * t + 32)))
+            act(a("JG"), ind(a("J"), ql))
             mms(a("B1", 256, 512), [(IDf, a("CT")), (NID, a("AD", t, t + E)), (NID, a("JG"))])
             take("C2", a("C2"), a("B1", 256, 512), 0.0, True)
+            mms(a("B2", E, 2 * E), [(ID, a("KB", E, 2 * E)), (NID, a("AD", 0, E)), (ID, a("JG"))])
+            act(a("G"), a("B2", E, 2 * E))
         for c in range(4):
             line[0] = "step 3"
             for lo, hi in CFG["dq"][c]:
@@ -562,19 +644,15 @@ def rank_program(g, core, T, topo):
                     act(ge, dd, AF.Sign, bias=1024.5)
                 act(v("AB", S(16 * c + lo, 16 * c + hi), ALL), dd, AF.Abs, bias=65536.0, scale=64.0)
             line[0] = None
-            bd, _, bn, _, k0, k1 = [p for p in parts if p[4] <= 4 * c < p[5]][0]
-            for src, bank in (("GE", bn), ("AB", bd)):
+            for src, bank in (("GE", "B6"), ("AB", "B5")):
                 mms(v(bank, S(0, 16), S(4 * c, 4 * c + 4)),
-                    [(m("OH", s), v(src, S(16 * c, 16 * c + 16), S(4 * s, 4 * s + 4))) for s in range(16)], False,
-                    4 * c + 4 == k1 and src == "GE")
-            if 4 * c + 4 == k1:
-                n, d, ks = v(bn, S(0, 16), S(k0, k1)), v(bd, S(0, 16), S(k0, k1)), S(k0, k1)
-                act(v("CS", ALL, ks), n, AF.Sign, bias=-17.0)
-                act(v("GK", ALL, ks), n, AF.Abs, bias=-6.5 * BIG, scale=BIG / 2)
-                mms(d, [(HID, v("CS", ALL, ks))], False)
-                tt(a("KY"), d, v("GK", ALL, ks), Op.min)
-        scan(a("KS"), a("RS0", 0, 256), a("KY"), Op.mult, Op.max)
-        ts(cd, a("KS", 15, 256, 16), 63, Op.bitwise_and)
+                    [(m("OH", s), v(src, S(16 * c, 16 * c + 16), S(4 * s, 4 * s + 4))) for s in range(16)], False, c == 3 and src == "GE")
+        act(a("CS"), a("B6", 0, E), AF.Sign, bias=-17.0)
+        act(a("GK"), a("B6", 0, E), AF.Abs, bias=-6.5 * BIG, scale=BIG / 2)
+        mms(a("B5", 0, E), [(HID, a("CS"))], False)
+        tt(a("KY"), a("B5", 0, E), a("GK"), Op.min)
+        scan(a("KS"), a("RS0", 0, E), a("KY"), Op.mult, Op.max)
+        ts(cd, a("KS", 15, E, 16), 63, Op.bitwise_and)
         cp(cu, cd)
         line[0] = "picks"
         for hh in (0, 256) if last else CFG["picks"]:
@@ -587,17 +665,19 @@ def rank_program(g, core, T, topo):
                 mms(a(bank, 256, 512), [(BLK, a("SB", hh, hh + 256))])
                 to_list(a("B4", 288, 304), "OH", ("SB", hh), 256)
             else:
-                act(a("NE"), ind(TNL, cu), scale=256.0)
-                mms(a(bank, 256, 512), [(BLK, a("NE")), (BLK, a("SB", hh, hh + 256))])
-                to_list(a("B6", 288, 304), "OH", ("NE", 0), 256, True, False)
-                to_list(a("B6", 288, 304), "OH", ("SB", 0), 256, False)
+                ts(c33, cd, 33, Op.bitwise_and)
+                act(nl, c33, AF.Abs, bias=-32.0 * 4096, scale=4096.0)
+                mms(a(bank, 256, 512), [(BLK, a("SB", hh, hh + 256))])
+                to_list(a("B6", 288, 304), "OH", ("SB", 0), 256, True, False)
+                mms(a("B6", 288, 304), [(IDf, nl)], False)
         line[0] = None
+        act(ef, c33, AF.Abs, bias=-33.0 * 8192, scale=8192.0)
 
         def wipes():
             act(a("TB", E, 2 * E), a("B3", 256, 512))
             act(wT, a("B6", 288, 304))
             act(a("sf", 96, 112), a("B6", 288, 304), bias=-4096.0)
-            pairs("E1", lambda lo: a("TB", E + lo, 2 * E), 160, "B1", CFG["eqa1"])
+            pairs("E1", lambda lo: a("TB", E + lo, 2 * E), 160, "B1", CFG["eqa3" if last else "eqa1"])
             act(a("LW"), a("B1", 0, 256), AF.Relu)
             mms(a("B5", 0, 16), [(IDf, wT)], True, False)
             to_list(a("B5", 0, 16), "OH", ("LW", 0), 256, False)
@@ -610,18 +690,17 @@ def rank_program(g, core, T, topo):
             act(a("TB", 0, E), a("B0", 256, 512))
             act(a("sf", 112, 128), a("B4", 288, 304))
             pairs("E2", lambda lo: a("TB", lo, E), 112, "B2", CFG["eqa2"])
-            act(a("LN", 0, E), ind(COM, cu), scale=-4352.0, bias=4096.0)
-            act(a("LN", E, 2 * E), a("B2", 0, 256), AF.Relu)
-            mms(a("B4", 320, 352), [(ID, a("ZE", 0, 32))], True, False)
-            mms(a("B4", 336, 352), [(IDf, a("sf", 112, 128))], False, False)
-            to_list(a("B4", 320, 352), "OH", ("LN", 0), 512, False)
+            act(a("LN"), a("B2", 0, 256), AF.Relu)
+            mms(a("B4", 320, 336), [(I1536, a("RS0", 1, 16 * 16, 16)), (IDf, ef)])
+            mms(a("B4", 336, 352), [(IDf, a("sf", 112, 128))], True, False)
+            to_list(a("B4", 336, 352), "OH", ("LN", 0), 256, False)
         for hh in (0, 256) if last else CFG["picks"]:
             (winners if hh else wipes)()
         tt(a("MM"), ind(TOC, cu), a("DL"), Op.mult)
         mms(a("B7", 0, 256), [(IDf, a("MM"))], False)
         if not last:
             act(a("sf", 128, 144), cd, bias=a("pc", 8 + t, 9 + t))
-        ts(a("su", 48, 80 if last else 96), a("sf", 96, 128 if last else 144), OFF, Op.add)
+        ts(a("su", 48, 80 if last else 96), a("sf", 96, 128 if last else 144), OFF, Op.add, W - 1.0, Op.min)
         act(a("EV"), ind(XR, el))
         if last:
             act(a("RS"), a("B7", 0, 256), bias=1.0)
@@ -676,6 +755,8 @@ def rank_program(g, core, T, topo):
             if ln in chain:
                 pre.setdefault(chain[ln], False)
             chain[ln] = j
+        if "behind" in o:
+            pre[o["behind"]] = False
         if o.get("remote"):
             sent_as.setdefault(o["msg"], []).append(j)
         o["pre"] = pre

@@ -1,54 +1,15 @@
 import numpy as np
-from concourse.mybir import AluOpType as Op, ActivationFunctionType as AF, AxisListType as AX
+from concourse.mybir import AluOpType as Op, ActivationFunctionType as AF
 
-W, E, RO, WIN, DUMP = 3072, 256, 4, 3584, 3328
+W, E, RO, WIN, ZERO, DUMP = 3072, 256, 4, 3600, 3328, 3344
+AT = {"XR": 16, "XO": 16 + WIN}
 OFF = 1536.0
-BIG = float(2 ** 20)
+GATE = float(2 ** 20)
 LOSE = float(2 ** 28)
 BF, F32, F16, I32, U16 = "bfloat16", "float32", "float16", "int32", "uint16"
 CYC, PE, SEM, GATHER, SCATTER, ISSUE, FLIGHT, START, LINK, HBM = 0.83, 0.42, 100, 1.56, 3.8, 600, 2300, 1800, 55, 220
 CALL, PCALL, FIRST = {"v": 75, "a": 40}, 3, 2000
 PASSES = 6
-CFG = {
-    "dq": (((0, 8), (8, 16)), ((0, 16),), ((0, 16),), ((0, 8), (8, 16))),
-    "kcut": 16, "on_v": ("Y1", "DL"),
-    "gev": ((1, 0), (3, 0), (3, 8)),
-    "eqa2": (10, 11, 12, 13, 14, 15),
-    "eqa1": (10, 11, 12, 13, 14, 15),
-    "picks": (0, 256), "lax": False, "lscan": (0, 256), "zscan": (0, 256), "pk": 64, "kq": ((0, 1), (1, 2), (2, 3), (3, 4)),
-    "pairs": ("l", "w"), "pairline": None,
-    "s1line": None, "transitive": True,
-    "s1_0": (("L", "a", 0, 64), ("L", "v", 64, 128), ("P", 0), ("P", 1), ("L", "a", 128, 160), ("L", "v", 192, 256), ("F", 0),
-             ("L", "a", 160, 192), ("P", 2), ("P", 3), ("S", 0), ("R", 0), ("F", 1), ("X", "a", 0, 32), ("S", 1), ("R", 1), ("X", "v", 32, 64),
-             ("X", "a", 64, 128), ("X", "a", 128, 192), ("X", "a", 192, 224), ("X", "a", 224, 256)),
-    "s1": (("L", "a", 0, 64), ("L", "v", 64, 96), ("L", "a", 96, 128), ("P", 0), ("P", 1), ("L", "a", 128, 160), ("F", 0),
-           ("L", "a", 160, 192), ("P", 2), ("S", 0), ("L", "v", 224, 256), ("L", "a", 192, 224), ("R", 0), ("P", 3), ("F", 1),
-           ("X", "a", 0, 32), ("S", 1), ("R", 1), ("X", "a", 32, 64), ("X", "a", 64, 128), ("X", "v", 128, 160),
-           ("X", "a", 160, 192), ("X", "a", 192, 224), ("X", "a", 224, 256)),
-    "sc": ((0, 64), (64, 128), (128, 192), (192, 224), (224, 256)),
-    "yp": ((0, 256),), "cuts": (0, 768, 1792, W), "rz": (0, 1), "pl": True, "late": 0, "ypool": (), "upper": True, "eqa3": tuple(range(10, 16)), "via": (), "whole": False,
-    "gxv": 32,
-}
-ORDER = {"v": "GL:1024< GL:3072< XO:0<ZE SX Ns*<SX Rp:0< XO:0<Ns Rq:0< Rp:128 XR:0<ZE Rq:128 MN:1024< MX:1024< XR:0<Nr MX:0< MN:0< MX:2048< MX:3072< MN:3072< MN:2048< MX:3584< MN:3584< Lu YS si:0< si:16< sf:0< qs XR:0<Ys D:0< D:512< D:1024< D:3072< D:2560< D:2048< GE:2560< D:3584< GE:3072< GE:3584< XO:0<Yr KY KS si:32 su:32 SB:256 SB:0 MM E2 E1 su:48 sf:208<B4 sf:208<sf Ns*<sf PT Ru PF:0<PT sf:192 ws", "a": "GL:0< GL:2048< FR:0< Lo:0< SU:0< GL:3584< N2:0< FR:128 Lo:128 SU:256 N2:128 GX:1024< GX:0< GX:2048< GX:3072< OG GX:3584< OR Y4:0< Y4:1< Ys sf:16<si U Y4:2< sf:48<si Y4:3< SG JG DL AB:0< GE:0< GE:512< AB:512< C2 AB:1024< GE:1024< AB:2560< GE:2048< AB:2048< AB:3072< AB:3584< CS GK LN:0< NE TB:0< sf:112 sf:128 E2*<TB TB:256 sf:160 E2*<E2 sf:96 Ro LN:256 E1*<TB C1 E1*<E1 LW EV", "v0": "QM PF:0<PI OH GL:1024< GL:3072< PF:1536<PI Rp:0< Rq:0< Rp:128 GX:0< Rq:128 MX:1024< Lu MN:1024< MX:0< MN:0< MX:2048< MX:3072< MN:2048< MN:3072< MX:3584< MN:3584< YS si:0< si:16< sf:0< qs XR:0<Ys D:0< D:512< D:1024< D:3072< D:3584< D:2560< GE:3584< D:2048< GE:2560< XO:0<Yr GE:3072< KY KS si:32 su:32 SB:256 SB:0 MM E2 E1 su:48 sf:208<B4 sf:208<sf Ns*<sf PT PF:0<PT Ru sf:192 ws", "a0": "GL:0< GL:2048< FR:0< SU:0< Lo:0< N2:0< FR:128 Lo:128 SU:256 N2:128 GX:1024< GX:512< GX:2048< GX:3072< OG GX:3584< OR Y4:0< Y4:1< Ys sf:16<si Y4:2< sf:48<si Y4:3< U JG SG AB:0< GE:0< DL C2 GE:512< AB:512< GE:1024< AB:3072< AB:1024< AB:2560< GE:2048< AB:2048< AB:3584< CS GK TS LN:0< NE TB:0< sf:128 sf:112 TB:256 E2*<TB sf:160 E2*<E2 sf:96 Ro LN:256 E1*<TB C1 E1*<E1 LW EV", "v3": "GL:1024< GL:3072< XO:0<ZE SX Ns*<SX Rp:0< XO:0<Ns Rq:0< Rp:128 Rq:128 XR:0<ZE MN:1024< MX:1024< XR:0<Nr MX:0< MN:0< MX:3072< MN:3072< MX:2048< MN:2048< MX:3584< MN:3584< Lu YS si:0< si:16< sf:0< qs XR:0<Ys D:0< D:512< D:1024< D:3072< D:2560< D:2048< GE:2560< D:3584< GE:3072< GE:3584< XO:0<Yr KY KS si:32 su:32 SB:0 SB:256 MM E1 su:48 sf:192 ws E2 sf:208<B4 sf:208<sf Ns*<sf", "a3": "GL:0< GL:2048< FR:0< Lo:0< SU:0< GL:3584< N2:0< FR:128 Lo:128 SU:256 N2:128 GX:1024< GX:0< GX:3072< GX:2048< OG GX:3584< OR Y4:0< Y4:1< Ys U Y4:2< Y4:3< SG AB:0< GE:0< GE:512< AB:512< DL AB:1024< GE:1024< AB:2560< GE:2048< AB:2048< AB:3072< AB:3584< CS GK NE TB:256 LN:0< sf:160 E1*<TB sf:96 TB:0< E1*<E1 LW sf:112 E2*<TB RS EV E2*<E2 LN:256"}
-
-
-ORDER = {"v": "GL:1024< GL:3072< XO:0<ZE SX Ns*<SX Rp:0< XO:0<Ns Rq:0< XR:0<ZE Rp:128 Rq:128 MX:1024< MN:1024< MX:0< MN:0< XR:0<Nr MX:2048< MN:3072< MX:3072< MN:3584< MX:3584< MN:2048< Lu YS si:0< si:16< sf:0< qs XR:0<Ys D:0< D:512< D:1024< D:2560< D:2048< D:3072< D:3584< GE:2560< GE:3072< GE:3584< KY KS si:32 su:32 SB:256 SB:0 E2 E1 su:48 MM sf:208<B4 sf:208<sf PT pl Ns*<sf PF:0<PT Ru sf:192 ws XO:0<Yr", "a": "GL:0< GL:2048< FR:0< Lo:0< GL:3584< SU:0< N2:0< FR:128 Lo:128 SU:256 N2:128 GX:1024< GX:0< GX:2048< GX:3072< GX:3584< OG OR Y4:0< Y4:1< Ys sf:16<si Y4:2< U Y4:3< sf:48<si JG SG C2 AB:0< GE:0< DL GE:512< AB:512< GE:1024< AB:2560< AB:1024< AB:2048< GE:2048< AB:3072< AB:3584< CS GK NE LN:0< TB:0< sf:112 E2*<TB TB:256 sf:160 E2*<E2 sf:128 sf:96 LN:256 E1*<TB C1 E1*<E1 Ro LW EV", "v0": "OH QM GL:1024< GL:3072< PF:0<PI Rp:0< Rq:0< GX:0< MX:0< MN:0< Rp:128 Rq:128 PF:1536<PI MX:1024< MN:2048< MX:2048< MN:3584< MN:1024< MX:3584< MX:3072< MN:3072< Lu YS si:0< si:16< sf:0< qs XR:0<Ys D:512< D:0< D:1024< D:2560< D:2048< GE:2560< D:3072< D:3584< GE:3072< GE:3584< KY KS si:32 su:32 SB:256 SB:0 MM E2 E1 Ru su:48 PT sf:208<B4 pl sf:208<sf PF:0<PT sf:192 ws XO:0<Yr Ns*<sf", "a0": "TS GL:0< GL:2048< FR:0< SU:0< Lo:0< N2:0< FR:128 GX:512< SU:256 N2:128 Lo:128 GX:1024< GX:2048< GX:3584< GX:3072< OG OR Y4:0< Y4:1< sf:16<si Ys Y4:2< Y4:3< U JG sf:48<si SG C2 AB:512< GE:512< GE:0< AB:0< AB:1024< GE:1024< AB:2048< AB:2560< GE:2048< AB:3584< AB:3072< CS GK DL sf:128 NE LN:0< TB:0< sf:112 E2*<TB TB:256 sf:160 E2*<E2 Ro sf:96 LN:256 E1*<TB C1 E1*<E1 LW EV", "v3": "GL:1024< GL:3072< XO:0<ZE SX Ns*<SX Rp:0< XO:0<Ns Rq:0< XR:0<ZE Rp:128 MX:1024< Rq:128 MN:1024< MX:0< MN:0< MX:3072< XR:0<Nr MX:2048< MN:3072< MN:2048< MX:3584< MN:3584< Lu YS si:0< si:16< sf:0< qs XR:0<Ys D:0< D:512< D:1024< D:2560< D:2048< D:3072< GE:2560< D:3584< GE:3072< GE:3584< KY KS si:32 su:32 SB:0 MM SB:256 E1 XO:0<Yr su:48 sf:192 ws E2 sf:208<B4 sf:208<sf Ns*<sf", "a3": "GL:0< GL:3584< GL:2048< FR:0< Lo:0< SU:0< N2:0< FR:128 SU:256 Lo:128 N2:128 GX:1024< GX:0< GX:3072< GX:2048< GX:3584< OG OR Y4:0< Y4:1< Y4:2< Ys Y4:3< U SG AB:0< GE:0< GE:512< DL AB:512< GE:1024< AB:1024< AB:2560< GE:2048< AB:2048< AB:3584< AB:3072< CS GK NE TB:256 sf:160 sf:96 sf:112 E1*<TB E1*<E1 LW TB:0< E2*<TB RS E2*<E2 LN:0< LN:256 EV"}
-
-
-_V2 = ("YS si:16< sf:0< qs XR:0<Ys D:0< D:512< D:1024< D:2048< D:2560< D:3072< GE:2560< D:3584< GE:3072< GE:3584< XO:0<Yr "
-       "KY KS si:32 su:32 ")
-_SC = "MN:1024< MX:1024< MN:2048< MX:2048< MX:3072< MN:3072< MX:3840< MN:3840< "
-_V1 = "GL:1024< XR:0<ZE XO:0<ZE SX Ns*<SX XO:0<Ns Rp:0< Rq:0< Rp:128 Rq:128 Lu GX MX:0< MN:0< XR:0<Nr " + _SC
-_V3 = "SB:256 si:64 SB:0 MM E2 su:48 E1 sf:208<B4 PT pl PF:0<PT sf:192 ws Ru sf:208<sf Ns*<sf"
-_A1 = "GL:0< GL:3584< GL:2048< GL:2560< FR:0< GL:3072< Lo:0< SU:0< N2:0< FR:128 Lo:128 SU:256 N2:128 GX:0< GX:1024< GX:2048< GX:3072< OG GX:3840< OR "
-_A2 = ("Y4:0< Ys sf:16<si Y4:1< U Y4:2< sf:48<si Y4:3< SG AB:0< GE:0< GE:512< AB:512< AB:1024< GE:1024< GE:2048< AB:2560< AB:2048< "
-       "AB:3072< AB:3584< CS GK DL JG ")
-_A3 = "C2 G:0<B2 sf:80 sf:128 TB:0< sf:176 sf:112 TB:256 E2*<TB sf:160 sf:96 E2*<E2 C1 LN E1*<TB E1*<E1 LW Ro EV"
-ORDER = {"v": _V1 + _V2 + _V3, "a": _A1 + _A2 + _A3,
-         "v0": "QM OH PF:0<PI PF:768< GL:1024< GL:3072< PF:1536<PI PF:2304< TH MK Rp:0< Rq:0< Lu GX Rp:128 Rq:128 G:0<KB MX:0< MN:0< " + _SC + _V2 + _V3,
-         "a0": "GL:0< GL:2048< FR:0< Lo:0< Os SU:0< N2:0< FR:128 Lo:128 SU:256 N2:128 GX:0< GX:1536< GX:2048< GX:3072< GX:3840< MK MB TS:0< TS:6 TS:1 TS:2 TS:3 TS:4 " + _A2 + "TS " + _A3,
-         "v3": _V1 + _V2 + "SB:0 si:64 SB:256 E1 E2:0< su:48 E2:544< MM sf:192 ws E2 sf:208<B4 sf:208<sf Ns*<sf",
-         "a3": _A1 + _A2 + "sf:80 TB:256 sf:176 sf:160 sf:96 E1*<TB TB:0< E1*<E1 sf:112 LW E2*<TB RS E2*<E2 EV LN"}
 
 
 def _s1(lg, xg):
@@ -62,14 +23,58 @@ def _s1(lg, xg):
     return tuple(o + [("X", e, lo, hi) for e, lo, hi in xg])
 
 
-CFG.update(s1=_s1([("a", 0, 64), ("v", 64, 128), ("a", 128, 160), ("a", 160, 192), ("a", 192, 224), ("a", 224, 256)],
-                  [("a", 0, 64), ("a", 64, 112), ("v", 112, 128), ("a", 128, 192), ("a", 192, 240), ("a", 240, 256)]),
-           s1_0=_s1([("a", 0, 64), ("v", 64, 128), ("a", 128, 192), ("v", 192, 256)],
-                    [("a", 0, 64), ("v", 64, 96), ("a", 96, 128), ("a", 128, 192), ("a", 192, 240), ("a", 240, 256)]),
-           sc=((0, 64), (64, 128), (128, 192), (192, 240), (240, 256)),
-           dq=(((0, 8), (8, 16)), ((0, 16),), ((0, 8), (8, 16)), ((0, 8), (8, 16))),
-           on_v=(), gev=((2, 8), (3, 0), (3, 8)), eqa1=tuple(range(11, 16)), eqa2=tuple(range(9, 16)), picks=(256, 0),
-           cuts=(0, 512, 1472, 2304, W), via=(0, 1), late=3, rz=(1, 0))
+CFG = {
+    "s1": _s1([("a", 0, 64), ("v", 64, 128), ("a", 128, 192), ("a", 192, 224), ("a", 224, 256)],
+              [("a", 0, 32), ("a", 32, 64), ("a", 64, 112), ("v", 112, 128), ("a", 128, 192), ("a", 192, 240), ("a", 240, 256)]),
+    "s1_0": _s1([("a", 0, 64), ("v", 64, 128), ("a", 128, 192), ("v", 192, 256)],
+                [("a", 0, 64), ("v", 64, 96), ("a", 96, 128), ("a", 128, 192), ("a", 192, 240), ("a", 240, 256)]),
+    "sc": ((0, 64), (64, 128), (128, 192), (192, 240), (240, 256)),
+    "parts": (((192, 256, (("v", 192, 224), ("a", 224, 256))), (128, 192, (("a", 128, 192),)),
+               (64, 128, (("v", 64, 80), ("a", 80, 128))), (0, 64, (("a", 32, 64), ("a", 0, 32)))),),
+    "vh": ((0, 256),), "kh": ((0, 256),), "yb": ("B2", "B3", "B0", "B1"),
+    "lq": "sasa", "pfq": "vava", "pfp": ((0, 128), (128, 256)), "xp": ((0, 160), (160, 256)), "erun": 3, "ttcut": {(3, 1): ((12, 14), (14, 16))},
+    "eg": (("v", 0, 32), ("a", 128, 160), ("a", 32, 64), ("a", 160, 192), ("v", 64, 80), ("a", 80, 96), ("a", 192, 224), ("a", 96, 128),
+           ("a", 224, 240), ("a", 240, 256)),
+    "og": "a", "yp": ((0, 256),), "c9": "a", "c5": "v", "wfirst": False,
+    "bk": (("B2", "B2", "B0", "B0"), ("B4", "B1", "B0", "B3")),
+    "eqa1": (11, 12, 13, 14, 15), "eqa2": (10, 11, 12, 13, 14, 15), "eqa3": (10, 11, 12, 13, 14, 15),
+    "cuts": (0, 512, 1472, 2304, W), "via": (0, 1), "late": 3, "rz": (1, 0),
+}
+ORDER = {'v': '-Ns:*<sf GL:1024<PF XR:0<ZE XO:0<ZE SX:0<XO Ns:*<SX XO:0<Ns Rp:0<B1 Rq:0<Rp Lu:0<Lo GX:1792<XO Rp:128<B3 Rq:128<Rp MX:0<RS0 MN:0<RS1 XR:0<Nr MN:1024<RS1 MX:1024<RS0 MN:2048<RS1 MX:2048<RS0 MN:3072<RS1 MX:3072<RS0 MN:3840<RS1 MX:3840<RS0 YS:0<G G:0<YS sf:0<G qs:*<sf XR:0<Ys EG:3072<XR MG:3072<EG MG:3080<EG EG:1024<XR MG:2048<EG MG:2056<EG MG:1024<EG MG:1032<EG MG:512<EG MG:520<EG MG:0<EG MG:8<EG RI:0<B6 FN:0<B6 C5:0<FN XO:0<Yr KS:0<RS0 si:32<KS su:32<si SB:256<TT si:64<si SB:0<TT MM:0<TT E2:0<TB E2:272<TB E2:544<TB E2:816<TB E2:1088<TB E2:1360<TB E2:1632<TB E1:0<TB E2:1904<TB E2:2176<TB E1:272<TB E1:544<TB E1:816<TB E2:2448<TB E1:1088<TB E1:1360<TB E1:1632<TB E1:1904<TB E1:2176<TB su:48<sf E1:2448<TB E1:2720<TB Ru:0<Ro PT:0<PF sf:208<B4 pl:0<sf sf:192<B3 ws:*<sf PF:0<PT sf:208<sf', 'a': 'GL:0<PF GL:2048<PF FR:0<B0 GL:3072<PF GL:3584<PF SU:0<B1 N2:0<B1 Lo:0<B0 FR:128<B2 Lo:128<B2 SU:256<B3 N2:128<B3 GX:0<XO GX:512<XO GX:1024<XO GX:2048<XO GX:3072<XO OG:0<XR GX:3840<XO OR:0<B4 Y16:0<B5 Ys:*<Y16 Yd:0<Y16 JG:0<J U:0<B7 EG:3584<XR EG:2048<XR EG:1280<XR sy:0<B4 EG:512<XR EG:0<XR C2:0<B1 SG:0<B7 RH:0<RI C9:0<FN DL:0<B0 NL:16<si TB:0<B0 NL:0<si sf:112<B4 E2:2720<TB E2:2992<TB E2:2720<E2 TB:256<B3 E2:3264<TB sf:160<B1 E2:2992<E2 E2:3536<TB E1:2992<TB E2:3808<TB E2:3264<E2 E2:3536<E2 E2:3808<E2 E1:2992<E1 E1:3264<TB E1:3536<TB sf:96<B1 E2:4080<TB E1:3264<E1 E1:3536<E1 E2:4080<E2 E1:3808<TB E1:4080<TB E1:3808<E1 E1:4080<E1 sf:128<si Ro:0<B7 LN:0<B6 C1:0<TS LW:0<B5 EV:0<XR', 'p': "B0:0<GL B0:64<GL B2:0<GL B1:0<FR B2:64<GL B1:384<FR B3:0<FR B3:384<FR B4:0<OG B1:0<OD B1:0<MX B1:240<MX B5:0<MX B5:240<MX B7:256<OR B4:256<Yd B2:0<Yd B5:0<KC B7:0<Ro B1:256<CT B5:192<EG B7:256<Lo B3:0<Yd B6:192<MG B5:128<EG B2:0<Yd' B6:128<MG B3:0<Yd' B6:64<MG B6:0<sy B6:0<MG B5:64<EG B5:0<EG B6:0<TH B5:0<RH B0:256<Lo B7:0<Ro' B0:0<SB B4:448<SB B3:256<SB B5:0<TH B1:464<SB B7:0<MM B6:64<E2 B6:16<E2 B6:176<E2 B6:224<E2 B4:320<RS0 B6:112<E2 B5:16<E1 B4:336<sf B6:160<E2 B6:0<E2 B5:192<E1 B5:64<E1 B5:240<E1 B5:112<E1 B3:0<sf B5:160<E1 B5:0<E1 B4:336<LN B3:0<LW +B1:0<ZE +B3:0<ZE"}
+
+
+def _e(n, lo, hi):
+    return "".join("%s:%d< " % (n, 272 * b) for b in range(lo, hi))
+
+
+_SC = "MX:0< Rq:128 MN:0< MX:1024 MN:1024 XR:0<Nr MX:2048 MN:2048 MX:3072 MN:3072 MX:3840 MN:3840 "
+_V1 = "-XO:0<Yr' -Ns*<sf GL:1024 GL:3584 XO:0<ZE SX Ns*<SX XR:0<Ns Rp:0< Rq:0< GX Rp:128 " + _SC
+_V0 = "OH O3 PF:0<PI GL:1024 Ro:0<Ru GL:3072 PF:768 Rp:0< Rq:0< GX PF:1536 Rp:128 " + _SC
+_V2 = ("Lu YS G:0<YS sf:0< qs XR:0<Ys EG:0< EG:1024 MG:0< MG:2048 MG:512 MG:2560 MG:1024 MG:3072 MG:1536 MG:3584 MG:3840 "
+       "RI FN C5 XO:0<Yr KS si:32 su:32 ")
+_V3 = "SB:256 SB:0< MM " + _e("E2", 0, 11) + _e("E1", 0, 4) + "su:48 " + _e("E1", 4, 10) + "sf:208<B4 PT pl Ru PF:0<PT sf:192 sf:208<sf ws PF:0<PT' sf:224"
+_V4 = "SB:0< SB:256 MM " + _e("E1", 0, 10) + _e("E2", 0, 7) + "sf:192 su:48 ws " + _e("E2", 7, 11) + "XO:0<Yr' sf:208<B4 sf:208<sf Ns*<sf"
+_A1 = "GL:0< GL:2048 FR:0< GL:3072 SU:0< Lo:0< FR:128 Lo:128 SU:256 GX:0< GX:1024 GX:2048 GX:3072 OG GX:3840 OR "
+_A0 = "GL:0< GL:2048 FR:0< SU:0< Lo:0< FR:128 Os SU:256 GX:0< Lo:128 GX:1024 GX:2048 GX:3072 OG GX:3840 OR "
+_A2 = "Y16 Ys Yd U JG EG:2048 sy EG:512 EG:2560 EG:1280 EG:3072 EG:1536 EG:3584 EG:3840 SG:0<B7 PF:2304 RH C9 DL C2 "
+_A3 = "sf:128 TB:0< sf:112 TB:256 E2*<TB sf:160 E2*<E2 sf:96 E1*<TB NL:0< LN E1*<E1 C1 Ro LW:0<B5 sf:16< EV"
+_A4 = "TB:256 sf:160 E1*<TB E1*<E1 sf:112 TB:0< LW sf:96 E2*<TB RS E2*<E2 NL LN EV"
+_P0 = "B0:0<GL B0:64<GL B1:0<FR B2:0<GL B2:64<GL B1:384 B7:0<XO B3:0<FR B3:384 B1:0<OD B7:0<Lo B7:64<Lo B7:128<Lo B7:192<Lo B4:0<Os B4:0<OG "
+_P1 = "B0:0<GL B0:64<GL B2:0<GL B1:0<FR B2:64<GL B1:384 B3:0<FR B3:384 B1:0<OD B7:0<Lo B7:64<Lo B7:128<Lo B7:192<Lo B4:0<OG "
+_P2 = ("B1:0<MX B1:0<OR B1:240<MX B5:0<MX B5:240<MX B5:0<KC B7:256<OR B2:0<Yd B4:256 B3:0<Yd B7:0<Ro B7:256<Lo B0:0<Yd B1:0<Yd "
+       "B6:0<sy B6:0<MG B6:1<MG B5:0<EG B6:0<MG' B5:1<EG B6:1<MG' B5:0<EG' B6:0<MG'' B5:1<EG' B6:1<MG'' B5:0<EG'' "
+       "B6:0<MG''' B5:1<EG'' B6:1<MG''' B6:1<MG'''' B5:0<EG''' B5:1<EG''' B5:1<EG'''' B0:256 B5:0<RH B5:0<C5 B5:0<C9 B7:0<Ro' B1:256 ")
+_P3 = ("B6:0<TH B5:0<TH B0:0<SB B4:448 B3:256 B1:464 B7:0<MM B6:16< B6:48 B6:80 B6:192<E2 B6:112 B6:224 B6:144 B6:176 B6:0<E2 B3:0<sf "
+       "B5:16< B4:320 B4:336<sf B4:336<LN B5:48 B5:80 B5:176<E1 B5:208 B5:240<E1 B5:112 B5:144 B5:0<E1 B3:0<LW +B1:0<ZL +B3:0<ZL +B6:0<ZE")
+_P4 = ("B5:0<TH B6:0<TH B3:256 B1:464 B0:0<SB B4:448 B3:0<sf B5:16< B5:48 B5:176<E1 B5:80 B5:208 B5:240<E1 B5:112 B5:144 B5:0<E1 "
+       "B7:0<MM B3:0<LW")
+ORDER = {"v": _V1 + _V2 + _V3, "a": _A1 + _A2 + _A3, "p": _P1 + _P2 + _P3,
+         "v0": _V0 + _V2 + _V3, "a0": _A0 + _A2 + _A3, "p0": _P0 + _P2 + _P3,
+         "v3": _V1 + _V2 + _V4, "a3": _A1 + _A2 + _A4, "p3": _P1 + _P2 + _P4}
+_X = [("a", 0, 32), ("v", 32, 64), ("a", 64, 128), ("a", 128, 192), ("a", 192, 240), ("a", 240, 256)]
+CFG.update(s1=_s1([("a", 0, 64), ("v", 64, 128), ("a", 128, 192), ("a", 192, 224), ("v", 224, 256)], _X),
+           s1_0=_s1([("a", 0, 64), ("v", 64, 128), ("a", 128, 192), ("v", 192, 256)], _X),
+           eqa1=tuple(range(10, 16)), eqa2=tuple(range(11, 16)), eqa3=tuple(range(10, 16)), erun=2, pfp=((0, 160), (160, 256)), pfq="vvva")
 
 
 def _s(n, d):
@@ -77,30 +82,30 @@ def _s(n, d):
 
 
 SCRATCH = {
-    "XO": _s(WIN, BF), "XR": _s(WIN, BF), "PI": _s(W, I32), "PF": _s(WIN, F32),
+    "XX": _s(16 + 2 * WIN, BF), "ml": _s(32, U16), "PI": _s(W, I32), "PF": _s(WIN, F32),
     "rds": _s(E, I32), "zs": _s(E, BF),
     "GL": _s(4096, F16), "GX": _s(4096, BF), "MX": _s(4096, BF), "MN": _s(4096, BF),
-    "D": _s(4096, F16), "AB": _s([64, 64], BF), "GE": _s([64, 64], BF), "KS": _s(E, I32), "YS": _s(E, I32), "G": _s(E, F32), "KB": _s(2 * E, BF), "Y4": _s(1024, F16),
-    "QM": _s(2048, BF), "X0": _s(512, BF),
+    "EG": _s(4096, F16), "MG": _s(4096, F16), "QM": _s(512, BF), "KS": _s(E, I32), "YS": _s(E, I32), "G": _s(E, I32), "KB": _s(E, BF),
+    "Y16": _s(E, F16), "Yd": _s(E, BF), "sy": _s(16, F16), "X0": _s(512, BF),
     "E1": _s([16, 272], BF), "E2": _s([16, 272], BF),
     "Ro": _s(E, F16), "Ru": _s(E, U16), "Lo": _s(E, F16), "Lu": _s(E, U16),
-    "OD": _s(E, BF), "NE": _s(E, BF), "pl": _s(16, U16), "Rp": _s(E, F32), "Rq": _s(E, U16),
-    "FR": _s(E, BF), "SU": _s(512, F32), "N2": _s(E, BF), "OG": _s(E, BF), "OR": _s(E, BF), "Os": _s(E, BF), "U": _s(E, BF),
-    "DL": _s(E, F32), "JG": _s(E, BF), "C1": _s(E, F32), "C2": _s(E, F32), "CS": _s(E, BF),
-    "GK": _s(E, F32), "KY": _s(E, F32), "SB": _s(512, F16), "TB": _s(2 * E, F16),
+    "OD": _s(E, BF), "pl": _s(16, U16), "Rp": _s(E, F32), "Rq": _s(E, U16),
+    "FR": _s(E, BF), "SU": _s(512, F32), "ZL": _s(512, BF), "OG": _s(E, BF), "OR": _s(E, BF), "Os": _s(32, BF), "U": _s(E, BF),
+    "DL": _s(E, F32), "JG": _s(E, BF), "C1": _s(E, F32), "C2": _s(E, F32), "C9": _s(E, BF), "C5": _s(E, BF),
+    "RI": _s(E, I32), "FN": _s(E, BF), "SB": _s(512, F16), "TB": _s(2 * E, F16),
     "EV": _s(E, BF), "MM": _s(E, F32), "LW": _s(E, BF), "LN": _s(E, BF), "SG": _s(512, BF),
-    "PT": _s(E, F32), "SX": _s(E, F32), "RS": _s(E, F32), "rr": _s(E, F32), "zr": _s(E, BF),
+    "PT": _s(E, F32), "SX": _s(E, F32), "RS": _s(E, F16), "rh": _s(E, F16), "rr": _s(E, F32), "zr": _s(E, BF),
     "sf": _s(256, F32), "si": _s(128, I32), "su": _s(128, U16),
-    "Ys": _s([RO, E], BF), "Yr": _s([RO, E], BF), "Ns": _s([RO, 288], U16), "Nr": _s([RO, 272], U16),
+    "Ys": _s(RO * E, BF), "Yr": _s([RO, E], BF), "Ns": _s([RO, 288], U16), "Nr": _s([RO, 272], U16),
     "qs": _s(RO * 32, U16), "qr": _s(RO * 16, U16), "ws": _s(RO * 16, U16), "wr": _s(RO * 16, U16),
     "COL": _s(E, F32), "XK": _s(272, BF), "IO": _s(E, F32), "IK": _s(E, BF), "pi": _s(16, I32), "pc": _s(16, F32),
-    "MK": _s(80, F32), "AD": _s(272, BF), "OH": _s([16, 128], BF), "DG": _s(2048, BF),
+    "MK": _s(80, F32), "AD": _s(272, BF), "OH": _s([16, 128], BF), "RH": _s(E, F16), "NL": _s(32, BF), "O3": _s([16, 128], BF), "DG": _s(2048, BF),
     "MB": _s(128 * 18, BF), "MF": _s(128 * 4, F32), "RS0": _s(1024, BF), "RS1": _s(1024, BF),
-    "KC": _s([16, 16], BF), "C21": _s([16, 16], BF), "C16": _s([16, 16], BF), "ZE": _s(512, BF), "ZC": _s(E, BF), "TH": _s(E, BF),
-    "CT": _s(E, F32), "TT": _s(5 * 64, F32), "TS": _s(1024, F32), "J": _s(W, BF), "cT": _s(80, F32),
+    "KC": _s(E, BF), "C21": _s(E, BF), "ZE": _s(512, BF), "ZC": _s(E, BF), "TH": _s(E, BF),
+    "CT": _s(E, F16), "TT": _s(5 * 64, F32), "TS": _s(1024, F32), "J": _s(W, BF), "cT": _s(80, F32),
 }
 for _b in range(8):
-    SCRATCH["B%d" % _b] = ("psum", [128, 32, 16] if _b in (5, 6) else [128, 512], F32)
+    SCRATCH["B%d" % _b] = ("psum", [128, 512], F32)
 MSG = ["y", "w", "n"]
 SEMAPHORES = (["v", "a", "p", "c", "sent", "left", "gone", "h0", "h1", "h2", "h3", "r_o", "r_rd", "r_z", "r_x", "r_ro", "r_zo"]
               + ["r_%s%d" % (m, t) for m in MSG for t in range(RO)] + ["d%d" % k for k in range(16)])
@@ -128,17 +133,16 @@ def rank_program(g, core, T, topo):
                     rid, pid, _ = topo.addr(to)
                     lo, hi = pieces[n]
                     g.wait_ge(T.sem["h%d" % n], spare(r, n).bit_count())
-                    g.remote_dma(T.XR[:, lo:hi], T.XO[:, lo:hi], T.sem.r_x, T.sem.sent, pid, rid, topo.mask(core, to))
+                    g.remote_dma(T.XX[:, AT["XR"] + lo:AT["XR"] + hi], T.XX[:, AT["XO"] + lo:AT["XO"] + hi], T.sem.r_x, T.sem.sent, pid, rid, topo.mask(core, to))
                     if n == CFG["via"][-1]:
                         g.wait_ge(T.sem.sent, len(CFG["via"]) * len(topo.engines(core, to)))
         return
     nxt, prv = T.cores[(rank + 1) % N], T.cores[(rank - 1) % N]
     Q = {"v": g.vector, "a": g.scalar, "p": g.tensor, "c": g, "s": g.sync}
-    ops = []
+    ops, named = [], set()
     ndma, queued = [0], [0, 0]
-    line = [None]
     now = [-1]
-    later = [0]
+    late = [False]
     out_cnt = {"sent": 0, "left": 0, "gone": 0}
     S = slice
     ALL = slice(None)
@@ -150,7 +154,16 @@ def rank_program(g, core, T, topo):
         mask = int.from_bytes(np.packbits(bits.reshape(-1), bitorder="little").tobytes(), "little")
         return (T[name][(ALL,) + ix], [(name, mask)])
 
+    def label(name, mask):
+        lo = (mask & -mask).bit_length() - 1
+        if name == "XX":
+            name = "XO" if lo >= AT["XO"] else "XR"
+            lo = max(0, lo - AT[name])
+        return name, lo
+
     def a(name, lo=0, hi=None, step=1):
+        if name in AT:
+            return a("XX", AT[name] + lo, AT[name] + (WIN if hi is None else hi), step)
         shape = SCRATCH[name][1]
         if len(shape) > 2:
             n = shape[2]
@@ -177,11 +190,13 @@ def rank_program(g, core, T, topo):
         for i in ins:
             if isinstance(i, tuple):
                 rd += i[1] + (i[2] if len(i) > 2 else [])
-        d = {"eng": eng, "fn": fn, "wr": wr, "rd": rd, "lat": SEM, "line": line[0] and (line[0], eng), "rank": len(ops) + later[0]}
+        d = {"eng": eng, "fn": fn, "wr": wr, "rd": rd, "lat": SEM, "rank": len(ops), "late": late[0]}
         d.update(kw)
         if wr and rd:
-            d["name"] = (now[0], eng, "%s:%d<%s" % (wr[0][0], (wr[0][1] & -wr[0][1]).bit_length() - 1,
-                                                   [i for i in ins if isinstance(i, tuple)][0][1][0][0]))
+            d["name"] = (now[0], eng, "%s:%d<%s" % (label(*wr[0]) + label(*[i for i in ins if isinstance(i, tuple)][0][1][0])[:1]))
+            while d["name"] in named:
+                d["name"] = d["name"][:2] + (d["name"][2] + "'",)
+            named.add(d["name"])
         if "cost" not in d:
             d["cost"] = cost(eng, outs[0], [i for i in ins if isinstance(i, tuple)], kw.get("per", 1.0))
         ops.append(d)
@@ -221,29 +236,23 @@ def rank_program(g, core, T, topo):
     def scan(out, d0, d1, o0, o1):
         op("v", lambda: g.vector.tensor_tensor_scan(out[0], d0[0], d1[0], 0.0, o0, o1), [out], [d0, d1], per=0.5)
 
-    def turn(out, in_):
-        op("v", lambda: g.vector.transpose(out[0], in_[0]), [out], [in_], per=0.5)
-
     def ms(out, c):
         op("v", lambda: g.vector.memset(out[0], c), [out], [], per=0.5)
 
     def act(out, x, f=AF.Identity, bias=0.0, scale=1.0):
         op("a", lambda: g.scalar.activation(out[0], x[0], f, bias=val(bias), scale=val(scale)), [out], [x, bias, scale])
 
-    def take(name, out, x, bias=0.0, relu=False):
-        if name not in CFG["on_v"]:
-            act(out, x, AF.Relu if relu else AF.Identity, bias=bias)
-        elif relu:
-            ts(out, x, bias, Op.add, 0.0, Op.max)
-        else:
-            ts(out, x, bias, Op.add)
-
-    def mm(out, l, r, st, sp):
-        op("p", lambda: g.tensor.matmul(out[0], l[0], r[0], st, sp), [out], [l, r])
+    def mml(trip, st=True, sp=True, alone=0):
+        def fn():
+            n = int(alone) or len(trip)
+            for k, (o, l, r) in enumerate(trip):
+                ins = g.tensor.matmul(o[0], l[0], r[0], st and k % n == 0, sp and k % n == n - 1)
+            return ins
+        op("p", fn, [o for o, l, r in trip], [x for o, l, r in trip for x in (r, l)],
+           cost=sum(cost("p", o, [l, r], 1.0) for o, l, r in trip), adds=not (st or sp or alone))
 
     def mms(out, pairs, st=True, sp=True):
-        for k, (l, r) in enumerate(pairs):
-            mm(out, l, r, st and k == 0, sp and k == len(pairs) - 1)
+        mml([(out, l, r) for l, r in pairs], st, sp)
 
     def iota(out, pat, base=0, cm=0, flag=True):
         op("c", lambda: g.iota(out[0], pat, base, cm, allow_small_or_imprecise_dtypes=True) if flag
@@ -288,19 +297,15 @@ def rank_program(g, core, T, topo):
         return (T[name][:] if lo is None else T[name][:, lo:hi], [])
 
     def m(buf, k):
-        return v(buf, k, ALL) if buf == "OH" else a(buf, 128 * k, 128 * k + 128)
-    ID, BLK, NTRI, IB, NIB, NBLK, HID, WD, B2, I1536, I255, NID, I12, P1536, BC0, I1024 = [m("MB", k) for k in range(16)]
+        return v(buf, k, ALL) if buf[0] == "O" else a(buf, 128 * k, 128 * k + 128)
+    ID, BLK, NTRI, IB, NIB, NBLK, HID, WD, B2, I1536, I255, NID, I12, P1536, BC0, I512, N128, IA = [m("MB", k) for k in range(18)]
     IDf, BLKf, TMPf = [m("MF", k) for k in range(3)]
-    pp, pm, pm4, gb, nb, pq, n4, npm = [a("pc", k, k + 1) for k in range(8)]
+    pp, pm, gb, nb, npm = [a("pc", k, k + 1) for k in (0, 1, 3, 4, 7)]
     cz, half, p2, lo8 = [a("pc", k, k + 1) for k in range(11, 15)]
-    iT, b12, dum2 = a("cT", 0, 16), a("cT", 16, 32), a("cT", 48, 80)
-    TOH, TOC, TOS, COM, TNL = [a("TT", 64 * k, 64 * k + 64) for k in range(5)]
-    qf, oT, dq, kq, om, nl, tT, lm = (a("sf", 0, 16), a("sf", 16, 32), a("sf", 32, 48), a("sf", 48, 64), a("sf", 64, 80),
-                                      a("sf", 80, 96), a("sf", 96, 128), a("sf", 128, 144))
-    lx, dum = a("sf", 144, 160), a("cT", 48, 64)
-    wT, ef, lw = a("sf", 160, 176), a("sf", 176, 192), a("sf", 192, 208)
-    yi, y7, cd, kk, c33 = [a("si", 16 * k, 16 * k + 16) for k in range(5)]
-    q0, jl, cu, el, cl, c1l = [a("su", 16 * k, 16 * k + 16) for k in range(6)]
+    iT, cq, dum2, dum = a("cT", 0, 16), a("cT", 16, 32), a("cT", 48, 80), a("cT", 48, 64)
+    TOH, TOC, TOS, TOW = [a("TT", 64 * k, 64 * k + 64) for k in range(4)]
+    qf, lw = a("sf", 0, 16), a("sf", 192, 208)
+    q0, el, cl, c1l = [a("su", 16 * k, 16 * k + 16) for k in (0, 3, 4, 5)]
     XO, XR, PF = a("XO"), a("XR"), a("PF")
     Lo = a("Lo")
     H = W // 2
@@ -311,7 +316,7 @@ def rank_program(g, core, T, topo):
     for lo, hi in pieces[1:len(pieces) - CFG["late"]]:
         dma("s", a("XO", lo, hi), hbm("x0", lo, hi))
     for k in range(4):
-        dma("as"[k % 2], a("PI", 768 * k, 768 * k + 768), hbm("lk", 768 * k, 768 * k + 768))
+        dma(CFG["lq"][k], a("PI", 768 * k, 768 * k + 768), hbm("lk", 768 * k, 768 * k + 768))
     for lo, hi in pieces[len(pieces) - CFG["late"]:]:
         dma("s", a("XO", lo, hi), hbm("x0", lo, hi))
     iota(a("pi", 0, 1), [[0, 1]], 0, 1, False)
@@ -333,17 +338,19 @@ def rank_program(g, core, T, topo):
     iota(a("IO", 0, 64), [[0, 2], [-1, 16], [0, 2]], 15)
     iota(a("IO", 64, 128), [[0, 2], [-1, 16], [-100, 2]], 115)
     iota(a("IO", 128, 192), [[-100, 2], [-1, 16], [0, 2]], 115)
+    iota(a("IO", 192, 256), [[-100, 2], [1, 16], [-100, 2]], 200)
     iota(a("IK"), [[0, 16], [-2, 16]], 62)
-    iota(a("CT"), [[-12, 256]], W)
+    iota(a("CT"), [[-12, 256]], W // 2)
     iota(a("pi", 8, 11), [[1, 3]], 0, 1, False)
+    iota(a("G"), [[2048, 16], [0, 16]], 0, 0, False)
+    iota(a("KB"), [[2048, 16], [0, 16]], -256)
     recv(prv, [a("Ru")], "r_rd")
     recv(prv, [a("XO", W, W + E)], "r_z")
     recv([helper((rank + 1) % N, n) if n in CFG["via"] else nxt for n in range(len(pieces))], [a("XR", lo, hi) for lo, hi in pieces], "r_x")
 
     ms(a("ZE"), 0.0)
     ts(a("pi", 1, 2), a("pi", 0, 1), 15, Op.bitwise_and)
-    ts(a("pi", 2, 3), a("pi", 0, 1), 2, Op.logical_shift_right, 3, Op.bitwise_and)
-    cp(a("pc", 0, 3), a("pi", 0, 3))
+    cp(a("pc", 0, 2), a("pi", 0, 2))
     c128 = a("COL", 0, 128)
     ts(ID, c128, pp, Op.is_equal)
     ts(a("MK", 0, 16), a("COL", 0, 16), pm, Op.is_equal)
@@ -357,60 +364,66 @@ def rank_program(g, core, T, topo):
         else:
             act(m("DG", k), ID, scale=a("MK", k, k + 1))
     act(IDf, ID)
-    act(BLKf, BLK)
+    act(BLKf, BLK, scale=-1.0)
+    for h in range(2):
+        act(a("ZL", 256 * h, 256 * h + 128), a("COL", 128 * h, 128 * h + 128))
+        act(a("ZL", 256 * h + 128, 256 * h + 256), a("ZE", 0, 128))
     for mat, src, c in ((IB, ID, 4096.0), (NIB, ID, -4096.0), (NBLK, BLK, -4096.0), (HID, ID, 0.5), (I1536, ID, -1536.0),
-                        (P1536, ID, 1536.0), (I1024, ID, 1024.0), (I255, ID, 255.0), (NID, ID, -1.0), (I12, ID, 12.0),
-                        (B2, BLK, 2 * LOSE)):
+                        (P1536, ID, 1536.0), (I512, ID, 512.0), (I255, ID, 255.0), (NID, ID, -1.0), (I12, ID, 12.0),
+                        (B2, BLK, 2 * LOSE), (N128, ID, 128.0), (IA, ID, GATE)):
         act(mat, src, scale=c)
     op("c", lambda: g.affine_select(NTRI[0], NBLK[0], [[1, 128]], Op.is_gt, 0.0, 0, -1), [NTRI], [NBLK])
     act(cz, a("MK", 1, 2), scale=float(W))
     act(a("ZC"), a("COL"), scale=a("MK", 0, 1), bias=cz)
-    act(pq, pm4, scale=-4.0, bias=pp)
-    act(n4, pm4, scale=-1.0)
     act(a("MK", 48, 52), a("COL", 0, 4), bias=gb)
-    act(a("MK", 56, 60), a("COL", 0, 4), AF.Abs, bias=n4)
-    act(a("MK", 52, 56), a("MK", 56, 60), scale=-1000.0, bias=pq)
+    ts(a("pi", 2, 3), a("pi", 1, 2), 1, Op.logical_shift_right)
+    ts(a("pi", 3, 4), a("pi", 1, 2), 1, Op.bitwise_and)
+    act(a("MK", 52, 53), a("pi", 2, 3), bias=gb)
+    for h in range(2):
+        act(a("MK", 53, 54), a("pi", 3, 4), AF.Abs, scale=1000.0, bias=-1000.0 * h)
+        act(a("MK", 54, 55), a("MK", 53, 54), bias=a("MK", 52, 53))
+        act(a("MK", 56 + 2 * h, 58 + 2 * h), a("COL", 0, 2), scale=8.0, bias=a("MK", 54, 55))
+    for k in range(4):
+        ts(m("QM", k), a("X0", 0, 128), a("MK", 56 + k, 57 + k), Op.is_equal)
+    act(a("MK", 55, 56), pm, scale=16.0)
+    ts(a("su", 96, 112), a("COL", 0, 16), a("MK", 55, 56), Op.add)
     now[0] = 0
     for k in range(4):
-        ts(a("QM", 512 * k, 512 * k + 512), a("X0"), a("MK", 52 + k, 53 + k), Op.is_equal)
-    for k in range(4):
         ts(v("OH", S(k, 16, 4), ALL), a("X0"), a("MK", 48 + k, 49 + k), Op.is_equal)
+    for k in range(2):
+        ts(a("O3", 1024 * k, 1024 * k + 1024), a("OH", 1024 * k, 1024 * k + 1024), -64.0, Op.mult)
     now[0] = -1
-    ms(a("PF", W, WIN), 0.0)
-    ms(a("XO", DUMP, WIN), 0.0)
+    ms(a("XO", ZERO, WIN), 0.0)
+    ms(a("XX", 0, 16), -512.0)
     ms(a("XR", W + 16, WIN), 0.0)
-    act(lo8, pm, AF.Sign, scale=-1.0, bias=7.5)
-    act(lo8, lo8, scale=256.5, bias=255.5)
+    act(lo8, pm, AF.Sign, scale=-1.0, bias=5.5)
+    act(lo8, lo8, scale=128.5, bias=126.5)
     act(a("XR", W, W + 16), a("ZE", 0, 16), bias=lo8)
     ms(a("RS0"), 1.0)
     ms(a("RS1"), 0.0)
     ms(a("RS0", 0, 1024, 16), 0.0)
     ms(a("RS1", 0, 1024, 16), 512.0)
     act(iT, a("COL", 0, 16), scale=16.0, bias=pm)
-    act(b12, iT, scale=12.0)
+    act(half, pm, scale=12.0)
+    act(cq, a("COL", 0, 16), scale=192.0 - 2048.0, bias=half)
     act(a("cT", 48, 64), iT, bias=DUMP - OFF)
     act(a("cT", 64, 80), iT, bias=DUMP - OFF)
-    tt(a("G"), a("COL"), a("XK", 0, E), Op.subtract)
-    act(a("KB", 0, E), a("G"), scale=128.0)
-    act(a("KB", E, 2 * E), a("G"), scale=128.0, bias=512.0)
     act(half, a("MK", 0, 1), scale=0.5)
     act(BC0, BLK, scale=half)
     act(npm, pm, scale=-8192.0)
     act(a("AD"), a("XK", 0, 272), AF.Abs, scale=8192.0, bias=npm)
     act(a("OD"), a("AD", 0, E), scale=-1.0, bias=-0.25)
-    now[0] = 0
-    tt(a("G"), a("KB", E, 2 * E), a("AD", 0, E), Op.subtract)
-    now[0] = -1
-    act(a("C21"), a("ZE", 0, E), bias=2 * BIG)
-    act(a("C16"), a("ZE", 0, E), bias=16.0)
-    for c in range(4):
-        for lo, hi in CFG["dq"][c]:
-            if (c, lo) in CFG["gev"]:
-                act(v("C16", S(lo, hi), S(4 * c, 4 * c + 4)), a("ZE", 0, 4 * (hi - lo)))
-    act(a("KC"), a("IK"), bias=0.5)
+    act(a("C21"), a("ZE", 0, E), bias=2.0 ** 19 - GATE * ((CFG["c9"] == "v") + (CFG["c5"] == "v")))
+    act(a("KC"), a("IK"), bias=0.5 * (CFG["c9"] == "a"))
+    late[0] = True
     act(a("SG", 0, 256), a("RS0", 0, 256), scale=0.5)
     act(a("LW"), a("RS1", 0, 256), scale=-LOSE / 256)
-    ts(a("TT", 0, 192), a("IO", 0, 192), pm, Op.is_equal)
+    ts(a("TT", 0, 256), a("IO", 0, 256), pm, Op.is_equal)
+    act(a("IO", 0, 64), TOS, scale=-4096.0 - OFF, bias=OFF)
+    act(a("IO", 64, 128), TOW, scale=8192.0)
+    tt(a("TT", 193, 256), a("IO", 1, 64), a("IO", 65, 128), Op.add)
+    act(a("TT", 192, 193), a("ZE", 0, 1), bias=OFF + 1024.0)
+    act(a("NL", 16, 32), a("ZE", 0, 16), bias=4.0)
     now[0] = 0
     scan(a("TH"), a("SG", 0, 256), a("LW"), Op.mult, Op.add)
     tt(a("MK", 16, 32), a("TH", 0, 16), a("MK", 0, 16), Op.mult)
@@ -424,20 +437,32 @@ def rank_program(g, core, T, topo):
     now[0] = 0
     for k in range(16):
         act(a("TS", 64 * k, 64 * k + 64), TOS, AF.Sign, bias=a("MK", 32 + k, 33 + k))
-    now[0] = -1
+    act(a("PF", W, W + 272), a("ZE", 0, 272))
+    act(a("PF", W + 272, WIN), a("ZE", 0, WIN - W - 272))
+    late[0] = False
     ts(a("Ro"), a("Ru"), -OFF, Op.add)
     now[0] = 0
-    mms(a("B7", 0, E), [(BLK, a("XO", 0, W, 12))])
-    act(a("Os"), a("B7", 0, E), AF.Relu, bias=1.0, scale=-1.0)
-    send(prv, a("OR"), a("Os"), "r_o")
+    mms(a("B7", 0, 16), [(m("OH", k), a("XO", 12 * k, W, 192)) for k in range(16)])
+    act(a("Os", 0, 16), a("B7", 0, 16))
+    send(prv, a("Os", 16, 32), a("Os", 0, 16), "r_o")
     now[0] = -1
     send(prv, a("XR", *pieces[-1]), a("XO", *pieces[-1]), "r_x")
     iota(a("J"), [[0, E], [1, 12]])
     ops[-1]["behind"] = len(ops) - 2
-    recv(nxt, [a("OR")], "r_o")
+    recv(nxt, [a("Os", 16, 32)], "r_o")
 
-    def to_list(out, mats, src, n, st=True, sp=True):
-        mms(out, [(m(mats, k), a(src[0], src[1] + k, src[1] + n, 16)) for k in range(16)], st, sp)
+    def to_list(out, src, base, lo, hi, st=True, sp=True):
+        mms(out, [(m("OH", k), a(src, base + lo + k, base + hi, 16)) for k in range(16)], st, sp)
+
+    def cols(bank, r, lo, hi):
+        return a(bank, 16 * r + lo, 16 * r + hi)
+
+    behind = {}
+
+    def follow(line):
+        if line in behind:
+            ops[-1]["behind"] = behind[line]
+        behind[line] = len(ops) - 1
 
     def own_update(t):
         recv(prv, [a("wr", 16 * t, 16 * t + 16)], "r_w%d" % t)
@@ -448,166 +473,112 @@ def rank_program(g, core, T, topo):
         ts(nw, a("SX"), 0.5, Op.mult, -0.25, Op.add)
         if t < RO - 1:
             send(prv, a3("Nr", t, t + 1, 0, 272), a3("Ns", t, t + 1, 0, 272), "r_n%d" % t)
-        cp(ind(XO, xl), nw)
+            cp(ind(a("XX", AT["XR"], AT["XO"] + WIN), a3("Ns", t, t + 1, 272, 288)), nw)
+        else:
+            cp(ind(XO, xl), nw)
 
-    def pairs(Eb, src, col, bank, blocks):
-        line[0] = CFG["pairline"] or Eb
-        for f in range(2):
-            for b in blocks:
-                e = a3(Eb, b, b + 1, 0, 256 - 16 * b)
-                if f == 0:
-                    act(e, src(16 * b), AF.Abs, bias=a("sf", col + b, col + b + 1), scale=-1.0)
-                else:
-                    act(e, e, AF.Relu, bias=1.0, scale=-1.0)
-        mms(a(bank, 0, 256), [(ID, a("TH"))], True, False)
-        for b in range(16):
-            if b not in blocks:
-                ts(a3(Eb, b, b + 1, 0, 256 - 16 * b), src(16 * b), a("sf", col + b, col + b + 1), Op.is_equal)
-            if b < 15:
-                mm(a(bank, 16 * b + 16, 256), B2, a3(Eb, b, b + 1, 16, 256 - 16 * b), False, False)
-        mm(a(bank, 0, 256), WD, a3(Eb, 0, 16, 0, 16), False, True)
-        line[0] = None
+    def pairs(Eb, base, col, bank, on_a, b0, b1):
+        if b1 == 16:
+            mms(a(bank, 0, 256), [(ID, a("TH"))], True, False)
+        for b in range(b0, b1):
+            e, src, me = a3(Eb, b, b + 1, 0, 256 - 16 * b), a("TB", base + 16 * b, base + E), a("sf", col + b, col + b + 1)
+            if b in on_a:
+                act(e, src, AF.Abs, bias=me, scale=-1.0)
+                follow("a1")
+                act(e, e, AF.Relu, bias=1.0, scale=-1.0)
+                follow("a2")
+            else:
+                ts(e, src, me, Op.is_equal)
+                follow("v")
+        behind.clear()
+        runs = [[b for b in range(b0, min(b1, 15)) if (b in on_a) == f] for f in (False, True)]
+        for run in [r[k:k + CFG["erun"]] for r in runs for k in range(0, len(r), CFG["erun"])]:
+            mml([(a(bank, 16 * b + 16, 256), B2, a3(Eb, b, b + 1, 16, 256 - 16 * b)) for b in run], False, False)
+        mms(a(bank, 16 * b0, 16 * b1), [(WD, v(Eb, S(b0, b1), S(0, 16)))], False, b0 == 0)
 
     for t in range(RO):
         last = t == RO - 1
         now[0] = t
-        Y = a3("Ys", t, t + 1, 0, E)
+        Y = a("Ys", E * t, E * t + E)
         locks = a("PI") if t == 0 else PF
 
         def lk_open(h):
-            if CFG["whole"]:
-                if h:
-                    mms(a("B1"), [(ID, a("ZE"))], True, False)
-                    mms(a("B1", 0, E), [(ID, a("Ro"))], False, False)
-                    mms(a("B1", E, 2 * E), [(ID, a("Ro"))], False, False)
-                    mms(a("B2", 0, E), [(ID, a("ZC"))], True, False)
-                return
             bs = "B%d" % (2 * h + 1)
-            mms(a(bs, 0, 384), [(ID, a("ZE", 0, 384))], True, False)
-            mms(a(bs, 0, 128), [(ID, a("Ro", 128 * h, 128 * h + 128))], False, False)
-            mms(a(bs, 128, 256), [(ID, a("Ro", 128 * h, 128 * h + 128))], False, False)
-            mms(a(bs, 256, 384), [(ID, a("ZC", 128 * h, 128 * h + 128))], False, False)
-
-        def lk_whole():
-            fr = a("FR")
-            act(fr, a("B0", 0, E), AF.Relu, bias=-1535.0)
-            mms(a("B1", 0, E), [(IB, fr), (NTRI, fr)], False, False)
-            mms(a("B1", E, 2 * E), [(IB, fr)], False)
-            mms(a("B2", 0, E), [(NBLK, fr)], False)
-            act(Lo, a("B0", 0, E))
-            act(a("SU", 0, E), a("B1", 0, E), AF.Relu, bias=OFF - 4096.0)
-            act(a("N2"), a("B2", 0, E), AF.Relu)
-            act(a("SU", E, 2 * E), a("B1", E, 2 * E), AF.Relu, bias=OFF - 4096.0)
-            mms(a("B3", 0, E), [(NIB, fr), (BLKf, a("SU", 0, E)), (BLK, a("N2"))])
-            tt(a("Rp"), a("B3", 0, E), a("SU", E, 2 * E), Op.max)
-            cp(a("Rq"), a("Rp"))
+            mml([(a(bs, 0, 256), ID, a("ZL", 256 * h, 256 * h + 256)), (a(bs, 0, 128), NID, a("Ro", 128 * h, 128 * h + 128)),
+                 (a(bs, 128, 256), ID, a("Ro", 128 * h, 128 * h + 128))], True, False)
 
         def lk_gather(eng, lo, hi):
-            line[0] = "gathers"
             gather(eng, a("GL", 16 * lo, 16 * hi), locks, a("Ru", lo, hi), -OFF)
-            line[0] = None
 
         def lk_pick(c):
-            if CFG["whole"]:
-                mms(a("B0", 64 * c, 64 * c + 64), [(m("DG", k), a("GL", 1024 * c + k, 1024 * c + 1024, 16)) for k in range(16)])
-            elif CFG["pk"] == 64:
-                mms(a("B%d" % (c // 2 * 2), 64 * (c % 2), 64 * (c % 2) + 64),
-                    [(m("DG", k), a("GL", 1024 * c + k, 1024 * c + 1024, 16)) for k in range(16)])
-            elif c % 2:
-                mms(a("B%d" % (c - 1), 0, 128), [(m("DG", k), a("GL", 1024 * c - 1024 + k, 1024 * c + 1024, 16)) for k in range(16)])
+            mms(a("B%d" % (c // 2 * 2), 64 * (c % 2), 64 * (c % 2) + 64),
+                [(m("DG", k), a("GL", 1024 * c + k, 1024 * c + 1024, 16)) for k in range(16)])
 
         def lk_free(h):
             bl, bs, fr = "B%d" % (2 * h), "B%d" % (2 * h + 1), a("FR", 128 * h, 128 * h + 128)
-            line[0] = CFG["s1line"]
-            take("FR%d" % h, fr, a(bl, 0, 128), -1535.0, True)
-            line[0] = None
-            mms(a(bs, 0, 128), [(IB, fr), (NTRI, fr)], False, False)
-            mms(a(bs, 128, 256), [(IB, fr)], False, False)
-            mms(a(bs, 256, 384), [(NBLK, fr)], False)
-            take("Lo%d" % h, a("Lo", 128 * h, 128 * h + 128), a(bl, 0, 128))
+            act(fr, a(bl, 0, 128), AF.Relu, bias=-1535.0)
+            mml([(a(bs, 0, 128), IB, fr), (a(bs, 0, 128), NTRI, fr), (a(bs, 128, 256), IB, fr)], False)
+            act(a("Lo", 128 * h, 128 * h + 128), a(bl, 0, 128))
 
         def lk_first(h):
             bl, bs, fr = "B%d" % (2 * h), "B%d" % (2 * h + 1), a("FR", 128 * h, 128 * h + 128)
-            line[0] = CFG["s1line"]
-            take("SU%d" % h, a("SU", 256 * h, 256 * h + 256), a(bs, 0, 256), OFF - 4096.0, True)
-            take("N2%d" % h, a("N2", 128 * h, 128 * h + 128), a(bs, 256, 384), 0.0, True)
-            line[0] = None
-            mms(a(bl, 128, 256), [(NIB, fr), (BLKf, a("SU", 256 * h, 256 * h + 128)), (BLK, a("N2", 128 * h, 128 * h + 128))])
+            act(a("SU", 256 * h, 256 * h + 256), a(bs, 0, 256), AF.Relu, bias=OFF - 4096.0)
+            mms(a(bs, 384, 512), [(NIB, fr), (BLK, a("ZC", 128 * h, 128 * h + 128)), (BLKf, a("SU", 256 * h, 256 * h + 128))])
 
         def lk_list(h):
-            tt(a("Rp", 128 * h, 128 * h + 128), a("B%d" % (2 * h), 128, 256), a("SU", 256 * h + 128, 256 * h + 256), Op.max)
+            tt(a("Rp", 128 * h, 128 * h + 128), a("B%d" % (2 * h + 1), 384, 512), a("SU", 256 * h + 128, 256 * h + 256), Op.max)
             cp(a("Rq", 128 * h, 128 * h + 128), a("Rp", 128 * h, 128 * h + 128))
 
         def cells(eng, lo, hi):
-            line[0] = "gathers"
             gather(eng, a("GX", 16 * lo, 16 * hi), XO, a("Rq", lo, hi))
-            line[0] = None
-
-        def scans(lo, hi):
-            n = 16 * (hi - lo)
-            line[0] = "scans"
-            scan(a("MX", 16 * lo, 16 * hi), a("RS0", 0, n), a("GX", 16 * lo, 16 * hi), Op.mult, Op.max)
-            scan(a("MN", 16 * lo, 16 * hi), a("RS1", 0, n), a("GX", 16 * lo, 16 * hi), Op.add, Op.min)
-            line[0] = None
-
-        def turn_locks():
-            for kh in range(4):
-                mms(a("B4", 64 * kh, 64 * kh + 64), [(m("QM", 4 * kh + sl), a("Lo", sl, E, 4)) for sl in range(4)])
 
         ql = q0 if t == 0 else a("qs", 32 * t - 32, 32 * t - 16)
-
-        def orphans():
-            act(a("OG"), ind(XR, ql))
-            mms(a("B3", 0, 256), [(BLK, a("OG"))])
-
-        def y_val(l0, l1):
-            for lo, hi in ((l0, CFG["sc"][-1][0]), CFG["sc"][-1]):
-                mx, mn = a("MX", 16 * lo + 15, 16 * hi, 16), a("MN", 16 * lo + 15, 16 * hi, 16)
-                mms(a("B1", lo, hi), [(BC0, mx), (BC0, mn)], False, hi == E)
-                mms(a("B5", lo, hi), [(HID, mx), (HID, mn)])
-            for r in range(4):
-                if r in CFG["ypool"]:
-                    gcopy(a("Y4", 4 * l0 + r, 4 * l1, 4), a("Y4", 4 * l0, 4 * l1, 4), l1 - l0)
-                else:
-                    take("Y%d" % r, a("Y4", 4 * l0 + r, 4 * l1, 4), a("B5", l0, l1), 1023.75)
-                if r == 0:
-                    take("Y", a3("Ys", t, t + 1, l0, l1), a("Y4", 4 * l0, 4 * l1, 4), -1024.0)
-
-        def primaries():
-            scan(a("YS"), a("G"), a("B1", 0, E), Op.max, Op.max)
-            ts(y7, a("YS", 15, E, 16), 7, Op.bitwise_and)
-            tt(qf, y7, b12, Op.add)
-            cp(a("qs", 32 * t, 32 * t + 16), qf)
-            cp(ind(XR, a("qs", 32 * t, 32 * t + 16)), Y)
-
         lk_open(0)
         lk_open(1)
         if t > 0:
             own_update(t - 1)
         else:
             for k in range(4):
-                cp(a("PF", 768 * k, 768 * k + 768), a("PI", 768 * k, 768 * k + 768))
+                (cp if CFG["pfq"][k] == "v" else act)(a("PF", 768 * k, 768 * k + 768), a("PI", 768 * k, 768 * k + 768))
         steps = {"L": lk_gather, "X": cells, "P": lk_pick, "F": lk_free, "S": lk_first, "R": lk_list}
         for st in CFG["s1_0" if t == 0 else "s1"]:
-            if not CFG["whole"] or st[0] in "LXP":
-                steps[st[0]](*st[1:])
-            elif st == ("F", 1):
-                lk_whole()
-        turn_locks()
+            steps[st[0]](*st[1:])
         if t > 0:
             recv(nxt, [a3("Nr", t - 1, t, 0, 272)], "r_n%d" % (t - 1))
-            cp(ind(XR, a("ws", 16 * t - 16, 16 * t)), a("ZE", 0, E))
             cp(ind(XR, a3("Nr", t - 1, t, 256, 272)), a3("Nr", t - 1, t, 0, E))
         for lo, hi in CFG["sc"]:
-            scans(lo, hi)
-        ts(a("Lu"), a("B4", 0, 256), OFF, Op.add)
+            n = 16 * (hi - lo)
+            scan(a("MX", 16 * lo, 16 * hi), a("RS0", 0, n), a("GX", 16 * lo, 16 * hi), Op.mult, Op.max)
+            scan(a("MN", 16 * lo, 16 * hi), a("RS1", 0, n), a("GX", 16 * lo, 16 * hi), Op.add, Op.min)
+        for h in range(2):
+            for l0 in (0, 8):
+                mml([(a("B7", 128 * h + 8 * l, 128 * h + 8 * l + 8), m("QM", 2 * h + s), a("Lo", 16 * s + l, E, 32))
+                     for l in range(l0, l0 + 8) for s in range(2)], alone=2)
+        ts(a("Lu"), a("B7", 0, E), OFF, Op.add)
         if t > 0:
-            orphans()
-            act(a("OR"), a("B3", 0, 256), AF.Relu, bias=1.0, scale=-1.0)
-        mms(a("B1", 0, E), [(ID, a("OD", 0, E)), (ID, a("KB", 0, E)), (I1024, a("OR"))], True, False)
-        for lo, hi in CFG["yp"]:
-            y_val(lo, hi)
-        primaries()
+            gather(CFG["og"], a("OG"), XR, ql)
+        else:
+            mml([(a("B4", k, E, 16), m("DG", k), a("Os", 16, 32)) for k in range(16)], alone=True)
+            act(a("OG"), a("B4", 0, E))
+        mms(a("B4", 0, 256), [(BLK, a("OG"))])
+        act(a("OR"), a("B4", 0, 256), AF.Relu, bias=1.0, scale=-1.0)
+
+        for (l0, l1), (b1, b5) in zip(CFG["yp"], (("B1", "B5"), ("B6", "B0"))):
+            mms(a(b1, l0, l1), [(ID, a("OD", l0, l1)), (ID, a("KB", l0, l1))], True, False)
+            mms(a(b1, l0, l1), [(I512, a("OR", l0, l1))], False, False)
+            cut = max([lo for lo, hi in CFG["sc"] if l0 <= lo < l1])
+            for lo, hi in ((l0, cut), (cut, l1))[l0 == cut:]:
+                mx, mn = a("MX", 16 * lo + 15, 16 * hi, 16), a("MN", 16 * lo + 15, 16 * hi, 16)
+                mms(a(b1, lo, hi), [(BC0, mx), (BC0, mn)], False, hi == l1)
+                mms(a(b5, lo, hi), [(HID, mx), (HID, mn)])
+            act(a("Y16", l0, l1), a(b5, l0, l1), bias=1023.75)
+            act(a("Ys", E * t + l0, E * t + l1), a("Y16", l0, l1), bias=-1024.0)
+            scan(a("YS", l0, l1), a("G", l0, l1), a(b1, l0, l1), Op.max, Op.max)
+            ts(a("G", l0, l1, 16), a("YS", l0 + 15, l1, 16), 0xFE07, Op.bitwise_and)
+            tt(a("sf", l0 // 16, l1 // 16), a("G", l0, l1, 16), a("cT", 16 + l0 // 16, 16 + l1 // 16), Op.add)
+            cp(a("qs", 32 * t + l0 // 16, 32 * t + l1 // 16), a("sf", l0 // 16, l1 // 16))
+            cp(ind(XR, a("qs", 32 * t + l0 // 16, 32 * t + l1 // 16)), a("Ys", E * t + l0, E * t + l1))
+        act(a("Yd"), ind(Y, a("su", 96, 112)), bias=-128.0)
         ql = a("qs", 32 * t, 32 * t + 16)
         send(nxt, a3("Yr", t, t + 1, 0, E), Y, "r_y%d" % t)
         send(nxt, a("qr", 16 * t, 16 * t + 16), ql, "r_y%d" % t)
@@ -615,117 +586,134 @@ def rank_program(g, core, T, topo):
             send(prv, a("zr"), Y, "r_zo")
         else:
             gcopy(a("XO", W, W + E), Y, E)
+            ops[-1]["behind"] = len(ops) - 2
+        mms(a("B4", 256, 272), [(m("OH", k), a("Yd", 16 * k, 16 * k + 16)) for k in range(16)])
+        act(a("sy"), a("B4", 256, 272), scale=-1.0)
         mms(a("B7", 256, 512), [(I255, a("OR", 0, 256)), (NID, Y)])
         act(a("U"), a("B7", 256, 512), AF.Abs)
         mms(a("B7", 0, 256), [(ID, a("Ro")), (I12, a("U"))])
         mms(a("B7", 256, 512), [(ID, Lo), (I12, a("U"))])
         act(a("SG"), a("B7"), AF.Sign, bias=-1534.5)
         mms(a("B7", 0, 256), [(ID, a("Ro")), (I12, a("U")), (I1536, a("SG", 0, 256))], True, False)
-        mms(a("B0", 256, 512), [(ID, Lo), (NID, a("Ro")), (I1536, a("SG", 256, 512)), (P1536, a("SG", 0, 256))])
-        take("DL", a("DL"), a("B0", 256, 512))
 
+        mms(a("B6", 0, E), [(ID, a("ZE", 0, E))], True, False)
+        mml([(a("B6", k, E, 16), ID, a("sy")) for k in range(16)], False, False)
         mms(a("B5", 0, E), [(ID, a("KC")), (ID, a("C21"))], True, False)
-        mms(a("B6", 0, E), [(ID, a("C16"))], True, False)
+
+        def chunk(c, bs, bk):
+            by = CFG["yb"][c]
+            mml([(a(by, r, 512, 8), ID, a("Yd", 64 * c, 64 * c + 64)) for r in range(8)], alone=True)
+            for h in range(2):
+                for l0, l1 in CFG["ttcut"].get((c, h), ((4 * c, 4 * c + 4),)):
+                    lo, hi = 2048 * h + 128 * l0, 2048 * h + 128 * l1
+                    tt(a("MG", lo, hi), a("EG", lo, hi), a(by, 128 * l0 - 512 * c, 128 * l1 - 512 * c), Op.max)
+                    for bank, mats, src in ((bk, "O3", "EG"), (bs, "OH", "MG")):
+                        mms(a(bank, h, E, 2), [(m(mats, s), a(src, 2048 * h + 128 * s, 2048 * h + 128 * s + 128)) for s in range(l0, l1)],
+                            False, (src, h, l1) == ("MG", 1, 16))
+
+        def verdict(lo, hi, bs, bk):
+            b0, b1 = lo // 16, hi // 16
+            for l0, l1 in CFG["vh"]:
+                ts(a("RI", l0, l1), a(bs, l0, l1), -17 / 32, Op.add, 0.0, Op.max)
+            for l0, l1 in CFG["vh"]:
+                tt(a("FN", l0, l1), a(bs, l0, l1), a("RI", l0, l1), Op.subtract)
+            act(a("RH", lo, hi), a("RI", lo, hi), bias=-2048.0)
+            mms(a(bk, lo, hi), [(N128, a("RH", lo, hi))], False, False)
+            for l0, l1 in CFG["vh"]:
+                act(a("C9", l0, l1), a("FN", l0, l1), AF.Sign, bias=-8.5 / 16)
+                ts(a("C5", l0, l1), a("FN", l0, l1), 4.5 / 16, Op.is_lt, 2.0, Op.mult)
+                mms(a(bk, l0, l1), [(IA, a("C5", l0, l1))], False, False)
+                mms(a(bk, l0, l1), [(IA, a("C9", l0, l1)), (HID, a("C9", l0, l1))], False, l1 == hi)
+            for l0, l1 in CFG["kh"]:
+                scan(a("KS", l0, l1), a("RS0", 0, l1 - l0), a(bk, l0, l1), Op.mult, Op.max)
+                ts(a("si", 32 + l0 // 16, 32 + l1 // 16), a("KS", l0 + 15, l1, 16), 63, Op.bitwise_and)
+                cp(a("su", 32 + l0 // 16, 32 + l1 // 16), a("si", 32 + l0 // 16, 32 + l1 // 16))
+            cu = a("su", 32 + b0, 32 + b1)
+
+            def targets():
+                tt(a("SB", E + lo, E + hi), ind(TOH, cu), a("Ro", lo, hi), Op.mult)
+                mms(a(bt, lo, hi), [(BLK, a("SB", E + lo, E + hi))])
+                act(a("TB", lo, hi), a(bt, lo, hi))
+                to_list(cols(lt, 28, b0, b1), "SB", E, lo, hi)
+                act(a("sf", 112 + b0, 112 + b1), cols(lt, 28, b0, b1))
+                pairs("E2", 0, 112, "B6", CFG["eqa2"], b0, b1)
+
+            def wiped():
+                tt(a("SB", lo, hi), ind(TOW, cu), a("Lo", lo, hi), Op.max)
+                mms(a(bw, E + lo, E + hi), [(BLK, a("SB", lo, hi))])
+                act(a("TB", E + lo, E + hi), a(bw, E + lo, E + hi), bias=-15 * OFF)
+                to_list(cols(lx, 29, b0, b1), "SB", 0, lo, hi)
+                act(a("sf", 160 + b0, 160 + b1), cols(lx, 29, b0, b1), bias=-15 * OFF)
+                act(a("sf", 96 + b0, 96 + b1), cols(lx, 29, b0, b1), bias=-15 * OFF - 8192.0 + AT["XR"])
+                act(a("NL", b0, b1), a("sf", 96 + b0, 96 + b1), AF.Abs, scale=8.0)
+                pairs("E1", E, 160, "B5", CFG["eqa3" if last else "eqa1"], b0, b1)
+            lt, lx, bt, bw = CFG["bk"][lo == 0]
+            for f in (wiped, targets) if last or CFG["wfirst"] else (targets, wiped):
+                f()
+            tt(a("MM", lo, hi), ind(TOC, cu), a("DL", lo, hi), Op.mult)
+            mms(a("B7", lo, hi), [(IDf, a("MM", lo, hi))], False, lo == 0)
+
+        for eng, lo, hi in CFG["eg"]:
+            gather(eng, a("EG", 16 * lo, 16 * hi), XR, a("Lu", lo, hi), 0.0625 - 128.0)
+        for c in range(4):
+            chunk(c, "B6", "B5")
+        mms(a("B0", 256, 512), [(ID, Lo), (NID, a("Ro")), (I1536, a("SG", 256, 512)), (P1536, a("SG", 0, 256))])
+        act(a("DL"), a("B0", 256, 512))
         if not last:
             act(a("JG"), ind(a("J"), ql))
-            mms(a("B1", 256, 512), [(IDf, a("CT")), (NID, a("AD", t, t + E)), (NID, a("JG"))])
-            take("C2", a("C2"), a("B1", 256, 512), 0.0, True)
-            mms(a("B2", E, 2 * E), [(ID, a("KB", E, 2 * E)), (NID, a("AD", 0, E)), (ID, a("JG"))])
-            act(a("G"), a("B2", E, 2 * E))
-        for c in range(4):
-            line[0] = "step 3"
-            for lo, hi in CFG["dq"][c]:
-                dd = a("D", 1024 * c + 64 * lo, 1024 * c + 64 * hi)
-                tt(dd, ind(XR, a("Lu", 64 * c + 4 * lo, 64 * c + 4 * hi)), a("Y4", 64 * lo, 64 * hi), Op.subtract)
-                ge = v("GE", S(16 * c + lo, 16 * c + hi), ALL)
-                if (c, lo) in CFG["gev"]:
-                    ts(ge, dd, -1024.0, Op.is_ge, 2.0, Op.mult)
-                else:
-                    act(ge, dd, AF.Sign, bias=1024.5)
-                act(v("AB", S(16 * c + lo, 16 * c + hi), ALL), dd, AF.Abs, bias=65536.0, scale=64.0)
-            line[0] = None
-            for src, bank in (("GE", "B6"), ("AB", "B5")):
-                mms(v(bank, S(0, 16), S(4 * c, 4 * c + 4)),
-                    [(m("OH", s), v(src, S(16 * c, 16 * c + 16), S(4 * s, 4 * s + 4))) for s in range(16)], False, c == 3 and src == "GE")
-        act(a("CS"), a("B6", 0, E), AF.Sign, bias=-17.0)
-        act(a("GK"), a("B6", 0, E), AF.Abs, bias=-6.5 * BIG, scale=BIG / 2)
-        mms(a("B5", 0, E), [(HID, a("CS"))], False)
-        tt(a("KY"), a("B5", 0, E), a("GK"), Op.min)
-        scan(a("KS"), a("RS0", 0, E), a("KY"), Op.mult, Op.max)
-        ts(cd, a("KS", 15, E, 16), 63, Op.bitwise_and)
-        cp(cu, cd)
-        line[0] = "picks"
-        for hh in (0, 256) if last else CFG["picks"]:
-            bank = "B0" if hh else "B3"
-            if hh:
-                tt(a("SB", 256, 512), ind(TOH, cu), a("Ro"), Op.mult)
-            else:
-                tt(a("SB", 0, 256), ind(TOS, cu), Lo, Op.mult)
-            if hh:
-                mms(a(bank, 256, 512), [(BLK, a("SB", hh, hh + 256))])
-                to_list(a("B4", 288, 304), "OH", ("SB", hh), 256)
-            else:
-                ts(c33, cd, 33, Op.bitwise_and)
-                act(nl, c33, AF.Abs, bias=-32.0 * 4096, scale=4096.0)
-                mms(a(bank, 256, 512), [(BLK, a("SB", hh, hh + 256))])
-                to_list(a("B6", 288, 304), "OH", ("SB", 0), 256, True, False)
-                mms(a("B6", 288, 304), [(IDf, nl)], False)
-        line[0] = None
-        act(ef, c33, AF.Abs, bias=-33.0 * 8192, scale=8192.0)
+            mms(a("B1", 256, 512), [(ID, a("CT")), (NID, a("AD", t, t + E)), (NID, a("JG"))])
+            act(a("C2"), a("B1", 256, 512), AF.Relu, bias=OFF)
+        verdict(0, E, "B6", "B5")
+        cd = a("si", 32, 48)
 
         def wipes():
-            act(a("TB", E, 2 * E), a("B3", 256, 512))
-            act(wT, a("B6", 288, 304))
-            act(a("sf", 96, 112), a("B6", 288, 304), bias=-4096.0)
-            pairs("E1", lambda lo: a("TB", E + lo, 2 * E), 160, "B1", CFG["eqa3" if last else "eqa1"])
-            act(a("LW"), a("B1", 0, 256), AF.Relu)
-            mms(a("B5", 0, 16), [(IDf, wT)], True, False)
-            to_list(a("B5", 0, 16), "OH", ("LW", 0), 256, False)
-            tt(lw, a("B5", 0, 16), dum, Op.min)
+            act(a("LW"), a("B5", 0, 256), AF.Relu)
+            mms(a("B3", 0, 16), [(IDf, a("sf", 160, 176))], True, False)
+            to_list(a("B3", 0, 16), "LW", 0, 0, E, False)
+            tt(lw, a("B3", 0, 16), dum, Op.min)
             wl = a("ws", 16 * t, 16 * t + 16)
             ts(wl, lw, OFF, Op.add)
             send(nxt, a("wr", 16 * t, 16 * t + 16), wl, "r_w%d" % t)
 
         def winners():
-            act(a("TB", 0, E), a("B0", 256, 512))
-            act(a("sf", 112, 128), a("B4", 288, 304))
-            pairs("E2", lambda lo: a("TB", lo, E), 112, "B2", CFG["eqa2"])
-            act(a("LN"), a("B2", 0, 256), AF.Relu)
-            mms(a("B4", 320, 336), [(I1536, a("RS0", 1, 16 * 16, 16)), (IDf, ef)])
+            act(a("LN"), a("B6", 0, 256), AF.Relu)
+            mms(a("B4", 320, 336), [(NIB, a("NL", 16, 32)), (ID, a("NL", 0, 16))])
             mms(a("B4", 336, 352), [(IDf, a("sf", 112, 128))], True, False)
-            to_list(a("B4", 336, 352), "OH", ("LN", 0), 256, False)
-        for hh in (0, 256) if last else CFG["picks"]:
-            (winners if hh else wipes)()
-        tt(a("MM"), ind(TOC, cu), a("DL"), Op.mult)
-        mms(a("B7", 0, 256), [(IDf, a("MM"))], False)
+            to_list(a("B4", 336, 352), "LN", 0, 0, E, False)
+        for f in (wipes, winners) if last or CFG["wfirst"] else (winners, wipes):
+            f()
+        if last:
+            act(a("RS"), a("B7", 0, 256), bias=1.0 - OFF)
+            send(prv, a("rh"), a("RS"), "r_ro")
         if not last:
             act(a("sf", 128, 144), cd, bias=a("pc", 8 + t, 9 + t))
-        ts(a("su", 48, 80 if last else 96), a("sf", 96, 128 if last else 144), OFF, Op.add, W - 1.0, Op.min)
-        act(a("EV"), ind(XR, el))
-        if last:
-            act(a("RS"), a("B7", 0, 256), bias=1.0)
-            send(prv, a("rr"), a("RS"), "r_ro")
-        else:
+        ts(a("su", 48, 80 if last else 96), a("sf", 96, 128 if last else 144), OFF, Op.add, W + 15.0, Op.min)
+        act(a("EV"), ind(a("XX", 0, AT["XO"]), el))
+        if not last:
             act(a("Ro"), a("B7", 0, 256), bias=1.0 - OFF)
             act(a("C1"), ind(a("TS"), c1l), bias=1536.0, scale=1536.0)
             tt(a("PT"), ind(PF, cl), a("C1"), Op.max)
             ts(a("Ru"), a("Ro"), OFF, Op.add)
         tt(a("sf", 208, 240), a("B4", 320, 352), dum2, Op.min)
-        if not last and CFG["pl"]:
+        if not last:
             ts(a("pl"), a("sf", 224, 240), OFF, Op.add)
-            tt(ind(PF, a("pl")), a("PT"), a("C2"), Op.subtract)
+            for lo, hi in CFG["pfp"]:
+                tt(ind(PF, a("pl", lo // 16, hi // 16)), a("PT", lo, hi), a("C2", lo, hi), Op.subtract)
         tt(a("sf", 208, 224), a("sf", 208, 224), a("sf", 224, 240), Op.max)
-        wide = 16 if last or CFG["pl"] else 32
+        if not last:
+            act(a("sf", 16, 32), a("sf", 208, 224), bias=float(WIN))
+            tt(a("sf", 224, 240), a("B3", 0, 16), a("sf", 16, 32), Op.min)
+        wide = 16 if last else 32
         ts(a3("Ns", t, t + 1, 256, 256 + wide), a("sf", 208, 208 + wide), OFF, Op.add)
-        if not last and not CFG["pl"]:
-            tt(ind(PF, a3("Ns", t, t + 1, 272, 288)), a("PT"), a("C2"), Op.subtract)
         recv(prv, [a3("Yr", t, t + 1, 0, E), a("qr", 16 * t, 16 * t + 16)], "r_y%d" % t)
-        cp(ind(XO, a("qr", 16 * t, 16 * t + 16)), a3("Yr", t, t + 1, 0, E))
+        for lo, hi in CFG["xp"]:
+            cp(ind(XO, a("qr", 16 * t + lo // 16, 16 * t + hi // 16)), a3("Yr", t, t + 1, lo, hi))
     now[0] = RO
     own_update(RO - 1)
     recv(nxt, [a("zr")], "r_zo")
     dma("s", hbm("zo"), a("zr"))
-    recv(nxt, [a("rr")], "r_ro")
+    recv(nxt, [a("rh")], "r_ro")
+    act(a("rr"), a("rh"), bias=OFF)
     dma("s", hbm("ro"), a("rr"))
     dma("s", hbm("xo", 0, H), a("XO", 0, H))
     dma("a", hbm("xo", H, W), a("XO", H, W))
@@ -735,38 +723,46 @@ def rank_program(g, core, T, topo):
         pre = {}
         for (name, mask), w in [(r, False) for r in o["rd"]] + [(r, True) for r in o["wr"]]:
             if SCRATCH[name][0] == "psum":
-                i = bank.get(name, j)
-                if i != j:
-                    pre[i] = pre.get(i, False) or ops[i]["eng"] != o["eng"]
-                bank[name] = j
-                if o["eng"] == "p":
-                    continue
+                held = bank.setdefault(name, [j])
+                for i in held[:1] if o.get("adds") else held:
+                    if i != j:
+                        pre[i] = pre.get(i, False) or ops[i]["eng"] != o["eng"]
+                bank[name] = held + [j] if o.get("adds") else [j]
+                continue
             keep = []
             for (i, m2, w2) in seen.get(name, []):
                 if i != j and (w or w2) and mask & m2:
                     if ops[i].get("remote") != "sent":
-                        same = ops[i]["eng"] == o["eng"] and o["eng"] in "va" and "sem" not in ops[i] and w and CFG["lax"]
-                        pre[i] = pre.get(i, False) or (o["eng"] != "x" and not same)
+                        pre[i] = pre.get(i, False) or o["eng"] != "x"
                 if i == j or not (w and not m2 & ~mask):
                     keep.append((i, m2, w2))
             seen[name] = keep + [(j, mask, w)]
-        ln = "remote" if o.get("remote") else "dma" if "dma" in o else o["line"] if o["eng"] == "p" or not ORDER["v"] else None
+        ln = "remote" if o.get("remote") else "dma" if "dma" in o else None
         if ln:
             if ln in chain:
                 pre.setdefault(chain[ln], False)
             chain[ln] = j
         if "behind" in o:
-            pre[o["behind"]] = False
+            pre.setdefault(o["behind"], False)
         if o.get("remote"):
             sent_as.setdefault(o["msg"], []).append(j)
         o["pre"] = pre
     for e in "va":
+        gate = [j for j, o in enumerate(ops) if o["eng"] == e and o["wr"] and o["wr"][0][0] == "GL"][1]
+        for o in ops:
+            if o["late"] and o["eng"] == e:
+                o["pre"].setdefault(gate, False)
+    for e in "vap":
         prev = None
+        rest = {t: [j for j, o in enumerate(ops) if o.get("name", (0, 0))[:2] == (t, e)] for t in range(-1, RO + 1)}
+        rest[-1] = []
         for t in range(RO):
-            left = [j for j, o in enumerate(ops) if o.get("name", (0, 0))[:2] == (t, e)]
-            for name in ORDER[e + ("0" if t == 0 else "3" if t == RO - 1 else "")].split():
+            for name in ORDER.get(e + str(t), ORDER.get(e, "")).split():
+                left = rest[t + (name[0] == "+") - (name[0] == "-")]
+                name = name.lstrip("+-")
                 head, tail = (name + "*").split("*")[:2]
-                hit = [j for j in left if ops[j]["name"][2].startswith(head) and ops[j]["name"][2].endswith(tail)]
+                hit = ([j for j in left if ops[j]["name"][2] == name]
+                       or [j for j in left if ops[j]["name"][2].startswith(head) and ops[j]["name"][2].endswith(tail)])
                 for j in hit:
                     left.remove(j)
                     if prev is not None:
@@ -836,7 +832,7 @@ def rank_program(g, core, T, topo):
                 known[key] = place[i]
                 for k, p in ops[i]["knew"].items():
                     known[k] = max(known.get(k, -1), p)
-        o["knew"] = dict(known) if CFG["transitive"] else {}
+        o["knew"] = dict(known)
     cnt = {"v": 0, "a": 0, "p": 0, "c": 0}
     for j in order:
         o = ops[j]

import numpy as np
from concourse.mybir import AluOpType as Op, ActivationFunctionType as AF

W, E, RO, WIN, ZERO, DUMP = 3072, 256, 4, 3600, 3328, 3344
AT = {"XR": 16, "XO": 16 + WIN}
OFF = 1536.0
GATE = float(2 ** 20)
LOSE = float(2 ** 28)
BF, F32, F16, I32, U16 = "bfloat16", "float32", "float16", "int32", "uint16"
CYC, PE, SEM, GATHER, SCATTER, ISSUE, FLIGHT, START, LINK, HBM = 0.83, 0.42, 100, 1.56, 3.8, 600, 2300, 1800, 55, 220
CALL, PCALL, FIRST = {"v": 75, "a": 40}, 3, 2000
PASSES = 6


def _s1(lg, xg):
    o = []
    for e, lo, hi in lg:
        o.append(("L", e, lo, hi))
        if hi % 64 == 0:
            o.append(("P", hi // 64 - 1))
        if hi % 128 == 0:
            o += [("F", hi // 128 - 1), ("S", hi // 128 - 1), ("R", hi // 128 - 1)]
    return tuple(o + [("X", e, lo, hi) for e, lo, hi in xg])


CFG = {
    "s1": _s1([("a", 0, 64), ("v", 64, 128), ("a", 128, 192), ("a", 192, 224), ("a", 224, 256)],
              [("a", 0, 32), ("a", 32, 64), ("a", 64, 112), ("v", 112, 128), ("a", 128, 192), ("a", 192, 240), ("a", 240, 256)]),
    "s1_0": _s1([("a", 0, 64), ("v", 64, 128), ("a", 128, 192), ("v", 192, 256)],
                [("a", 0, 64), ("v", 64, 96), ("a", 96, 128), ("a", 128, 192), ("a", 192, 240), ("a", 240, 256)]),
    "sc": ((0, 64), (64, 128), (128, 192), (192, 240), (240, 256)),
    "parts": (((192, 256, (("v", 192, 224), ("a", 224, 256))), (128, 192, (("a", 128, 192),)),
               (64, 128, (("v", 64, 80), ("a", 80, 128))), (0, 64, (("a", 32, 64), ("a", 0, 32)))),),
    "vh": ((0, 256),), "kh": ((0, 256),), "yb": ("B2", "B3", "B0", "B1"),
    "lq": "sasa", "pfq": "vava", "pfp": ((0, 128), (128, 256)), "xp": ((0, 160), (160, 256)), "erun": 3, "ttcut": {(3, 1): ((12, 14), (14, 16))},
    "eg": (("v", 0, 32), ("a", 128, 160), ("a", 32, 64), ("a", 160, 192), ("v", 64, 80), ("a", 80, 96), ("a", 192, 224), ("a", 96, 128),
           ("a", 224, 240), ("a", 240, 256)),
    "og": "a", "yp": ((0, 256),), "c9": "a", "c5": "v", "wfirst": False,
    "bk": (("B2", "B2", "B0", "B0"), ("B4", "B1", "B0", "B3")),
    "eqa1": (11, 12, 13, 14, 15), "eqa2": (10, 11, 12, 13, 14, 15), "eqa3": (10, 11, 12, 13, 14, 15),
    "cuts": (0, 512, 1472, 2304, W), "via": (0, 1), "late": 3, "rz": (1, 0),
}
ORDER = {'v': '-Ns:*<sf GL:1024<PF XR:0<ZE XO:0<ZE SX:0<XO Ns:*<SX XO:0<Ns Rp:0<B1 Rq:0<Rp Lu:0<Lo GX:1792<XO Rp:128<B3 Rq:128<Rp MX:0<RS0 MN:0<RS1 XR:0<Nr MN:1024<RS1 MX:1024<RS0 MN:2048<RS1 MX:2048<RS0 MN:3072<RS1 MX:3072<RS0 MN:3840<RS1 MX:3840<RS0 YS:0<G G:0<YS sf:0<G qs:*<sf XR:0<Ys EG:3072<XR MG:3072<EG MG:3080<EG EG:1024<XR MG:2048<EG MG:2056<EG MG:1024<EG MG:1032<EG MG:512<EG MG:520<EG MG:0<EG MG:8<EG RI:0<B6 FN:0<B6 C5:0<FN XO:0<Yr KS:0<RS0 si:32<KS su:32<si SB:256<TT si:64<si SB:0<TT MM:0<TT E2:0<TB E2:272<TB E2:544<TB E2:816<TB E2:1088<TB E2:1360<TB E2:1632<TB E1:0<TB E2:1904<TB E2:2176<TB E1:272<TB E1:544<TB E1:816<TB E2:2448<TB E1:1088<TB E1:1360<TB E1:1632<TB E1:1904<TB E1:2176<TB su:48<sf E1:2448<TB E1:2720<TB Ru:0<Ro PT:0<PF sf:208<B4 pl:0<sf sf:192<B3 ws:*<sf PF:0<PT sf:208<sf', 'a': 'GL:0<PF GL:2048<PF FR:0<B0 GL:3072<PF GL:3584<PF SU:0<B1 N2:0<B1 Lo:0<B0 FR:128<B2 Lo:128<B2 SU:256<B3 N2:128<B3 GX:0<XO GX:512<XO GX:1024<XO GX:2048<XO GX:3072<XO OG:0<XR GX:3840<XO OR:0<B4 Y16:0<B5 Ys:*<Y16 Yd:0<Y16 JG:0<J U:0<B7 EG:3584<XR EG:2048<XR EG:1280<XR sy:0<B4 EG:512<XR EG:0<XR C2:0<B1 SG:0<B7 RH:0<RI C9:0<FN DL:0<B0 NL:16<si TB:0<B0 NL:0<si sf:112<B4 E2:2720<TB E2:2992<TB E2:2720<E2 TB:256<B3 E2:3264<TB sf:160<B1 E2:2992<E2 E2:3536<TB E1:2992<TB E2:3808<TB E2:3264<E2 E2:3536<E2 E2:3808<E2 E1:2992<E1 E1:3264<TB E1:3536<TB sf:96<B1 E2:4080<TB E1:3264<E1 E1:3536<E1 E2:4080<E2 E1:3808<TB E1:4080<TB E1:3808<E1 E1:4080<E1 sf:128<si Ro:0<B7 LN:0<B6 C1:0<TS LW:0<B5 EV:0<XR', 'p': "B0:0<GL B0:64<GL B2:0<GL B1:0<FR B2:64<GL B1:384<FR B3:0<FR B3:384<FR B4:0<OG B1:0<OD B1:0<MX B1:240<MX B5:0<MX B5:240<MX B7:256<OR B4:256<Yd B2:0<Yd B5:0<KC B7:0<Ro B1:256<CT B5:192<EG B7:256<Lo B3:0<Yd B6:192<MG B5:128<EG B2:0<Yd' B6:128<MG B3:0<Yd' B6:64<MG B6:0<sy B6:0<MG B5:64<EG B5:0<EG B6:0<TH B5:0<RH B0:256<Lo B7:0<Ro' B0:0<SB B4:448<SB B3:256<SB B5:0<TH B1:464<SB B7:0<MM B6:64<E2 B6:16<E2 B6:176<E2 B6:224<E2 B4:320<RS0 B6:112<E2 B5:16<E1 B4:336<sf B6:160<E2 B6:0<E2 B5:192<E1 B5:64<E1 B5:240<E1 B5:112<E1 B3:0<sf B5:160<E1 B5:0<E1 B4:336<LN B3:0<LW +B1:0<ZE +B3:0<ZE"}


def _e(n, lo, hi):
    return "".join("%s:%d< " % (n, 272 * b) for b in range(lo, hi))


_SC = "MX:0< Rq:128 MN:0< MX:1024 MN:1024 XR:0<Nr MX:2048 MN:2048 MX:3072 MN:3072 MX:3840 MN:3840 "
_V1 = "-XO:0<Yr' -Ns*<sf GL:1024 GL:3584 XO:0<ZE SX Ns*<SX XR:0<Ns Rp:0< Rq:0< GX Rp:128 " + _SC
_V0 = "OH O3 PF:0<PI GL:1024 Ro:0<Ru GL:3072 PF:768 Rp:0< Rq:0< GX PF:1536 Rp:128 " + _SC
_V2 = ("Lu YS G:0<YS sf:0< qs XR:0<Ys EG:0< EG:1024 MG:0< MG:2048 MG:512 MG:2560 MG:1024 MG:3072 MG:1536 MG:3584 MG:3840 "
       "RI FN C5 XO:0<Yr KS si:32 su:32 ")
_V3 = "SB:256 SB:0< MM " + _e("E2", 0, 11) + _e("E1", 0, 4) + "su:48 " + _e("E1", 4, 10) + "sf:208<B4 PT pl Ru PF:0<PT sf:192 sf:208<sf ws PF:0<PT' sf:224"
_V4 = "SB:0< SB:256 MM " + _e("E1", 0, 10) + _e("E2", 0, 7) + "sf:192 su:48 ws " + _e("E2", 7, 11) + "XO:0<Yr' sf:208<B4 sf:208<sf Ns*<sf"
_A1 = "GL:0< GL:2048 FR:0< GL:3072 SU:0< Lo:0< FR:128 Lo:128 SU:256 GX:0< GX:1024 GX:2048 GX:3072 OG GX:3840 OR "
_A0 = "GL:0< GL:2048 FR:0< SU:0< Lo:0< FR:128 Os SU:256 GX:0< Lo:128 GX:1024 GX:2048 GX:3072 OG GX:3840 OR "
_A2 = "Y16 Ys Yd U JG EG:2048 sy EG:512 EG:2560 EG:1280 EG:3072 EG:1536 EG:3584 EG:3840 SG:0<B7 PF:2304 RH C9 DL C2 "
_A3 = "sf:128 TB:0< sf:112 TB:256 E2*<TB sf:160 E2*<E2 sf:96 E1*<TB NL:0< LN E1*<E1 C1 Ro LW:0<B5 sf:16< EV"
_A4 = "TB:256 sf:160 E1*<TB E1*<E1 sf:112 TB:0< LW sf:96 E2*<TB RS E2*<E2 NL LN EV"
_P0 = "B0:0<GL B0:64<GL B1:0<FR B2:0<GL B2:64<GL B1:384 B7:0<XO B3:0<FR B3:384 B1:0<OD B7:0<Lo B7:64<Lo B7:128<Lo B7:192<Lo B4:0<Os B4:0<OG "
_P1 = "B0:0<GL B0:64<GL B2:0<GL B1:0<FR B2:64<GL B1:384 B3:0<FR B3:384 B1:0<OD B7:0<Lo B7:64<Lo B7:128<Lo B7:192<Lo B4:0<OG "
_P2 = ("B1:0<MX B1:0<OR B1:240<MX B5:0<MX B5:240<MX B5:0<KC B7:256<OR B2:0<Yd B4:256 B3:0<Yd B7:0<Ro B7:256<Lo B0:0<Yd B1:0<Yd "
       "B6:0<sy B6:0<MG B6:1<MG B5:0<EG B6:0<MG' B5:1<EG B6:1<MG' B5:0<EG' B6:0<MG'' B5:1<EG' B6:1<MG'' B5:0<EG'' "
       "B6:0<MG''' B5:1<EG'' B6:1<MG''' B6:1<MG'''' B5:0<EG''' B5:1<EG''' B5:1<EG'''' B0:256 B5:0<RH B5:0<C5 B5:0<C9 B7:0<Ro' B1:256 ")
_P3 = ("B6:0<TH B5:0<TH B0:0<SB B4:448 B3:256 B1:464 B7:0<MM B6:16< B6:48 B6:80 B6:192<E2 B6:112 B6:224 B6:144 B6:176 B6:0<E2 B3:0<sf "
       "B5:16< B4:320 B4:336<sf B4:336<LN B5:48 B5:80 B5:176<E1 B5:208 B5:240<E1 B5:112 B5:144 B5:0<E1 B3:0<LW +B1:0<ZL +B3:0<ZL +B6:0<ZE")
_P4 = ("B5:0<TH B6:0<TH B3:256 B1:464 B0:0<SB B4:448 B3:0<sf B5:16< B5:48 B5:176<E1 B5:80 B5:208 B5:240<E1 B5:112 B5:144 B5:0<E1 "
       "B7:0<MM B3:0<LW")
ORDER = {"v": _V1 + _V2 + _V3, "a": _A1 + _A2 + _A3, "p": _P1 + _P2 + _P3,
         "v0": _V0 + _V2 + _V3, "a0": _A0 + _A2 + _A3, "p0": _P0 + _P2 + _P3,
         "v3": _V1 + _V2 + _V4, "a3": _A1 + _A2 + _A4, "p3": _P1 + _P2 + _P4}
_X = [("a", 0, 32), ("v", 32, 64), ("a", 64, 128), ("a", 128, 192), ("a", 192, 240), ("a", 240, 256)]
CFG.update(s1=_s1([("a", 0, 64), ("v", 64, 128), ("a", 128, 192), ("a", 192, 224), ("v", 224, 256)], _X),
           s1_0=_s1([("a", 0, 64), ("v", 64, 128), ("a", 128, 192), ("v", 192, 256)], _X),
           eqa1=tuple(range(10, 16)), eqa2=tuple(range(11, 16)), eqa3=tuple(range(10, 16)), erun=2, pfp=((0, 160), (160, 256)), pfq="vvva")


def _s(n, d):
    return ("sbuf", [128] + (n if isinstance(n, list) else [n]), d)


SCRATCH = {
    "XX": _s(16 + 2 * WIN, BF), "ml": _s(32, U16), "PI": _s(W, I32), "PF": _s(WIN, F32),
    "rds": _s(E, I32), "zs": _s(E, BF),
    "GL": _s(4096, F16), "GX": _s(4096, BF), "MX": _s(4096, BF), "MN": _s(4096, BF),
    "EG": _s(4096, F16), "MG": _s(4096, F16), "QM": _s(512, BF), "KS": _s(E, I32), "YS": _s(E, I32), "G": _s(E, I32), "KB": _s(E, BF),
    "Y16": _s(E, F16), "Yd": _s(E, BF), "sy": _s(16, F16), "X0": _s(512, BF),
    "E1": _s([16, 272], BF), "E2": _s([16, 272], BF),
    "Ro": _s(E, F16), "Ru": _s(E, U16), "Lo": _s(E, F16), "Lu": _s(E, U16),
    "OD": _s(E, BF), "pl": _s(16, U16), "Rp": _s(E, F32), "Rq": _s(E, U16),
    "FR": _s(E, BF), "SU": _s(512, F32), "ZL": _s(512, BF), "OG": _s(E, BF), "OR": _s(E, BF), "Os": _s(32, BF), "U": _s(E, BF),
    "DL": _s(E, F32), "JG": _s(E, BF), "C1": _s(E, F32), "C2": _s(E, F32), "C9": _s(E, BF), "C5": _s(E, BF),
    "RI": _s(E, I32), "FN": _s(E, BF), "SB": _s(512, F16), "TB": _s(2 * E, F16),
    "EV": _s(E, BF), "MM": _s(E, F32), "LW": _s(E, BF), "LN": _s(E, BF), "SG": _s(512, BF),
    "PT": _s(E, F32), "SX": _s(E, F32), "RS": _s(E, F16), "rh": _s(E, F16), "rr": _s(E, F32), "zr": _s(E, BF),
    "sf": _s(256, F32), "si": _s(128, I32), "su": _s(128, U16),
    "Ys": _s(RO * E, BF), "Yr": _s([RO, E], BF), "Ns": _s([RO, 288], U16), "Nr": _s([RO, 272], U16),
    "qs": _s(RO * 32, U16), "qr": _s(RO * 16, U16), "ws": _s(RO * 16, U16), "wr": _s(RO * 16, U16),
    "COL": _s(E, F32), "XK": _s(272, BF), "IO": _s(E, F32), "IK": _s(E, BF), "pi": _s(16, I32), "pc": _s(16, F32),
    "MK": _s(80, F32), "AD": _s(272, BF), "OH": _s([16, 128], BF), "RH": _s(E, F16), "NL": _s(32, BF), "O3": _s([16, 128], BF), "DG": _s(2048, BF),
    "MB": _s(128 * 18, BF), "MF": _s(128 * 4, F32), "RS0": _s(1024, BF), "RS1": _s(1024, BF),
    "KC": _s(E, BF), "C21": _s(E, BF), "ZE": _s(512, BF), "ZC": _s(E, BF), "TH": _s(E, BF),
    "CT": _s(E, F16), "TT": _s(5 * 64, F32), "TS": _s(1024, F32), "J": _s(W, BF), "cT": _s(80, F32),
}
for _b in range(8):
    SCRATCH["B%d" % _b] = ("psum", [128, 512], F32)
MSG = ["y", "w", "n"]
SEMAPHORES = (["v", "a", "p", "c", "sent", "left", "gone", "h0", "h1", "h2", "h3", "r_o", "r_rd", "r_z", "r_x", "r_ro", "r_zo"]
              + ["r_%s%d" % (m, t) for m in MSG for t in range(RO)] + ["d%d" % k for k in range(16)])


def rank_program(g, core, T, topo):
    rank = T.rank_of(core)
    N = len(T.cores)
    cuts = CFG["cuts"]
    pieces = list(zip(cuts, cuts[1:]))

    def helper(r, n):
        me, to = T.cores[r], T.cores[(r - 1) % N]
        return [c for c in topo.cores_of(me) if c not in T.cores and topo.die(c) != topo.die(me) and topo.may_write(c, to)][0]

    def spare(r, n):
        me = T.cores[r]
        return topo.mask(me, helper(r, n)) & topo.mask(me, T.cores[(r - 1) % N])

    if rank is None:
        for r in range(N):
            for n in CFG["via"]:
                if helper(r, n) == core:
                    to = T.cores[(r - 1) % N]
                    rid, pid, _ = topo.addr(to)
                    lo, hi = pieces[n]
                    g.wait_ge(T.sem["h%d" % n], spare(r, n).bit_count())
                    g.remote_dma(T.XX[:, AT["XR"] + lo:AT["XR"] + hi], T.XX[:, AT["XO"] + lo:AT["XO"] + hi], T.sem.r_x, T.sem.sent, pid, rid, topo.mask(core, to))
                    if n == CFG["via"][-1]:
                        g.wait_ge(T.sem.sent, len(CFG["via"]) * len(topo.engines(core, to)))
        return
    nxt, prv = T.cores[(rank + 1) % N], T.cores[(rank - 1) % N]
    Q = {"v": g.vector, "a": g.scalar, "p": g.tensor, "c": g, "s": g.sync}
    ops, named = [], set()
    ndma, queued = [0], [0, 0]
    now = [-1]
    late = [False]
    out_cnt = {"sent": 0, "left": 0, "gone": 0}
    S = slice
    ALL = slice(None)

    def v(name, *ix):
        shape = SCRATCH[name][1][1:]
        bits = np.zeros(shape, np.uint8)
        bits[ix] = 1
        mask = int.from_bytes(np.packbits(bits.reshape(-1), bitorder="little").tobytes(), "little")
        return (T[name][(ALL,) + ix], [(name, mask)])

    def label(name, mask):
        lo = (mask & -mask).bit_length() - 1
        if name == "XX":
            name = "XO" if lo >= AT["XO"] else "XR"
            lo = max(0, lo - AT[name])
        return name, lo

    def a(name, lo=0, hi=None, step=1):
        if name in AT:
            return a("XX", AT[name] + lo, AT[name] + (WIN if hi is None else hi), step)
        shape = SCRATCH[name][1]
        if len(shape) > 2:
            n = shape[2]
            hi = shape[1] * n if hi is None else hi
            return v(name, S(lo // n, hi // n), ALL)
        hi = shape[1] if hi is None else hi
        return v(name, S(lo, hi, step) if step > 1 else S(lo, hi))

    def a3(name, r0, r1, lo, hi):
        return v(name, r0 if r1 == r0 + 1 else S(r0, r1), S(lo, hi))

    def ind(win, off):
        return (win[0].indirect(off[0]), win[1], off[1])

    def val(x):
        return x[0] if isinstance(x, tuple) else x

    def op(eng, fn, outs, ins, **kw):
        wr, rd = [], []
        for o in outs:
            wr += o[1]
            if len(o) > 2:
                rd += o[2]
        for i in ins:
            if isinstance(i, tuple):
                rd += i[1] + (i[2] if len(i) > 2 else [])
        d = {"eng": eng, "fn": fn, "wr": wr, "rd": rd, "lat": SEM, "rank": len(ops), "late": late[0]}
        d.update(kw)
        if wr and rd:
            d["name"] = (now[0], eng, "%s:%d<%s" % (label(*wr[0]) + label(*[i for i in ins if isinstance(i, tuple)][0][1][0])[:1]))
            while d["name"] in named:
                d["name"] = d["name"][:2] + (d["name"][2] + "'",)
            named.add(d["name"])
        if "cost" not in d:
            d["cost"] = cost(eng, outs[0], [i for i in ins if isinstance(i, tuple)], kw.get("per", 1.0))
        ops.append(d)

    def width(x):
        return 16 * x[2][0][1].bit_count() if len(x) > 2 else x[1][0][1].bit_count()

    def cost(eng, out, ins, per):
        n = width(out)
        kinds = [SCRATCH[x[1][0][0]] for x in [out] + ins if width(x) == n]
        if eng == "p":
            return PCALL + max(64, n) * PE * (4 if SCRATCH[ins[0][1][0][0]][2] == F32 else 1)
        if eng == "c":
            return 170 + 2 * n * CYC
        if len(out) > 2:
            return 55 + n * SCATTER * CYC
        if any(len(x) > 2 for x in ins):
            return 55 + n * GATHER * CYC
        if per == 0.5 and any(k[2] in (F32, I32) for k in kinds):
            per = 1.0
        if per == 2.0 and any(k[0] == "psum" for k in kinds):
            per = 1.0
        return CALL[eng] + max(64, n * per) * CYC

    def cp(out, in_):
        op("v", lambda: g.vector.tensor_copy(out[0], in_[0]), [out], [in_], per=0.5)

    def tt(out, x, y, o):
        op("v", lambda: g.vector.tensor_tensor(out[0], x[0], y[0], o), [out], [x, y], per=2.0)

    def ts(out, x, s1, o0, s2=None, o1=None):
        if o1 is None:
            op("v", lambda: g.vector.tensor_scalar(out[0], x[0], val(s1), None, o0), [out], [x, s1], per=0.5)
        else:
            op("v", lambda: g.vector.tensor_scalar(out[0], x[0], val(s1), val(s2), o0, o1), [out], [x, s1, s2], per=0.5)

    def scan(out, d0, d1, o0, o1):
        op("v", lambda: g.vector.tensor_tensor_scan(out[0], d0[0], d1[0], 0.0, o0, o1), [out], [d0, d1], per=0.5)

    def ms(out, c):
        op("v", lambda: g.vector.memset(out[0], c), [out], [], per=0.5)

    def act(out, x, f=AF.Identity, bias=0.0, scale=1.0):
        op("a", lambda: g.scalar.activation(out[0], x[0], f, bias=val(bias), scale=val(scale)), [out], [x, bias, scale])

    def mml(trip, st=True, sp=True, alone=0):
        def fn():
            n = int(alone) or len(trip)
            for k, (o, l, r) in enumerate(trip):
                ins = g.tensor.matmul(o[0], l[0], r[0], st and k % n == 0, sp and k % n == n - 1)
            return ins
        op("p", fn, [o for o, l, r in trip], [x for o, l, r in trip for x in (r, l)],
           cost=sum(cost("p", o, [l, r], 1.0) for o, l, r in trip), adds=not (st or sp or alone))

    def mms(out, pairs, st=True, sp=True):
        mml([(out, l, r) for l, r in pairs], st, sp)

    def iota(out, pat, base=0, cm=0, flag=True):
        op("c", lambda: g.iota(out[0], pat, base, cm, allow_small_or_imprecise_dtypes=True) if flag
           else g.iota(out[0], pat, base, cm), [out], [])

    def gcopy(out, in_, n):
        op("c", lambda: g.affine_select(out[0], in_[0], [[0, n]], Op.is_gt, 0.0, 1, 0), [out], [in_])

    def nbytes(x, y):
        name, mask = (x[1] or y[1])[0]
        return 128 * mask.bit_count() * (4 if SCRATCH[name][2] in (F32, I32) else 2)

    def dma(eng, out, in_):
        s = "d%d" % ndma[0]
        ndma[0] += 1
        op(eng, lambda: Q[eng].dma_start(out[0], in_[0]), [out], [in_], sem=s, val=16, cost=60, dma=nbytes(out, in_))

    def send(dst, out, in_, sem):
        rid, pid, _ = topo.addr(dst)
        hop = sem[0] == "h"
        loc = "left" if sem == "r_x" or hop else "gone" if sem == "r_rd" else "sent"
        mask = spare(rank, int(sem[1])) if hop else topo.mask(core, dst)
        out_cnt[loc] += mask.bit_count()
        op("c", lambda: g.remote_dma(out[0], in_[0], T.sem[sem], T.sem[loc], pid, rid, mask), [], [in_],
           remote=loc, cost=ISSUE + (FIRST if sum(out_cnt.values()) == mask.bit_count() else 0), msg="r_x" if hop else sem,
           lat=FLIGHT + (FLIGHT + FIRST if hop else 0) + (nbytes(in_, in_) * (1.4 if hop else 1) + (queued[hop] if now[0] < 0 else 0)) / LINK)
        queued[hop] += nbytes(in_, in_) * (0.3 if hop else 0.8) * (loc == "left")

    def recv(src, bufs, sem):
        srcs = src if isinstance(src, list) else [src] * len(bufs)
        op("x", None, bufs, [], sem=sem, val=sum(len(topo.engines(s, core)) for s in srcs), cost=0, lat=0)

    def gather(eng, out, win, off, bias=None):
        if eng == "a":
            act(out, ind(win, off), bias=bias or 0.0)
        elif bias is None:
            cp(out, ind(win, off))
        else:
            ts(out, ind(win, off), bias, Op.add)

    def hbm(name, lo=None, hi=None):
        return (T[name][:] if lo is None else T[name][:, lo:hi], [])

    def m(buf, k):
        return v(buf, k, ALL) if buf[0] == "O" else a(buf, 128 * k, 128 * k + 128)
    ID, BLK, NTRI, IB, NIB, NBLK, HID, WD, B2, I1536, I255, NID, I12, P1536, BC0, I512, N128, IA = [m("MB", k) for k in range(18)]
    IDf, BLKf, TMPf = [m("MF", k) for k in range(3)]
    pp, pm, gb, nb, npm = [a("pc", k, k + 1) for k in (0, 1, 3, 4, 7)]
    cz, half, p2, lo8 = [a("pc", k, k + 1) for k in range(11, 15)]
    iT, cq, dum2, dum = a("cT", 0, 16), a("cT", 16, 32), a("cT", 48, 80), a("cT", 48, 64)
    TOH, TOC, TOS, TOW = [a("TT", 64 * k, 64 * k + 64) for k in range(4)]
    qf, lw = a("sf", 0, 16), a("sf", 192, 208)
    q0, el, cl, c1l = [a("su", 16 * k, 16 * k + 16) for k in (0, 3, 4, 5)]
    XO, XR, PF = a("XO"), a("XR"), a("PF")
    Lo = a("Lo")
    H = W // 2

    dma("a", a("zs"), hbm("z0"))
    dma("s", a("XO", *pieces[0]), hbm("x0", *pieces[0]))
    dma("a", a("rds"), hbm("rd"))
    for lo, hi in pieces[1:len(pieces) - CFG["late"]]:
        dma("s", a("XO", lo, hi), hbm("x0", lo, hi))
    for k in range(4):
        dma(CFG["lq"][k], a("PI", 768 * k, 768 * k + 768), hbm("lk", 768 * k, 768 * k + 768))
    for lo, hi in pieces[len(pieces) - CFG["late"]:]:
        dma("s", a("XO", lo, hi), hbm("x0", lo, hi))
    iota(a("pi", 0, 1), [[0, 1]], 0, 1, False)
    iota(a("COL"), [[1, 256]])
    iota(a("X0"), [[-4, 4], [1, 128]])
    cp(a("Rq"), a("rds"))
    for n, (lo, hi) in enumerate(pieces):
        if n == CFG["rz"][0]:
            send(nxt, a("Ru"), a("Rq"), "r_rd")
        if n == CFG["rz"][1]:
            send(nxt, a("XO", W, W + E), a("zs"), "r_z")
        if n == len(pieces) - CFG["late"]:
            queued[:] = [0, -FIRST * LINK]
        if n in CFG["via"]:
            send(helper(rank, n), a("XO", lo, hi), a("XO", lo, hi), "h%d" % n)
        elif n < len(pieces) - 1:
            send(prv, a("XR", lo, hi), a("XO", lo, hi), "r_x")
    iota(a("XK"), [[0, 17], [1, 16]])
    iota(a("IO", 0, 64), [[0, 2], [-1, 16], [0, 2]], 15)
    iota(a("IO", 64, 128), [[0, 2], [-1, 16], [-100, 2]], 115)
    iota(a("IO", 128, 192), [[-100, 2], [-1, 16], [0, 2]], 115)
    iota(a("IO", 192, 256), [[-100, 2], [1, 16], [-100, 2]], 200)
    iota(a("IK"), [[0, 16], [-2, 16]], 62)
    iota(a("CT"), [[-12, 256]], W // 2)
    iota(a("pi", 8, 11), [[1, 3]], 0, 1, False)
    iota(a("G"), [[2048, 16], [0, 16]], 0, 0, False)
    iota(a("KB"), [[2048, 16], [0, 16]], -256)
    recv(prv, [a("Ru")], "r_rd")
    recv(prv, [a("XO", W, W + E)], "r_z")
    recv([helper((rank + 1) % N, n) if n in CFG["via"] else nxt for n in range(len(pieces))], [a("XR", lo, hi) for lo, hi in pieces], "r_x")

    ms(a("ZE"), 0.0)
    ts(a("pi", 1, 2), a("pi", 0, 1), 15, Op.bitwise_and)
    cp(a("pc", 0, 2), a("pi", 0, 2))
    c128 = a("COL", 0, 128)
    ts(ID, c128, pp, Op.is_equal)
    ts(a("MK", 0, 16), a("COL", 0, 16), pm, Op.is_equal)
    act(gb, pm, scale=-1.0, bias=pp)
    act(nb, gb, scale=-1.0, bias=-7.5)
    act(TMPf, c128, AF.Abs, bias=nb)
    ts(BLK, TMPf, 8.0, Op.is_lt)
    for k in range(16):
        if k % 2:
            ts(m("DG", k), ID, a("MK", k, k + 1), Op.mult)
        else:
            act(m("DG", k), ID, scale=a("MK", k, k + 1))
    act(IDf, ID)
    act(BLKf, BLK, scale=-1.0)
    for h in range(2):
        act(a("ZL", 256 * h, 256 * h + 128), a("COL", 128 * h, 128 * h + 128))
        act(a("ZL", 256 * h + 128, 256 * h + 256), a("ZE", 0, 128))
    for mat, src, c in ((IB, ID, 4096.0), (NIB, ID, -4096.0), (NBLK, BLK, -4096.0), (HID, ID, 0.5), (I1536, ID, -1536.0),
                        (P1536, ID, 1536.0), (I512, ID, 512.0), (I255, ID, 255.0), (NID, ID, -1.0), (I12, ID, 12.0),
                        (B2, BLK, 2 * LOSE), (N128, ID, 128.0), (IA, ID, GATE)):
        act(mat, src, scale=c)
    op("c", lambda: g.affine_select(NTRI[0], NBLK[0], [[1, 128]], Op.is_gt, 0.0, 0, -1), [NTRI], [NBLK])
    act(cz, a("MK", 1, 2), scale=float(W))
    act(a("ZC"), a("COL"), scale=a("MK", 0, 1), bias=cz)
    act(a("MK", 48, 52), a("COL", 0, 4), bias=gb)
    ts(a("pi", 2, 3), a("pi", 1, 2), 1, Op.logical_shift_right)
    ts(a("pi", 3, 4), a("pi", 1, 2), 1, Op.bitwise_and)
    act(a("MK", 52, 53), a("pi", 2, 3), bias=gb)
    for h in range(2):
        act(a("MK", 53, 54), a("pi", 3, 4), AF.Abs, scale=1000.0, bias=-1000.0 * h)
        act(a("MK", 54, 55), a("MK", 53, 54), bias=a("MK", 52, 53))
        act(a("MK", 56 + 2 * h, 58 + 2 * h), a("COL", 0, 2), scale=8.0, bias=a("MK", 54, 55))
    for k in range(4):
        ts(m("QM", k), a("X0", 0, 128), a("MK", 56 + k, 57 + k), Op.is_equal)
    act(a("MK", 55, 56), pm, scale=16.0)
    ts(a("su", 96, 112), a("COL", 0, 16), a("MK", 55, 56), Op.add)
    now[0] = 0
    for k in range(4):
        ts(v("OH", S(k, 16, 4), ALL), a("X0"), a("MK", 48 + k, 49 + k), Op.is_equal)
    for k in range(2):
        ts(a("O3", 1024 * k, 1024 * k + 1024), a("OH", 1024 * k, 1024 * k + 1024), -64.0, Op.mult)
    now[0] = -1
    ms(a("XO", ZERO, WIN), 0.0)
    ms(a("XX", 0, 16), -512.0)
    ms(a("XR", W + 16, WIN), 0.0)
    act(lo8, pm, AF.Sign, scale=-1.0, bias=5.5)
    act(lo8, lo8, scale=128.5, bias=126.5)
    act(a("XR", W, W + 16), a("ZE", 0, 16), bias=lo8)
    ms(a("RS0"), 1.0)
    ms(a("RS1"), 0.0)
    ms(a("RS0", 0, 1024, 16), 0.0)
    ms(a("RS1", 0, 1024, 16), 512.0)
    act(iT, a("COL", 0, 16), scale=16.0, bias=pm)
    act(half, pm, scale=12.0)
    act(cq, a("COL", 0, 16), scale=192.0 - 2048.0, bias=half)
    act(a("cT", 48, 64), iT, bias=DUMP - OFF)
    act(a("cT", 64, 80), iT, bias=DUMP - OFF)
    act(half, a("MK", 0, 1), scale=0.5)
    act(BC0, BLK, scale=half)
    act(npm, pm, scale=-8192.0)
    act(a("AD"), a("XK", 0, 272), AF.Abs, scale=8192.0, bias=npm)
    act(a("OD"), a("AD", 0, E), scale=-1.0, bias=-0.25)
    act(a("C21"), a("ZE", 0, E), bias=2.0 ** 19 - GATE * ((CFG["c9"] == "v") + (CFG["c5"] == "v")))
    act(a("KC"), a("IK"), bias=0.5 * (CFG["c9"] == "a"))
    late[0] = True
    act(a("SG", 0, 256), a("RS0", 0, 256), scale=0.5)
    act(a("LW"), a("RS1", 0, 256), scale=-LOSE / 256)
    ts(a("TT", 0, 256), a("IO", 0, 256), pm, Op.is_equal)
    act(a("IO", 0, 64), TOS, scale=-4096.0 - OFF, bias=OFF)
    act(a("IO", 64, 128), TOW, scale=8192.0)
    tt(a("TT", 193, 256), a("IO", 1, 64), a("IO", 65, 128), Op.add)
    act(a("TT", 192, 193), a("ZE", 0, 1), bias=OFF + 1024.0)
    act(a("NL", 16, 32), a("ZE", 0, 16), bias=4.0)
    now[0] = 0
    scan(a("TH"), a("SG", 0, 256), a("LW"), Op.mult, Op.add)
    tt(a("MK", 16, 32), a("TH", 0, 16), a("MK", 0, 16), Op.mult)
    op("a", lambda: g.scalar.activation(T.MK[:, 64:80], T.MK[:, 16:32], AF.Identity, scale=-0.5, accum_out=p2[0]),
       [a("MK", 64, 80), p2], [a("MK", 16, 32)])
    act(WD, BLK, scale=p2)
    now[0] = -1
    act(a("MK", 32, 48), a("MK", 0, 16), bias=-0.5)
    ts(a("pi", 12, 15), a("pi", 8, 11), 15, Op.bitwise_and)
    act(a("pc", 8, 11), a("pi", 12, 15), scale=64.0, bias=-OFF)
    now[0] = 0
    for k in range(16):
        act(a("TS", 64 * k, 64 * k + 64), TOS, AF.Sign, bias=a("MK", 32 + k, 33 + k))
    act(a("PF", W, W + 272), a("ZE", 0, 272))
    act(a("PF", W + 272, WIN), a("ZE", 0, WIN - W - 272))
    late[0] = False
    ts(a("Ro"), a("Ru"), -OFF, Op.add)
    now[0] = 0
    mms(a("B7", 0, 16), [(m("OH", k), a("XO", 12 * k, W, 192)) for k in range(16)])
    act(a("Os", 0, 16), a("B7", 0, 16))
    send(prv, a("Os", 16, 32), a("Os", 0, 16), "r_o")
    now[0] = -1
    send(prv, a("XR", *pieces[-1]), a("XO", *pieces[-1]), "r_x")
    iota(a("J"), [[0, E], [1, 12]])
    ops[-1]["behind"] = len(ops) - 2
    recv(nxt, [a("Os", 16, 32)], "r_o")

    def to_list(out, src, base, lo, hi, st=True, sp=True):
        mms(out, [(m("OH", k), a(src, base + lo + k, base + hi, 16)) for k in range(16)], st, sp)

    def cols(bank, r, lo, hi):
        return a(bank, 16 * r + lo, 16 * r + hi)

    behind = {}

    def follow(line):
        if line in behind:
            ops[-1]["behind"] = behind[line]
        behind[line] = len(ops) - 1

    def own_update(t):
        recv(prv, [a("wr", 16 * t, 16 * t + 16)], "r_w%d" % t)
        cp(ind(XO, a("wr", 16 * t, 16 * t + 16)), a("ZE", 0, E))
        xl = a3("Ns", t, t + 1, 256, 272)
        tt(a("SX"), ind(XO, xl), a("EV"), Op.add)
        nw = a3("Ns", t, t + 1, 0, E)
        ts(nw, a("SX"), 0.5, Op.mult, -0.25, Op.add)
        if t < RO - 1:
            send(prv, a3("Nr", t, t + 1, 0, 272), a3("Ns", t, t + 1, 0, 272), "r_n%d" % t)
            cp(ind(a("XX", AT["XR"], AT["XO"] + WIN), a3("Ns", t, t + 1, 272, 288)), nw)
        else:
            cp(ind(XO, xl), nw)

    def pairs(Eb, base, col, bank, on_a, b0, b1):
        if b1 == 16:
            mms(a(bank, 0, 256), [(ID, a("TH"))], True, False)
        for b in range(b0, b1):
            e, src, me = a3(Eb, b, b + 1, 0, 256 - 16 * b), a("TB", base + 16 * b, base + E), a("sf", col + b, col + b + 1)
            if b in on_a:
                act(e, src, AF.Abs, bias=me, scale=-1.0)
                follow("a1")
                act(e, e, AF.Relu, bias=1.0, scale=-1.0)
                follow("a2")
            else:
                ts(e, src, me, Op.is_equal)
                follow("v")
        behind.clear()
        runs = [[b for b in range(b0, min(b1, 15)) if (b in on_a) == f] for f in (False, True)]
        for run in [r[k:k + CFG["erun"]] for r in runs for k in range(0, len(r), CFG["erun"])]:
            mml([(a(bank, 16 * b + 16, 256), B2, a3(Eb, b, b + 1, 16, 256 - 16 * b)) for b in run], False, False)
        mms(a(bank, 16 * b0, 16 * b1), [(WD, v(Eb, S(b0, b1), S(0, 16)))], False, b0 == 0)

    for t in range(RO):
        last = t == RO - 1
        now[0] = t
        Y = a("Ys", E * t, E * t + E)
        locks = a("PI") if t == 0 else PF

        def lk_open(h):
            bs = "B%d" % (2 * h + 1)
            mml([(a(bs, 0, 256), ID, a("ZL", 256 * h, 256 * h + 256)), (a(bs, 0, 128), NID, a("Ro", 128 * h, 128 * h + 128)),
                 (a(bs, 128, 256), ID, a("Ro", 128 * h, 128 * h + 128))], True, False)

        def lk_gather(eng, lo, hi):
            gather(eng, a("GL", 16 * lo, 16 * hi), locks, a("Ru", lo, hi), -OFF)

        def lk_pick(c):
            mms(a("B%d" % (c // 2 * 2), 64 * (c % 2), 64 * (c % 2) + 64),
                [(m("DG", k), a("GL", 1024 * c + k, 1024 * c + 1024, 16)) for k in range(16)])

        def lk_free(h):
            bl, bs, fr = "B%d" % (2 * h), "B%d" % (2 * h + 1), a("FR", 128 * h, 128 * h + 128)
            act(fr, a(bl, 0, 128), AF.Relu, bias=-1535.0)
            mml([(a(bs, 0, 128), IB, fr), (a(bs, 0, 128), NTRI, fr), (a(bs, 128, 256), IB, fr)], False)
            act(a("Lo", 128 * h, 128 * h + 128), a(bl, 0, 128))

        def lk_first(h):
            bl, bs, fr = "B%d" % (2 * h), "B%d" % (2 * h + 1), a("FR", 128 * h, 128 * h + 128)
            act(a("SU", 256 * h, 256 * h + 256), a(bs, 0, 256), AF.Relu, bias=OFF - 4096.0)
            mms(a(bs, 384, 512), [(NIB, fr), (BLK, a("ZC", 128 * h, 128 * h + 128)), (BLKf, a("SU", 256 * h, 256 * h + 128))])

        def lk_list(h):
            tt(a("Rp", 128 * h, 128 * h + 128), a("B%d" % (2 * h + 1), 384, 512), a("SU", 256 * h + 128, 256 * h + 256), Op.max)
            cp(a("Rq", 128 * h, 128 * h + 128), a("Rp", 128 * h, 128 * h + 128))

        def cells(eng, lo, hi):
            gather(eng, a("GX", 16 * lo, 16 * hi), XO, a("Rq", lo, hi))

        ql = q0 if t == 0 else a("qs", 32 * t - 32, 32 * t - 16)
        lk_open(0)
        lk_open(1)
        if t > 0:
            own_update(t - 1)
        else:
            for k in range(4):
                (cp if CFG["pfq"][k] == "v" else act)(a("PF", 768 * k, 768 * k + 768), a("PI", 768 * k, 768 * k + 768))
        steps = {"L": lk_gather, "X": cells, "P": lk_pick, "F": lk_free, "S": lk_first, "R": lk_list}
        for st in CFG["s1_0" if t == 0 else "s1"]:
            steps[st[0]](*st[1:])
        if t > 0:
            recv(nxt, [a3("Nr", t - 1, t, 0, 272)], "r_n%d" % (t - 1))
            cp(ind(XR, a3("Nr", t - 1, t, 256, 272)), a3("Nr", t - 1, t, 0, E))
        for lo, hi in CFG["sc"]:
            n = 16 * (hi - lo)
            scan(a("MX", 16 * lo, 16 * hi), a("RS0", 0, n), a("GX", 16 * lo, 16 * hi), Op.mult, Op.max)
            scan(a("MN", 16 * lo, 16 * hi), a("RS1", 0, n), a("GX", 16 * lo, 16 * hi), Op.add, Op.min)
        for h in range(2):
            for l0 in (0, 8):
                mml([(a("B7", 128 * h + 8 * l, 128 * h + 8 * l + 8), m("QM", 2 * h + s), a("Lo", 16 * s + l, E, 32))
                     for l in range(l0, l0 + 8) for s in range(2)], alone=2)
        ts(a("Lu"), a("B7", 0, E), OFF, Op.add)
        if t > 0:
            gather(CFG["og"], a("OG"), XR, ql)
        else:
            mml([(a("B4", k, E, 16), m("DG", k), a("Os", 16, 32)) for k in range(16)], alone=True)
            act(a("OG"), a("B4", 0, E))
        mms(a("B4", 0, 256), [(BLK, a("OG"))])
        act(a("OR"), a("B4", 0, 256), AF.Relu, bias=1.0, scale=-1.0)

        for (l0, l1), (b1, b5) in zip(CFG["yp"], (("B1", "B5"), ("B6", "B0"))):
            mms(a(b1, l0, l1), [(ID, a("OD", l0, l1)), (ID, a("KB", l0, l1))], True, False)
            mms(a(b1, l0, l1), [(I512, a("OR", l0, l1))], False, False)
            cut = max([lo for lo, hi in CFG["sc"] if l0 <= lo < l1])
            for lo, hi in ((l0, cut), (cut, l1))[l0 == cut:]:
                mx, mn = a("MX", 16 * lo + 15, 16 * hi, 16), a("MN", 16 * lo + 15, 16 * hi, 16)
                mms(a(b1, lo, hi), [(BC0, mx), (BC0, mn)], False, hi == l1)
                mms(a(b5, lo, hi), [(HID, mx), (HID, mn)])
            act(a("Y16", l0, l1), a(b5, l0, l1), bias=1023.75)
            act(a("Ys", E * t + l0, E * t + l1), a("Y16", l0, l1), bias=-1024.0)
            scan(a("YS", l0, l1), a("G", l0, l1), a(b1, l0, l1), Op.max, Op.max)
            ts(a("G", l0, l1, 16), a("YS", l0 + 15, l1, 16), 0xFE07, Op.bitwise_and)
            tt(a("sf", l0 // 16, l1 // 16), a("G", l0, l1, 16), a("cT", 16 + l0 // 16, 16 + l1 // 16), Op.add)
            cp(a("qs", 32 * t + l0 // 16, 32 * t + l1 // 16), a("sf", l0 // 16, l1 // 16))
            cp(ind(XR, a("qs", 32 * t + l0 // 16, 32 * t + l1 // 16)), a("Ys", E * t + l0, E * t + l1))
        act(a("Yd"), ind(Y, a("su", 96, 112)), bias=-128.0)
        ql = a("qs", 32 * t, 32 * t + 16)
        send(nxt, a3("Yr", t, t + 1, 0, E), Y, "r_y%d" % t)
        send(nxt, a("qr", 16 * t, 16 * t + 16), ql, "r_y%d" % t)
        if last:
            send(prv, a("zr"), Y, "r_zo")
        else:
            gcopy(a("XO", W, W + E), Y, E)
            ops[-1]["behind"] = len(ops) - 2
        mms(a("B4", 256, 272), [(m("OH", k), a("Yd", 16 * k, 16 * k + 16)) for k in range(16)])
        act(a("sy"), a("B4", 256, 272), scale=-1.0)
        mms(a("B7", 256, 512), [(I255, a("OR", 0, 256)), (NID, Y)])
        act(a("U"), a("B7", 256, 512), AF.Abs)
        mms(a("B7", 0, 256), [(ID, a("Ro")), (I12, a("U"))])
        mms(a("B7", 256, 512), [(ID, Lo), (I12, a("U"))])
        act(a("SG"), a("B7"), AF.Sign, bias=-1534.5)
        mms(a("B7", 0, 256), [(ID, a("Ro")), (I12, a("U")), (I1536, a("SG", 0, 256))], True, False)

        mms(a("B6", 0, E), [(ID, a("ZE", 0, E))], True, False)
        mml([(a("B6", k, E, 16), ID, a("sy")) for k in range(16)], False, False)
        mms(a("B5", 0, E), [(ID, a("KC")), (ID, a("C21"))], True, False)

        def chunk(c, bs, bk):
            by = CFG["yb"][c]
            mml([(a(by, r, 512, 8), ID, a("Yd", 64 * c, 64 * c + 64)) for r in range(8)], alone=True)
            for h in range(2):
                for l0, l1 in CFG["ttcut"].get((c, h), ((4 * c, 4 * c + 4),)):
                    lo, hi = 2048 * h + 128 * l0, 2048 * h + 128 * l1
                    tt(a("MG", lo, hi), a("EG", lo, hi), a(by, 128 * l0 - 512 * c, 128 * l1 - 512 * c), Op.max)
                    for bank, mats, src in ((bk, "O3", "EG"), (bs, "OH", "MG")):
                        mms(a(bank, h, E, 2), [(m(mats, s), a(src, 2048 * h + 128 * s, 2048 * h + 128 * s + 128)) for s in range(l0, l1)],
                            False, (src, h, l1) == ("MG", 1, 16))

        def verdict(lo, hi, bs, bk):
            b0, b1 = lo // 16, hi // 16
            for l0, l1 in CFG["vh"]:
                ts(a("RI", l0, l1), a(bs, l0, l1), -17 / 32, Op.add, 0.0, Op.max)
            for l0, l1 in CFG["vh"]:
                tt(a("FN", l0, l1), a(bs, l0, l1), a("RI", l0, l1), Op.subtract)
            act(a("RH", lo, hi), a("RI", lo, hi), bias=-2048.0)
            mms(a(bk, lo, hi), [(N128, a("RH", lo, hi))], False, False)
            for l0, l1 in CFG["vh"]:
                act(a("C9", l0, l1), a("FN", l0, l1), AF.Sign, bias=-8.5 / 16)
                ts(a("C5", l0, l1), a("FN", l0, l1), 4.5 / 16, Op.is_lt, 2.0, Op.mult)
                mms(a(bk, l0, l1), [(IA, a("C5", l0, l1))], False, False)
                mms(a(bk, l0, l1), [(IA, a("C9", l0, l1)), (HID, a("C9", l0, l1))], False, l1 == hi)
            for l0, l1 in CFG["kh"]:
                scan(a("KS", l0, l1), a("RS0", 0, l1 - l0), a(bk, l0, l1), Op.mult, Op.max)
                ts(a("si", 32 + l0 // 16, 32 + l1 // 16), a("KS", l0 + 15, l1, 16), 63, Op.bitwise_and)
                cp(a("su", 32 + l0 // 16, 32 + l1 // 16), a("si", 32 + l0 // 16, 32 + l1 // 16))
            cu = a("su", 32 + b0, 32 + b1)

            def targets():
                tt(a("SB", E + lo, E + hi), ind(TOH, cu), a("Ro", lo, hi), Op.mult)
                mms(a(bt, lo, hi), [(BLK, a("SB", E + lo, E + hi))])
                act(a("TB", lo, hi), a(bt, lo, hi))
                to_list(cols(lt, 28, b0, b1), "SB", E, lo, hi)
                act(a("sf", 112 + b0, 112 + b1), cols(lt, 28, b0, b1))
                pairs("E2", 0, 112, "B6", CFG["eqa2"], b0, b1)

            def wiped():
                tt(a("SB", lo, hi), ind(TOW, cu), a("Lo", lo, hi), Op.max)
                mms(a(bw, E + lo, E + hi), [(BLK, a("SB", lo, hi))])
                act(a("TB", E + lo, E + hi), a(bw, E + lo, E + hi), bias=-15 * OFF)
                to_list(cols(lx, 29, b0, b1), "SB", 0, lo, hi)
                act(a("sf", 160 + b0, 160 + b1), cols(lx, 29, b0, b1), bias=-15 * OFF)
                act(a("sf", 96 + b0, 96 + b1), cols(lx, 29, b0, b1), bias=-15 * OFF - 8192.0 + AT["XR"])
                act(a("NL", b0, b1), a("sf", 96 + b0, 96 + b1), AF.Abs, scale=8.0)
                pairs("E1", E, 160, "B5", CFG["eqa3" if last else "eqa1"], b0, b1)
            lt, lx, bt, bw = CFG["bk"][lo == 0]
            for f in (wiped, targets) if last or CFG["wfirst"] else (targets, wiped):
                f()
            tt(a("MM", lo, hi), ind(TOC, cu), a("DL", lo, hi), Op.mult)
            mms(a("B7", lo, hi), [(IDf, a("MM", lo, hi))], False, lo == 0)

        for eng, lo, hi in CFG["eg"]:
            gather(eng, a("EG", 16 * lo, 16 * hi), XR, a("Lu", lo, hi), 0.0625 - 128.0)
        for c in range(4):
            chunk(c, "B6", "B5")
        mms(a("B0", 256, 512), [(ID, Lo), (NID, a("Ro")), (I1536, a("SG", 256, 512)), (P1536, a("SG", 0, 256))])
        act(a("DL"), a("B0", 256, 512))
        if not last:
            act(a("JG"), ind(a("J"), ql))
            mms(a("B1", 256, 512), [(ID, a("CT")), (NID, a("AD", t, t + E)), (NID, a("JG"))])
            act(a("C2"), a("B1", 256, 512), AF.Relu, bias=OFF)
        verdict(0, E, "B6", "B5")
        cd = a("si", 32, 48)

        def wipes():
            act(a("LW"), a("B5", 0, 256), AF.Relu)
            mms(a("B3", 0, 16), [(IDf, a("sf", 160, 176))], True, False)
            to_list(a("B3", 0, 16), "LW", 0, 0, E, False)
            tt(lw, a("B3", 0, 16), dum, Op.min)
            wl = a("ws", 16 * t, 16 * t + 16)
            ts(wl, lw, OFF, Op.add)
            send(nxt, a("wr", 16 * t, 16 * t + 16), wl, "r_w%d" % t)

        def winners():
            act(a("LN"), a("B6", 0, 256), AF.Relu)
            mms(a("B4", 320, 336), [(NIB, a("NL", 16, 32)), (ID, a("NL", 0, 16))])
            mms(a("B4", 336, 352), [(IDf, a("sf", 112, 128))], True, False)
            to_list(a("B4", 336, 352), "LN", 0, 0, E, False)
        for f in (wipes, winners) if last or CFG["wfirst"] else (winners, wipes):
            f()
        if last:
            act(a("RS"), a("B7", 0, 256), bias=1.0 - OFF)
            send(prv, a("rh"), a("RS"), "r_ro")
        if not last:
            act(a("sf", 128, 144), cd, bias=a("pc", 8 + t, 9 + t))
        ts(a("su", 48, 80 if last else 96), a("sf", 96, 128 if last else 144), OFF, Op.add, W + 15.0, Op.min)
        act(a("EV"), ind(a("XX", 0, AT["XO"]), el))
        if not last:
            act(a("Ro"), a("B7", 0, 256), bias=1.0 - OFF)
            act(a("C1"), ind(a("TS"), c1l), bias=1536.0, scale=1536.0)
            tt(a("PT"), ind(PF, cl), a("C1"), Op.max)
            ts(a("Ru"), a("Ro"), OFF, Op.add)
        tt(a("sf", 208, 240), a("B4", 320, 352), dum2, Op.min)
        if not last:
            ts(a("pl"), a("sf", 224, 240), OFF, Op.add)
            for lo, hi in CFG["pfp"]:
                tt(ind(PF, a("pl", lo // 16, hi // 16)), a("PT", lo, hi), a("C2", lo, hi), Op.subtract)
        tt(a("sf", 208, 224), a("sf", 208, 224), a("sf", 224, 240), Op.max)
        if not last:
            act(a("sf", 16, 32), a("sf", 208, 224), bias=float(WIN))
            tt(a("sf", 224, 240), a("B3", 0, 16), a("sf", 16, 32), Op.min)
        wide = 16 if last else 32
        ts(a3("Ns", t, t + 1, 256, 256 + wide), a("sf", 208, 208 + wide), OFF, Op.add)
        recv(prv, [a3("Yr", t, t + 1, 0, E), a("qr", 16 * t, 16 * t + 16)], "r_y%d" % t)
        for lo, hi in CFG["xp"]:
            cp(ind(XO, a("qr", 16 * t + lo // 16, 16 * t + hi // 16)), a3("Yr", t, t + 1, lo, hi))
    now[0] = RO
    own_update(RO - 1)
    recv(nxt, [a("zr")], "r_zo")
    dma("s", hbm("zo"), a("zr"))
    recv(nxt, [a("rh")], "r_ro")
    act(a("rr"), a("rh"), bias=OFF)
    dma("s", hbm("ro"), a("rr"))
    dma("s", hbm("xo", 0, H), a("XO", 0, H))
    dma("a", hbm("xo", H, W), a("XO", H, W))

    seen, bank, chain, sent_as = {}, {}, {}, {}
    for j, o in enumerate(ops):
        pre = {}
        for (name, mask), w in [(r, False) for r in o["rd"]] + [(r, True) for r in o["wr"]]:
            if SCRATCH[name][0] == "psum":
                held = bank.setdefault(name, [j])
                for i in held[:1] if o.get("adds") else held:
                    if i != j:
                        pre[i] = pre.get(i, False) or ops[i]["eng"] != o["eng"]
                bank[name] = held + [j] if o.get("adds") else [j]
                continue
            keep = []
            for (i, m2, w2) in seen.get(name, []):
                if i != j and (w or w2) and mask & m2:
                    if ops[i].get("remote") != "sent":
                        pre[i] = pre.get(i, False) or o["eng"] != "x"
                if i == j or not (w and not m2 & ~mask):
                    keep.append((i, m2, w2))
            seen[name] = keep + [(j, mask, w)]
        ln = "remote" if o.get("remote") else "dma" if "dma" in o else None
        if ln:
            if ln in chain:
                pre.setdefault(chain[ln], False)
            chain[ln] = j
        if "behind" in o:
            pre.setdefault(o["behind"], False)
        if o.get("remote"):
            sent_as.setdefault(o["msg"], []).append(j)
        o["pre"] = pre
    for e in "va":
        gate = [j for j, o in enumerate(ops) if o["eng"] == e and o["wr"] and o["wr"][0][0] == "GL"][1]
        for o in ops:
            if o["late"] and o["eng"] == e:
                o["pre"].setdefault(gate, False)
    for e in "vap":
        prev = None
        rest = {t: [j for j, o in enumerate(ops) if o.get("name", (0, 0))[:2] == (t, e)] for t in range(-1, RO + 1)}
        rest[-1] = []
        for t in range(RO):
            for name in ORDER.get(e + str(t), ORDER.get(e, "")).split():
                left = rest[t + (name[0] == "+") - (name[0] == "-")]
                name = name.lstrip("+-")
                head, tail = (name + "*").split("*")[:2]
                hit = ([j for j in left if ops[j]["name"][2] == name]
                       or [j for j in left if ops[j]["name"][2].startswith(head) and ops[j]["name"][2].endswith(tail)])
                for j in hit:
                    left.remove(j)
                    if prev is not None:
                        ops[j]["pre"].setdefault(prev, False)
                    prev = j
    for o in ops:
        if o["eng"] == "x":
            o["pre"].update({i: False for i in sent_as[o["sem"]]})

    before, after = [[] for o in ops], [[] for o in ops]
    moved_bytes = {True: 0, False: 0}
    for o in ops:
        if "dma" in o:
            moved_bytes[bool(o["wr"])] += o["dma"]
            o["lat"] = START + moved_bytes[bool(o["wr"])] / HBM
    for j, o in enumerate(ops):
        for i, sem in o["pre"].items():
            gap = ops[i]["lat"] if sem or o["eng"] == "x" else 0
            before[j].append((i, gap))
            after[i].append((j, gap))

    def lay(pre, post, rank_of, first):
        todo, end, busy = [len(x) for x in pre], [0.0] * len(ops), {e: [] for e in "vapcsx"}
        ready = [j for j in range(len(ops)) if not todo[j]]
        while ready:
            j = min(ready, key=lambda k: (rank_of[k], k))
            ready.remove(j)
            at, c, q = max([end[i] + gap for i, gap in pre[j]] + [first[j]]), ops[j]["cost"], busy[ops[j]["eng"]]
            n = len(q)
            while n and q[n - 1][1] > at:
                n -= 1
            while n < len(q) and q[n][0] < at + c:
                at = max(at, q[n][1])
                n += 1
            if c:
                q.insert(n, (at, at + c))
            end[j] = at + c
            for k, gap in post[j]:
                todo[k] -= 1
                if not todo[k]:
                    ready.append(k)
        assert not any(todo), [ops[j].get("name") for j in range(len(ops)) if todo[j]][:20]
        return end

    zero, lat = [0.0] * len(ops), [o["lat"] for o in ops]
    if "hook" in CFG:
        CFG["hook"](ops, before, after, lay)
    best, first = None, CFG.get("first") or [o["rank"] for o in ops]
    for n in range(PASSES):
        end = lay(before, after, first, zero)
        span = max(x + y for x, y in zip(end, lat))
        if best is None or span < best[0]:
            best = (span, end)
        first = [-x for x in lay(after, before, [-x for x in end], lat)]
    order = sorted(range(len(ops)), key=lambda j: (best[1][j] - ops[j]["cost"], best[1][j], j))

    place = {j: n for n, j in enumerate(order)}
    done = {e: {} for e in "vapcsx"}
    for j in order:
        o, known = ops[j], done[ops[j]["eng"]]
        o["deps"] = {}
        for i in sorted([i for i, sem in o["pre"].items() if sem], key=lambda i: -place[i]):
            key = ops[i].get("remote") or ops[i].get("sem", ops[i]["eng"])
            if place[i] > known.get(key, -1):
                o["deps"][key] = i
                ops[i]["inc"] = True
                known[key] = place[i]
                for k, p in ops[i]["knew"].items():
                    known[k] = max(known.get(k, -1), p)
        o["knew"] = dict(known)
    cnt = {"v": 0, "a": 0, "p": 0, "c": 0}
    for j in order:
        o = ops[j]
        if o["eng"] == "x":
            continue
        q = Q[o["eng"]]
        for key, i in o["deps"].items():
            q.wait_ge(T.sem[key], out_cnt[key] if key in out_cnt else ops[i]["val"])
        ins = o["fn"]()
        if o.get("remote"):
            continue
        if "sem" in o:
            ins.then_inc(T.sem[o["sem"]], 16)
        elif o.get("inc"):
            cnt[o["eng"]] += 1
            o["val"] = cnt[o["eng"]]
            ins.then_inc(T.sem[o["eng"]], 1)
    g.wait_ge(T.sem.sent, out_cnt["sent"])
    for o in ops:
        if "sem" in o and o["eng"] != "x" and not o.get("inc"):
            Q[o["eng"]].wait_ge(T.sem[o["sem"]], 16)
